import numpy as np
import ml_dtypes


def mxq(x, axis, fmt="e4m3"):
    dtype, down = {"e4m3": (ml_dtypes.float8_e4m3fn, 7), "e5m2": (ml_dtypes.float8_e5m2, 14)}[fmt]
    v = np.moveaxis(np.asarray(x, np.float32).astype(ml_dtypes.bfloat16).astype(np.float64), axis, -1)
    blocks = v.reshape(v.shape[:-1] + (-1, 32))
    amax = np.abs(blocks).max(-1, keepdims=True)
    byte = np.maximum(np.where(amax > 0, np.frexp(amax)[1] - 1 + 127, 0) - down, 1)
    scale = np.exp2(byte - 127.0)
    codes = (blocks / scale).astype(np.float32).astype(dtype).astype(np.float64)
    return np.moveaxis((codes * scale).reshape(v.shape), -1, axis)


WIDE = False


def mx_kscale(k):
    if not WIDE:
        return np.ones(k)
    levels = np.array([10, -10, 5, -5, 0])
    if k % 512:
        return np.exp2(np.random.permutation(np.resize(levels, k // 32))).repeat(32)
    a = np.empty((k // 512, 16))
    for p in range(k // 512):
        a[p, :8] = np.random.permutation(np.resize(levels, 8))
        for g in range(8):
            far = levels[np.abs(levels - a[p, g]) >= 10]
            a[p, g + 8] = far[np.random.randint(len(far))]
    return np.exp2(a.ravel()).repeat(32)


def f64(x):
    return np.asarray(x).astype(np.float64)


def striped(idx):
    return np.tile(idx.reshape(-1, 16).T, (8, 1)).astype(np.uint16)


def unstriped(offs):
    return offs[:16].T.reshape(-1).astype(np.int64)


def striped8(idx):
    return np.concatenate([x.reshape(-1, 16).T for x in idx]).astype(np.uint16)


def runs(offs, k):
    lists = np.stack([offs[16 * r : 16 * r + 16].T.reshape(-1) for r in range(8)]).astype(np.int64)
    return lists[np.arange(k) % 512 // 64]


def pack_weight(w):
    k, n = w.shape
    w = f64(np.asarray(w, np.float32).astype(ml_dtypes.bfloat16)).reshape(k // 32, 32, n)
    amax = np.abs(w).max(1)
    byte = np.clip(np.where(amax > 0, np.frexp(amax)[1] - 1 + 127 - 7, 1), 1, 254)
    scaled = (w * np.exp2(127.0 - byte)[:, None, :]).reshape(k, n).astype(np.float32)
    words = np.ascontiguousarray(scaled.reshape(k // 512, 128, 4, n).transpose(0, 1, 3, 2)).astype(ml_dtypes.float8_e4m3fn).view(np.uint8)
    return words, np.ascontiguousarray(byte.astype(np.uint8).reshape(k // 512, 16, n))


def unpack_weight(words, scales):
    g, p, n, _ = words.shape
    vals = np.ascontiguousarray(words).view(ml_dtypes.float8_e4m3fn).astype(np.float64) * np.repeat(np.exp2(scales.astype(np.float64) - 127.0), 8, axis=1)[..., None]
    return vals.transpose(0, 1, 3, 2).reshape(g * 512, n)

def planes(y):
    n, m = y.shape
    v = y.astype(np.float32).astype(ml_dtypes.bfloat16).astype(np.float64).reshape(n // 32, 32, m)
    top = np.abs(v).max(1)
    byte = np.clip(np.where(top > 0, np.frexp(top)[1] - 1 + 127 - 7, 1), 1, 254)
    codes = (v * np.exp2(127.0 - byte)[:, None, :]).reshape(n, m).astype(np.float32).astype(ml_dtypes.float8_e4m3fn).view(np.uint8)
    words = codes.reshape(n // 512, 128, 4, m).transpose(0, 1, 3, 2)
    return np.ascontiguousarray(words), np.ascontiguousarray(byte.astype(np.uint8).reshape(n // 512, 16, m))


K, T, S, N, H, U = 512, 2048, 512, 512, 512, 1024


def setup_inputs():
    n = np.random.standard_normal
    s = mx_kscale(K)[:, None]
    u = mx_kscale(H)
    packed_xT = pack_weight(n((K, T)) * s)
    packed_w3 = pack_weight(n((H, N)) / np.sqrt(2 * H) / u[:, None])
    packed_w4 = pack_weight(n((H, N)) / np.sqrt(2 * H) / u[:, None])
    ang = 3 * n((H, U))
    return {
        "x_words": packed_xT[0],
        "x_scales": packed_xT[1],
        "w1": (n((K, H)) / np.sqrt(K) / s * u).astype(np.float32),
        "w2": (n((K, H)) / np.sqrt(K) / s * u).astype(np.float32),
        "ct": np.cos(ang).astype(np.float32),
        "st": np.sin(ang).astype(np.float32),
        "w3_words": packed_w3[0],
        "w3_scales": packed_w3[1],
        "w4_words": packed_w4[0],
        "w4_scales": packed_w4[1],
        "offs": striped(np.random.permutation(T)[:S]),
        "pos": striped8(np.random.randint(0, U, (8, S))),
    }


def reference(x_words, x_scales, w1, w2, ct, st, w3_words, w3_scales, w4_words, w4_scales, offs, pos):
    xq = unpack_weight(x_words, x_scales)[:, unstriped(offs)]
    y = mxq(f64(w1), 0, "e4m3").T @ xq
    c = f64(ct)[np.arange(H)[:, None], runs(pos, H)]
    e = mxq(f64(w2), 0, "e4m3").T @ xq
    q = f64(st)[np.arange(H)[:, None], runs(pos, H)]
    z = y * c - (e * q)
    z2 = y * q + e * c
    out_0 = unpack_weight(w3_words, w3_scales).T @ mxq(z, 0, "e4m3") + unpack_weight(w4_words, w4_scales).T @ mxq(z2, 0, "e4m3")
    return (out_0,) + planes(out_0)

@@ -1,0 +1,190 @@
+from contextlib import ExitStack
+
+import concourse.mybir as mybir
+
+K, T, S, N, H, U = 512, 2048, 512, 512, 512, 1024
+FLOPS = 2 * S * (2 * K * H + 2 * H * N)
+
+F32 = mybir.dt.float32
+BF16 = mybir.dt.bfloat16
+I32 = mybir.dt.int32
+U32 = mybir.dt.uint32
+U16 = mybir.dt.uint16
+U8 = mybir.dt.uint8
+FP8X4 = mybir.dt.float8_e4m3fn_x4
+ALU = mybir.AluOpType
+
+P = 128
+PACK = 4
+BLK = 128
+NBLK = S // BLK
+W1_SPLIT = 88
+
+
+def tile_picked_headrope_none_po_kernel(tc, x_words, x_scales, w1, w2, ct, st, w3_words, w3_scales, w4_words, w4_scales, offs, pos, out_0, out_1, out_2):
+    nc = tc.nc
+    with ExitStack() as ctx:
+        keep = ctx.enter_context(tc.tile_pool(name="keep", bufs=1))
+        psum = ctx.enter_context(tc.psum_pool(name="psum", bufs=1))
+
+        def sb(name, shape, dtype):
+            return keep.tile(shape, dtype, name=name, align_bytes=64)
+
+        def words_of(dram):
+            return dram[0].rearrange("p n j -> p (n j)").bitcast(I32)
+
+        def load_scale_rows(queue, tile, first_row, dram):
+            for q in range(4):
+                rows = slice(32 * q + first_row, 32 * q + first_row + 4)
+                queue.dma_start(out=tile[rows, :].bitcast(I32), in_=dram[0][4 * q : 4 * q + 4, :].bitcast(I32))
+
+        offs_t = keep.tile([P, S // 16], U16, name="offs_t")
+        pos_t = keep.tile([P, S // 16], U16, name="pos_t")
+        x_tab = sb("x_tab", [P, T], U32)
+        xs_tab = sb("xs_tab", [P, T], U8)
+        w_raw = [sb("w_raw%d" % i, [P, PACK, H], F32) for i in range(2)]
+        c_tab = [sb("c_tab%d" % t, [P, U], F32) for t in range(PACK)]
+        s_tab = [sb("s_tab%d" % t, [P, U], F32) for t in range(PACK)]
+        wo_raw = sb("wo_raw", [P, 2, N], I32)
+        wos_raw = sb("wos_raw", [P, N], U8)
+
+        nc.vector.memset(xs_tab[:].bitcast(I32), 0)
+        nc.vector.memset(wos_raw[:].bitcast(I32), 0)
+
+        ct_v = ct.rearrange("(p t) u -> p t u", t=PACK)
+        st_v = st.rearrange("(p t) u -> p t u", t=PACK)
+
+        def load_tables(t):
+            nc.sync.dma_start(out=c_tab[t][:], in_=ct_v[:, t, :])
+            nc.sync.dma_start(out=s_tab[t][:], in_=st_v[:, t, :])
+
+        nc.sync.dma_start(out=x_tab[:].bitcast(I32), in_=words_of(x_words))
+        nc.sync.dma_start(offs_t[:], offs)
+        load_scale_rows(nc.scalar, xs_tab, 0, x_scales)
+        nc.sync.dma_start(out=w_raw[0][:], in_=w1.rearrange("(p j) c -> p j c", j=PACK))
+        nc.sync.dma_start(pos_t[:], pos)
+        load_tables(0)
+        nc.sync.dma_start(out=w_raw[1][:], in_=w2.rearrange("(p j) c -> p j c", j=PACK))
+        for t in range(1, PACK):
+            load_tables(t)
+        nc.sync.dma_start(out=wo_raw[:, 0, :], in_=words_of(w3_words))
+        nc.sync.dma_start(out=wo_raw[:, 1, :], in_=words_of(w4_words))
+        load_scale_rows(nc.sync, wos_raw, 0, w3_scales)
+        load_scale_rows(nc.sync, wos_raw, 4, w4_scales)
+
+        x_codes = sb("x_codes", [P, S], U32)
+        x_sc = sb("x_sc", [P, S], U8)
+        nc.vector.tensor_copy(x_codes[:], x_tab[:].indirect(offs_t[:]))
+        nc.vector.tensor_copy(x_sc[:], xs_tab[:].indirect(offs_t[:]))
+
+        w_bf = [sb("w_bf%d" % i, [P, PACK * H], BF16) for i in range(2)]
+        w_codes = [sb("w_codes%d" % i, [P, H], U32) for i in range(2)]
+        w_sc = [sb("w_sc%d" % i, [P, H], U8) for i in range(2)]
+
+        def deal_views(i, ms):
+            dst = w_bf[i][:].rearrange("p (t m j) -> p m j t", t=PACK, j=PACK)
+            src = w_raw[i][:].rearrange("p j (m t) -> p m j t", t=PACK)
+            return dst[:, ms], src[:, ms]
+
+        def quantize_w(i):
+            nc.vector.quantize_mx(out=w_codes[i][:].bitcast(FP8X4), scales=w_sc[i][:], in_=w_bf[i][:])
+
+        def project(i, t):
+            acc = psum.tile([P, S], F32, name="proj%d" % i, bufs=3 - i)
+            cols = slice(t * P, (t + 1) * P)
+            nc.tensor.matmul_mx(out=acc[:], lhsT=w_codes[i][:, cols].bitcast(FP8X4), lhsT_scale=w_sc[i][:, cols],
+                                rhs=x_codes[:].bitcast(FP8X4), rhs_scale=x_sc[:], start=True, stop=True)
+            return acc
+
+        trig = [sb("trig%d" % t, [P, 2, S], F32) for t in range(PACK)]
+        prod = [sb("prod%d" % i, [P, PACK, 2, S], F32) for i in range(2)]
+
+        def look_up(t):
+            nc.vector.tensor_copy(trig[t][:, 0, :], c_tab[t][:].indirect(pos_t[:]))
+            nc.vector.tensor_copy(trig[t][:, 1, :], s_tab[t][:].indirect(pos_t[:]))
+
+        def multiply(i, t, acc, toks):
+            n = toks.stop - toks.start
+            nc.vector.tensor_tensor(out=prod[i][:, t, :, toks], in0=acc[:, toks].unsqueeze(1).to_broadcast([P, 2, n]),
+                                    in1=trig[t][:, :, toks], op=ALU.mult)
+
+        dst, src = deal_views(0, slice(0, W1_SPLIT))
+        nc.vector.tensor_copy(out=dst, in_=src)
+        dst, src = deal_views(0, slice(W1_SPLIT, P))
+        nc.scalar.copy(out=dst, in_=src)
+        dst, src = deal_views(1, slice(0, P))
+        nc.scalar.copy(out=dst, in_=src)
+
+        whole = slice(0, S)
+        quantize_w(0)
+        look_up(0)
+        multiply(0, 0, project(0, 0), whole)
+        look_up(1)
+        quantize_w(1)
+        multiply(0, 1, project(0, 1), whole)
+        multiply(1, 0, project(1, 0), whole)
+        look_up(2)
+        multiply(1, 1, project(1, 1), whole)
+        multiply(0, 2, project(0, 2), whole)
+        look_up(3)
+        multiply(1, 2, project(1, 2), whole)
+        last = [project(0, 3), project(1, 3)]
+
+        wo = sb("wo", [P, 2, N], I32)
+        wos = sb("wos", [P, N], U8)
+        nc.vector.tensor_copy(out=wo[:].rearrange("p a (t m) -> p a m t", t=PACK), in_=wo_raw[:].rearrange("p a (m t) -> p a m t", t=PACK))
+        nc.vector.tensor_copy(out=wos[:].rearrange("p (t m) -> p m t", t=PACK), in_=wos_raw[:].rearrange("p (m t) -> p m t", t=PACK))
+
+        z_bf = [sb("z_bf%d" % b, [P, 2, BLK * PACK], BF16) for b in range(NBLK)]
+        z_codes = [sb("z_codes%d" % b, [P, 2, BLK], U32) for b in range(NBLK)]
+        z_sc = [sb("z_sc%d" % b, [P, 2, BLK], U8) for b in range(NBLK)]
+        o_bf = [sb("o_bf%d" % b, [P, BLK * PACK], BF16) for b in range(NBLK)]
+        o_f32 = [sb("o_f32%d" % b, [P, PACK, BLK], F32) for b in range(NBLK)]
+        o_codes = sb("o_codes", [P, S], U32)
+        o_sc = sb("o_sc", [P, S], U8)
+        out_v = out_0.rearrange("(p t) n -> p t n", t=PACK)
+        out_words = words_of(out_1)
+
+        def toks_of(b):
+            return slice(b * BLK, (b + 1) * BLK)
+
+        def last_products(b):
+            for i in range(2):
+                multiply(i, PACK - 1, last[i], toks_of(b))
+
+        def rotate(b):
+            for a, op in ((0, ALU.subtract), (1, ALU.add)):
+                dst = z_bf[b][:, a, :].rearrange("p (c i t) -> p c t i", i=4, t=PACK)
+                in0 = prod[0][:, :, a, toks_of(b)].rearrange("p t (c i) -> p c t i", i=4)
+                in1 = prod[1][:, :, 1 - a, toks_of(b)].rearrange("p t (c i) -> p c t i", i=4)
+                nc.vector.tensor_tensor(out=dst, in0=in0, in1=in1, op=op)
+
+        def second_product(b):
+            nc.vector.quantize_mx(out=z_codes[b][:].rearrange("p a n -> p (a n)").bitcast(FP8X4),
+                                  scales=z_sc[b][:].rearrange("p a n -> p (a n)"),
+                                  in_=z_bf[b][:].rearrange("p a n -> p (a n)"))
+            acc = psum.tile([P, PACK, BLK], F32, name="o_acc", bufs=3)
+            for t in range(PACK):
+                cols = slice(t * P, (t + 1) * P)
+                for a in range(2):
+                    nc.tensor.matmul_mx(out=acc[:, t, :], lhsT=wo[:, a, cols].bitcast(FP8X4), lhsT_scale=wos[4 * a :, cols],
+                                        rhs=z_codes[b][:, a, :].bitcast(FP8X4), rhs_scale=z_sc[b][:, a, :],
+                                        start=(a == 0), stop=(a == 1))
+            nc.scalar.copy(out=o_bf[b][:].rearrange("p (n t) -> p n t", t=PACK), in_=acc[:].rearrange("p t n -> p n t"))
+            nc.scalar.copy(out=o_f32[b][:], in_=acc[:])
+            nc.sync.dma_start(out=out_v[:, :, toks_of(b)], in_=o_f32[b][:])
+
+        def hand_on(b):
+            toks = toks_of(b)
+            nc.vector.quantize_mx(out=o_codes[:, toks].bitcast(FP8X4), scales=o_sc[:, toks], in_=o_bf[b][:])
+            nc.sync.dma_start(out=out_words[:, toks], in_=o_codes[:, toks].bitcast(I32))
+
+        steps = (last_products, rotate, second_product, hand_on)
+        lag = (0, 1, 2, 4)
+        for tick in range(NBLK + lag[-1]):
+            for step, d in zip(steps, lag):
+                if 0 <= tick - d < NBLK:
+                    step(tick - d)
+        for q in range(4):
+            queue = nc.scalar if q % 2 else nc.sync
+            queue.dma_start(out=out_2[0][4 * q : 4 * q + 4, :].bitcast(I32), in_=o_sc[32 * q : 32 * q + 4, :].bitcast(I32))

@@ -63,9 +63,8 @@ def tile_picked_headrope_none_po_kernel(tc, x_words, x_scales, w1, w2, ct, st, w
         load_scale_rows(nc.scalar, xs_tab, 0, x_scales)
         nc.sync.dma_start(out=w_raw[0][:], in_=w1.rearrange("(p j) c -> p j c", j=PACK))
         nc.sync.dma_start(pos_t[:], pos)
-        load_tables(0)
         nc.sync.dma_start(out=w_raw[1][:], in_=w2.rearrange("(p j) c -> p j c", j=PACK))
-        for t in range(1, PACK):
+        for t in range(PACK):
             load_tables(t)
         nc.sync.dma_start(out=wo_raw[:, 0, :], in_=words_of(w3_words))
         nc.sync.dma_start(out=wo_raw[:, 1, :], in_=words_of(w4_words))
@@ -90,7 +89,7 @@ def tile_picked_headrope_none_po_kernel(tc, x_words, x_scales, w1, w2, ct, st, w
             nc.vector.quantize_mx(out=w_codes[i][:].bitcast(FP8X4), scales=w_sc[i][:], in_=w_bf[i][:])
 
         def project(i, t):
-            acc = psum.tile([P, S], F32, name="proj%d" % i, bufs=3 - i)
+            acc = psum.tile([P, S], F32, name="proj", bufs=5)
             cols = slice(t * P, (t + 1) * P)
             nc.tensor.matmul_mx(out=acc[:], lhsT=w_codes[i][:, cols].bitcast(FP8X4), lhsT_scale=w_sc[i][:, cols],
                                 rhs=x_codes[:].bitcast(FP8X4), rhs_scale=x_sc[:], start=True, stop=True)
@@ -108,26 +107,25 @@ def tile_picked_headrope_none_po_kernel(tc, x_words, x_scales, w1, w2, ct, st, w
             nc.vector.tensor_tensor(out=prod[i][:, t, :, toks], in0=acc[:, toks].unsqueeze(1).to_broadcast([P, 2, n]),
                                     in1=trig[t][:, :, toks], op=ALU.mult)
 
-        dst, src = deal_views(0, slice(0, W1_SPLIT))
-        nc.vector.tensor_copy(out=dst, in_=src)
-        dst, src = deal_views(0, slice(W1_SPLIT, P))
-        nc.scalar.copy(out=dst, in_=src)
-        dst, src = deal_views(1, slice(0, P))
-        nc.scalar.copy(out=dst, in_=src)
+        def multiply_aside(i, t):
+            acc = project(i, t)
+            plain = sb("plain%d_%d" % (i, t), [P, S], F32)
+            nc.scalar.copy(out=plain[:], in_=acc[:])
+            for a in range(2):
+                nc.gpsimd.tensor_tensor(out=prod[i][:, t, a, :], in0=plain[:], in1=trig[t][:, a, :], op=ALU.mult)
 
-        whole = slice(0, S)
-        quantize_w(0)
-        look_up(0)
-        multiply(0, 0, project(0, 0), whole)
-        look_up(1)
-        quantize_w(1)
-        multiply(0, 1, project(0, 1), whole)
-        multiply(1, 0, project(1, 0), whole)
-        look_up(2)
-        multiply(1, 1, project(1, 1), whole)
-        multiply(0, 2, project(0, 2), whole)
-        look_up(3)
-        multiply(1, 2, project(1, 2), whole)
+        for i in range(2):
+            dst, src = deal_views(i, slice(0, W1_SPLIT))
+            nc.vector.tensor_copy(out=dst, in_=src)
+            dst, src = deal_views(i, slice(W1_SPLIT, P))
+            nc.scalar.copy(out=dst, in_=src)
+            quantize_w(i)
+
+        for t in range(PACK):
+            look_up(t)
+        for t, i in ((0, 0), (0, 1), (1, 0), (1, 1), (2, 0)):
+            multiply_aside(i, t)
+        multiply(1, 2, project(1, 2), slice(0, S))
         last = [project(0, 3), project(1, 3)]
 
         wo = sb("wo", [P, 2, N], I32)

@@ -48,7 +48,7 @@ def tile_picked_headrope_none_po_kernel(tc, x_words, x_scales, w1, w2, ct, st, w
         wo_raw = sb("wo_raw", [P, 2, N], I32)
         wos_raw = sb("wos_raw", [P, N], U8)
 
-        nc.vector.memset(xs_tab[:].bitcast(I32), 0)
+        nc.gpsimd.memset(xs_tab[:].bitcast(I32), 0)
         nc.vector.memset(wos_raw[:].bitcast(I32), 0)
 
         ct_v = ct.rearrange("(p t) u -> p t u", t=PACK)
@@ -58,13 +58,14 @@ def tile_picked_headrope_none_po_kernel(tc, x_words, x_scales, w1, w2, ct, st, w
             nc.sync.dma_start(out=c_tab[t][:], in_=ct_v[:, t, :])
             nc.sync.dma_start(out=s_tab[t][:], in_=st_v[:, t, :])
 
-        nc.sync.dma_start(out=x_tab[:].bitcast(I32), in_=words_of(x_words))
         nc.sync.dma_start(offs_t[:], offs)
-        load_scale_rows(nc.scalar, xs_tab, 0, x_scales)
+        nc.sync.dma_start(out=x_tab[:].bitcast(I32), in_=words_of(x_words))
+        load_scale_rows(nc.sync, xs_tab, 0, x_scales)
         nc.sync.dma_start(out=w_raw[0][:], in_=w1.rearrange("(p j) c -> p j c", j=PACK))
         nc.sync.dma_start(pos_t[:], pos)
         nc.sync.dma_start(out=w_raw[1][:], in_=w2.rearrange("(p j) c -> p j c", j=PACK))
-        for t in range(PACK):
+        load_tables(0)
+        for t in range(1, PACK):
             load_tables(t)
         nc.sync.dma_start(out=wo_raw[:, 0, :], in_=words_of(w3_words))
         nc.sync.dma_start(out=wo_raw[:, 1, :], in_=words_of(w4_words))
@@ -96,23 +97,11 @@ def tile_picked_headrope_none_po_kernel(tc, x_words, x_scales, w1, w2, ct, st, w
             return acc
 
         trig = [sb("trig%d" % t, [P, 2, S], F32) for t in range(PACK)]
-        prod = [sb("prod%d" % i, [P, PACK, 2, S], F32) for i in range(2)]
+        prod = sb("prod", [P, PACK, 2, 2, S], F32)
 
         def look_up(t):
             nc.vector.tensor_copy(trig[t][:, 0, :], c_tab[t][:].indirect(pos_t[:]))
             nc.vector.tensor_copy(trig[t][:, 1, :], s_tab[t][:].indirect(pos_t[:]))
-
-        def multiply(i, t, acc, toks):
-            n = toks.stop - toks.start
-            nc.vector.tensor_tensor(out=prod[i][:, t, :, toks], in0=acc[:, toks].unsqueeze(1).to_broadcast([P, 2, n]),
-                                    in1=trig[t][:, :, toks], op=ALU.mult)
-
-        def multiply_aside(i, t):
-            acc = project(i, t)
-            plain = sb("plain%d_%d" % (i, t), [P, S], F32)
-            nc.scalar.copy(out=plain[:], in_=acc[:])
-            for a in range(2):
-                nc.gpsimd.tensor_tensor(out=prod[i][:, t, a, :], in0=plain[:], in1=trig[t][:, a, :], op=ALU.mult)
 
         for i in range(2):
             dst, src = deal_views(i, slice(0, W1_SPLIT))
@@ -120,13 +109,24 @@ def tile_picked_headrope_none_po_kernel(tc, x_words, x_scales, w1, w2, ct, st, w
             dst, src = deal_views(i, slice(W1_SPLIT, P))
             nc.scalar.copy(out=dst, in_=src)
             quantize_w(i)
-
         for t in range(PACK):
             look_up(t)
-        for t, i in ((0, 0), (0, 1), (1, 0), (1, 1), (2, 0)):
-            multiply_aside(i, t)
-        multiply(1, 2, project(1, 2), slice(0, S))
-        last = [project(0, 3), project(1, 3)]
+
+        on_gpsimd = 5
+        for t in range(PACK):
+            accs = [project(i, t) for i in range(2)]
+            aside = [a for a in range(2) if 2 * t + a < on_gpsimd]
+            if aside:
+                plain = sb("plain%d" % t, [P, 2, S], F32)
+                for i in range(2):
+                    nc.scalar.copy(out=plain[:, i, :], in_=accs[i][:])
+            for a in aside:
+                nc.gpsimd.tensor_tensor(out=prod[:, t, a, :, :], in0=plain[:], in1=trig[t][:, a, :].unsqueeze(1).to_broadcast([P, 2, S]), op=ALU.mult)
+            rest = slice(len(aside), 2)
+            if len(aside) < 2:
+                for i in range(2):
+                    nc.vector.tensor_tensor(out=prod[:, t, rest, i, :], in0=accs[i][:].unsqueeze(1).to_broadcast([P, 2 - len(aside), S]),
+                                            in1=trig[t][:, rest, :], op=ALU.mult)
 
         wo = sb("wo", [P, 2, N], I32)
         wos = sb("wos", [P, N], U8)
@@ -146,16 +146,11 @@ def tile_picked_headrope_none_po_kernel(tc, x_words, x_scales, w1, w2, ct, st, w
         def toks_of(b):
             return slice(b * BLK, (b + 1) * BLK)
 
-        def last_products(b):
-            for i in range(2):
-                multiply(i, PACK - 1, last[i], toks_of(b))
-
-        def rotate(b):
-            for a, op in ((0, ALU.subtract), (1, ALU.add)):
-                dst = z_bf[b][:, a, :].rearrange("p (c i t) -> p c t i", i=4, t=PACK)
-                in0 = prod[0][:, :, a, toks_of(b)].rearrange("p t (c i) -> p c t i", i=4)
-                in1 = prod[1][:, :, 1 - a, toks_of(b)].rearrange("p t (c i) -> p c t i", i=4)
-                nc.vector.tensor_tensor(out=dst, in0=in0, in1=in1, op=op)
+        def rotate(b, a):
+            dst = z_bf[b][:, a, :].rearrange("p (c i t) -> p c t i", i=2, t=PACK)
+            in0 = prod[:, :, a, 0, toks_of(b)].rearrange("p t (c i) -> p c t i", i=2)
+            in1 = prod[:, :, 1 - a, 1, toks_of(b)].rearrange("p t (c i) -> p c t i", i=2)
+            nc.vector.tensor_tensor(out=dst, in0=in0, in1=in1, op=(ALU.subtract, ALU.add)[a])
 
         def second_product(b):
             nc.vector.quantize_mx(out=z_codes[b][:].rearrange("p a n -> p (a n)").bitcast(FP8X4),
@@ -177,12 +172,15 @@ def tile_picked_headrope_none_po_kernel(tc, x_words, x_scales, w1, w2, ct, st, w
             nc.vector.quantize_mx(out=o_codes[:, toks].bitcast(FP8X4), scales=o_sc[:, toks], in_=o_bf[b][:])
             nc.sync.dma_start(out=out_words[:, toks], in_=o_codes[:, toks].bitcast(I32))
 
-        steps = (last_products, rotate, second_product, hand_on)
-        lag = (0, 1, 2, 4)
-        for tick in range(NBLK + lag[-1]):
-            for step, d in zip(steps, lag):
-                if 0 <= tick - d < NBLK:
-                    step(tick - d)
+        for b in range(NBLK + 2):
+            if b < NBLK:
+                rotate(b, 0)
+            if 1 <= b <= NBLK:
+                second_product(b - 1)
+            if b < NBLK:
+                rotate(b, 1)
+            if b >= 2:
+                hand_on(b - 2)
         for q in range(4):
             queue = nc.scalar if q % 2 else nc.sync
             queue.dma_start(out=out_2[0][4 * q : 4 * q + 4, :].bitcast(I32), in_=o_sc[32 * q : 32 * q + 4, :].bitcast(I32))

@@ -30,6 +30,9 @@ def tile_picked_headrope_none_po_kernel(tc, x_words, x_scales, w1, w2, ct, st, w
         def sb(name, shape, dtype):
             return keep.tile(shape, dtype, name=name, align_bytes=64)
 
+        def bank(k, shape):
+            return psum.tile(shape, F32, name="bank%d" % k)
+
         def words_of(dram):
             return dram[0].rearrange("p n j -> p (n j)").bitcast(I32)
 
@@ -90,7 +93,7 @@ def tile_picked_headrope_none_po_kernel(tc, x_words, x_scales, w1, w2, ct, st, w
             nc.vector.quantize_mx(out=w_codes[i][:].bitcast(FP8X4), scales=w_sc[i][:], in_=w_bf[i][:])
 
         def project(i, t):
-            acc = psum.tile([P, S], F32, name="proj", bufs=5)
+            acc = bank(2 * t + i, [P, S])
             cols = slice(t * P, (t + 1) * P)
             nc.tensor.matmul_mx(out=acc[:], lhsT=w_codes[i][:, cols].bitcast(FP8X4), lhsT_scale=w_sc[i][:, cols],
                                 rhs=x_codes[:].bitcast(FP8X4), rhs_scale=x_sc[:], start=True, stop=True)
@@ -112,26 +115,33 @@ def tile_picked_headrope_none_po_kernel(tc, x_words, x_scales, w1, w2, ct, st, w
         for t in range(PACK):
             look_up(t)
 
-        on_gpsimd = 5
+        def from_psum(t, i, acc, factors):
+            n = factors.stop - factors.start
+            nc.vector.tensor_tensor(out=prod[:, t, factors, i, :], in0=acc[:].unsqueeze(1).to_broadcast([P, n, S]),
+                                    in1=trig[t][:, factors, :], op=ALU.mult)
+
         for t in range(PACK):
             accs = [project(i, t) for i in range(2)]
-            aside = [a for a in range(2) if 2 * t + a < on_gpsimd]
-            if aside:
+            if t < 2:
                 plain = sb("plain%d" % t, [P, 2, S], F32)
                 for i in range(2):
                     nc.scalar.copy(out=plain[:, i, :], in_=accs[i][:])
-            for a in aside:
-                nc.gpsimd.tensor_tensor(out=prod[:, t, a, :, :], in0=plain[:], in1=trig[t][:, a, :].unsqueeze(1).to_broadcast([P, 2, S]), op=ALU.mult)
-            rest = slice(len(aside), 2)
-            if len(aside) < 2:
+                for a in range(2):
+                    nc.gpsimd.tensor_tensor(out=prod[:, t, a, :, :], in0=plain[:], in1=trig[t][:, a, :].unsqueeze(1).to_broadcast([P, 2, S]), op=ALU.mult)
+            elif t == 2:
+                plain = sb("plain%d" % t, [P, S], F32)
+                nc.scalar.copy(out=plain[:], in_=accs[0][:])
+                nc.gpsimd.tensor_tensor(out=prod[:, t, 0, 0, :], in0=plain[:], in1=trig[t][:, 0, :], op=ALU.mult)
+                from_psum(t, 0, accs[0], slice(1, 2))
+                from_psum(t, 1, accs[1], slice(0, 2))
+            else:
                 for i in range(2):
-                    nc.vector.tensor_tensor(out=prod[:, t, rest, i, :], in0=accs[i][:].unsqueeze(1).to_broadcast([P, 2 - len(aside), S]),
-                                            in1=trig[t][:, rest, :], op=ALU.mult)
+                    from_psum(t, i, accs[i], slice(0, 2))
 
         wo = sb("wo", [P, 2, N], I32)
         wos = sb("wos", [P, N], U8)
-        nc.vector.tensor_copy(out=wo[:].rearrange("p a (t m) -> p a m t", t=PACK), in_=wo_raw[:].rearrange("p a (m t) -> p a m t", t=PACK))
-        nc.vector.tensor_copy(out=wos[:].rearrange("p (t m) -> p m t", t=PACK), in_=wos_raw[:].rearrange("p (m t) -> p m t", t=PACK))
+        nc.gpsimd.tensor_copy(out=wo[:].rearrange("p a (t m) -> p a t m", t=PACK), in_=wo_raw[:].rearrange("p a (m t) -> p a t m", t=PACK))
+        nc.gpsimd.tensor_copy(out=wos[:].rearrange("p (t m) -> p t m", t=PACK), in_=wos_raw[:].rearrange("p (m t) -> p t m", t=PACK))
 
         z_bf = [sb("z_bf%d" % b, [P, 2, BLK * PACK], BF16) for b in range(NBLK)]
         z_codes = [sb("z_codes%d" % b, [P, 2, BLK], U32) for b in range(NBLK)]
@@ -152,17 +162,23 @@ def tile_picked_headrope_none_po_kernel(tc, x_words, x_scales, w1, w2, ct, st, w
             in1 = prod[:, :, 1 - a, 1, toks_of(b)].rearrange("p t (c i) -> p c t i", i=2)
             nc.vector.tensor_tensor(out=dst, in0=in0, in1=in1, op=(ALU.subtract, ALU.add)[a])
 
+        def quantize_z(b, a):
+            nc.vector.quantize_mx(out=z_codes[b][:, a, :].rearrange("p a n -> p (a n)").bitcast(FP8X4),
+                                  scales=z_sc[b][:, a, :].rearrange("p a n -> p (a n)"),
+                                  in_=z_bf[b][:, a, :].rearrange("p a n -> p (a n)"))
+
+        def out_pass(dst, b, t, a):
+            cols = slice(t * P, (t + 1) * P)
+            nc.tensor.matmul_mx(out=dst, lhsT=wo[:, a, cols].bitcast(FP8X4), lhsT_scale=wos[4 * a :, cols],
+                                rhs=z_codes[b][:, a, :].bitcast(FP8X4), rhs_scale=z_sc[b][:, a, :],
+                                start=(a == 0), stop=(a == 1))
+
         def second_product(b):
-            nc.vector.quantize_mx(out=z_codes[b][:].rearrange("p a n -> p (a n)").bitcast(FP8X4),
-                                  scales=z_sc[b][:].rearrange("p a n -> p (a n)"),
-                                  in_=z_bf[b][:].rearrange("p a n -> p (a n)"))
-            acc = psum.tile([P, PACK, BLK], F32, name="o_acc", bufs=3)
+            quantize_z(b, slice(0, 2))
+            acc = bank(b, [P, PACK, BLK])
             for t in range(PACK):
-                cols = slice(t * P, (t + 1) * P)
                 for a in range(2):
-                    nc.tensor.matmul_mx(out=acc[:, t, :], lhsT=wo[:, a, cols].bitcast(FP8X4), lhsT_scale=wos[4 * a :, cols],
-                                        rhs=z_codes[b][:, a, :].bitcast(FP8X4), rhs_scale=z_sc[b][:, a, :],
-                                        start=(a == 0), stop=(a == 1))
+                    out_pass(acc[:, t, :], b, t, a)
             nc.scalar.copy(out=o_bf[b][:].rearrange("p (n t) -> p n t", t=PACK), in_=acc[:].rearrange("p t n -> p n t"))
             nc.scalar.copy(out=o_f32[b][:], in_=acc[:])
             nc.sync.dma_start(out=out_v[:, :, toks_of(b)], in_=o_f32[b][:])
@@ -172,15 +188,34 @@ def tile_picked_headrope_none_po_kernel(tc, x_words, x_scales, w1, w2, ct, st, w
             nc.vector.quantize_mx(out=o_codes[:, toks].bitcast(FP8X4), scales=o_sc[:, toks], in_=o_bf[b][:])
             nc.sync.dma_start(out=out_words[:, toks], in_=o_codes[:, toks].bitcast(I32))
 
-        for b in range(NBLK + 2):
-            if b < NBLK:
-                rotate(b, 0)
-            if 1 <= b <= NBLK:
+        last = NBLK - 1
+        for b in range(last):
+            rotate(b, 0)
+            if b >= 1:
                 second_product(b - 1)
-            if b < NBLK:
-                rotate(b, 1)
+            rotate(b, 1)
             if b >= 2:
                 hand_on(b - 2)
+        second_product(last - 1)
+        rotate(last, 0)
+        hand_on(last - 2)
+        quantize_z(last, slice(0, 1))
+        accs = [bank(last + t, [P, BLK]) for t in range(PACK)]
+        for t in range(PACK):
+            out_pass(accs[t][:], last, t, 0)
+        rotate(last, 1)
+        quantize_z(last, slice(1, 2))
+        hand_on(last - 1)
+        for t in range(PACK):
+            out_pass(accs[t][:], last, t, 1)
+            if t % 2:
+                nc.vector.tensor_copy(out=o_f32[last][:, t, :], in_=accs[t][:])
+            else:
+                nc.scalar.copy(out=o_f32[last][:, t, :], in_=accs[t][:])
+        nc.sync.dma_start(out=out_v[:, :, toks_of(last)], in_=o_f32[last][:])
+        nc.vector.tensor_copy(out=o_bf[last][:].rearrange("p (c i t) -> p c t i", i=4, t=PACK),
+                              in_=o_f32[last][:].rearrange("p t (c i) -> p c t i", i=4))
+        hand_on(last)
         for q in range(4):
             queue = nc.scalar if q % 2 else nc.sync
             queue.dma_start(out=out_2[0][4 * q : 4 * q + 4, :].bitcast(I32), in_=o_sc[32 * q : 32 * q + 4, :].bitcast(I32))

@@ -27,8 +27,8 @@ def tile_picked_headrope_none_po_kernel(tc, x_words, x_scales, w1, w2, ct, st, w
         keep = ctx.enter_context(tc.tile_pool(name="keep", bufs=1))
         psum = ctx.enter_context(tc.psum_pool(name="psum", bufs=1))
 
-        def sb(name, shape, dtype):
-            return keep.tile(shape, dtype, name=name, align_bytes=64)
+        def sb(name, shape, dtype, tag=""):
+            return keep.tile(shape, dtype, name=name, tag=tag or name, align_bytes=64)
 
         def bank(k, shape):
             return psum.tile(shape, F32, name="bank%d" % k)
@@ -131,19 +131,19 @@ def tile_picked_headrope_none_po_kernel(tc, x_words, x_scales, w1, w2, ct, st, w
             elif t == 2:
                 plain = sb("plain%d" % t, [P, S], F32)
                 nc.scalar.copy(out=plain[:], in_=accs[0][:])
-                nc.gpsimd.tensor_tensor(out=prod[:, t, 0, 0, :], in0=plain[:], in1=trig[t][:, 0, :], op=ALU.mult)
-                from_psum(t, 0, accs[0], slice(1, 2))
+                nc.gpsimd.tensor_tensor(out=prod[:, t, :, 0, :], in0=plain[:].unsqueeze(1).to_broadcast([P, 2, S]), in1=trig[t][:], op=ALU.mult)
                 from_psum(t, 1, accs[1], slice(0, 2))
             else:
                 for i in range(2):
                     from_psum(t, i, accs[i], slice(0, 2))
 
         wo = sb("wo", [P, 2, N], I32)
+        nc.vector.tensor_copy(out=wo[:].rearrange("p a (t m) -> p a m t", t=PACK), in_=wo_raw[:].rearrange("p a (m t) -> p a m t", t=PACK))
         wos = sb("wos", [P, N], U8)
-        nc.gpsimd.tensor_copy(out=wo[:].rearrange("p a (t m) -> p a t m", t=PACK), in_=wo_raw[:].rearrange("p a (m t) -> p a t m", t=PACK))
-        nc.gpsimd.tensor_copy(out=wos[:].rearrange("p (t m) -> p t m", t=PACK), in_=wos_raw[:].rearrange("p (m t) -> p t m", t=PACK))
+        nc.vector.tensor_copy(out=wos[:].rearrange("p (t m) -> p m t", t=PACK), in_=wos_raw[:].rearrange("p (m t) -> p m t", t=PACK))
 
-        z_bf = [sb("z_bf%d" % b, [P, 2, BLK * PACK], BF16) for b in range(NBLK)]
+        z_all = sb("z_all", [P, 2 * S * PACK], BF16, "wos_raw")
+        z_bf = [[z_all[:, (2 * b + a) * BLK * PACK : (2 * b + a + 1) * BLK * PACK] for a in range(2)] for b in range(NBLK)]
         z_codes = [sb("z_codes%d" % b, [P, 2, BLK], U32) for b in range(NBLK)]
         z_sc = [sb("z_sc%d" % b, [P, 2, BLK], U8) for b in range(NBLK)]
         o_bf = [sb("o_bf%d" % b, [P, BLK * PACK], BF16) for b in range(NBLK)]
@@ -157,15 +157,13 @@ def tile_picked_headrope_none_po_kernel(tc, x_words, x_scales, w1, w2, ct, st, w
             return slice(b * BLK, (b + 1) * BLK)
 
         def rotate(b, a):
-            dst = z_bf[b][:, a, :].rearrange("p (c i t) -> p c t i", i=2, t=PACK)
+            dst = z_bf[b][a].rearrange("p (c i t) -> p c t i", i=2, t=PACK)
             in0 = prod[:, :, a, 0, toks_of(b)].rearrange("p t (c i) -> p c t i", i=2)
             in1 = prod[:, :, 1 - a, 1, toks_of(b)].rearrange("p t (c i) -> p c t i", i=2)
             nc.vector.tensor_tensor(out=dst, in0=in0, in1=in1, op=(ALU.subtract, ALU.add)[a])
 
         def quantize_z(b, a):
-            nc.vector.quantize_mx(out=z_codes[b][:, a, :].rearrange("p a n -> p (a n)").bitcast(FP8X4),
-                                  scales=z_sc[b][:, a, :].rearrange("p a n -> p (a n)"),
-                                  in_=z_bf[b][:, a, :].rearrange("p a n -> p (a n)"))
+            nc.vector.quantize_mx(out=z_codes[b][:, a, :].bitcast(FP8X4), scales=z_sc[b][:, a, :], in_=z_bf[b][a])
 
         def out_pass(dst, b, t, a):
             cols = slice(t * P, (t + 1) * P)
@@ -174,7 +172,6 @@ def tile_picked_headrope_none_po_kernel(tc, x_words, x_scales, w1, w2, ct, st, w
                                 start=(a == 0), stop=(a == 1))
 
         def second_product(b):
-            quantize_z(b, slice(0, 2))
             acc = bank(b, [P, PACK, BLK])
             for t in range(PACK):
                 for a in range(2):
@@ -189,23 +186,19 @@ def tile_picked_headrope_none_po_kernel(tc, x_words, x_scales, w1, w2, ct, st, w
             nc.sync.dma_start(out=out_words[:, toks], in_=o_codes[:, toks].bitcast(I32))
 
         last = NBLK - 1
-        for b in range(last):
+        for b in range(NBLK):
             rotate(b, 0)
-            if b >= 1:
-                second_product(b - 1)
             rotate(b, 1)
             if b >= 2:
                 hand_on(b - 2)
-        second_product(last - 1)
-        rotate(last, 0)
-        hand_on(last - 2)
-        quantize_z(last, slice(0, 1))
+            quantize_z(b, 0)
+            quantize_z(b, 1)
+            if b < last:
+                second_product(b)
+        hand_on(last - 1)
         accs = [bank(last + t, [P, BLK]) for t in range(PACK)]
         for t in range(PACK):
             out_pass(accs[t][:], last, t, 0)
-        rotate(last, 1)
-        quantize_z(last, slice(1, 2))
-        hand_on(last - 1)
         for t in range(PACK):
             out_pass(accs[t][:], last, t, 1)
             if t % 2:

@@ -1,6 +1,7 @@
 from contextlib import ExitStack
 
 import concourse.mybir as mybir
+from concourse.masks import make_identity
 
 K, T, S, N, H, U = 512, 2048, 512, 512, 512, 1024
 FLOPS = 2 * S * (2 * K * H + 2 * H * N)
@@ -18,7 +19,7 @@ P = 128
 PACK = 4
 BLK = 128
 NBLK = S // BLK
-W1_SPLIT = 88
+W1_SPLIT = 92
 
 
 def tile_picked_headrope_none_po_kernel(tc, x_words, x_scales, w1, w2, ct, st, w3_words, w3_scales, w4_words, w4_scales, offs, pos, out_0, out_1, out_2):
@@ -53,6 +54,9 @@ def tile_picked_headrope_none_po_kernel(tc, x_words, x_scales, w1, w2, ct, st, w
 
         nc.gpsimd.memset(xs_tab[:].bitcast(I32), 0)
         nc.vector.memset(wos_raw[:].bitcast(I32), 0)
+
+        ident = sb("ident", [P, P], F32)
+        make_identity(nc, ident[:])
 
         ct_v = ct.rearrange("(p t) u -> p t u", t=PACK)
         st_v = st.rearrange("(p t) u -> p t u", t=PACK)
@@ -134,7 +138,7 @@ def tile_picked_headrope_none_po_kernel(tc, x_words, x_scales, w1, w2, ct, st, w
                 nc.gpsimd.tensor_tensor(out=prod[:, t, :, 0, :], in0=plain[:].unsqueeze(1).to_broadcast([P, 2, S]), in1=trig[t][:], op=ALU.mult)
                 from_psum(t, 1, accs[1], slice(0, 2))
             else:
-                for i in range(2):
+                for i in (1, 0):
                     from_psum(t, i, accs[i], slice(0, 2))
 
         wo = sb("wo", [P, 2, N], I32)
@@ -146,7 +150,8 @@ def tile_picked_headrope_none_po_kernel(tc, x_words, x_scales, w1, w2, ct, st, w
         z_bf = [[z_all[:, (2 * b + a) * BLK * PACK : (2 * b + a + 1) * BLK * PACK] for a in range(2)] for b in range(NBLK)]
         z_codes = [sb("z_codes%d" % b, [P, 2, BLK], U32) for b in range(NBLK)]
         z_sc = [sb("z_sc%d" % b, [P, 2, BLK], U8) for b in range(NBLK)]
-        o_bf = [sb("o_bf%d" % b, [P, BLK * PACK], BF16) for b in range(NBLK)]
+        o_all = sb("o_all", [P, S * PACK], BF16)
+        o_bf = [o_all[:, b * BLK * PACK : (b + 1) * BLK * PACK] for b in range(NBLK)]
         o_f32 = [sb("o_f32%d" % b, [P, PACK, BLK], F32) for b in range(NBLK)]
         o_codes = sb("o_codes", [P, S], U32)
         o_sc = sb("o_sc", [P, S], U8)
@@ -162,8 +167,10 @@ def tile_picked_headrope_none_po_kernel(tc, x_words, x_scales, w1, w2, ct, st, w
             in1 = prod[:, :, 1 - a, 1, toks_of(b)].rearrange("p t (c i) -> p c t i", i=2)
             nc.vector.tensor_tensor(out=dst, in0=in0, in1=in1, op=(ALU.subtract, ALU.add)[a])
 
-        def quantize_z(b, a):
-            nc.vector.quantize_mx(out=z_codes[b][:, a, :].bitcast(FP8X4), scales=z_sc[b][:, a, :], in_=z_bf[b][a])
+        def quantize_z(b, first, end):
+            nc.vector.quantize_mx(out=z_codes[b][:, first:end, :].rearrange("p a n -> p (a n)").bitcast(FP8X4),
+                                  scales=z_sc[b][:, first:end, :].rearrange("p a n -> p (a n)"),
+                                  in_=z_all[:, (2 * b + first) * BLK * PACK : (2 * b + end) * BLK * PACK])
 
         def out_pass(dst, b, t, a):
             cols = slice(t * P, (t + 1) * P)
@@ -171,44 +178,65 @@ def tile_picked_headrope_none_po_kernel(tc, x_words, x_scales, w1, w2, ct, st, w
                                 rhs=z_codes[b][:, a, :].bitcast(FP8X4), rhs_scale=z_sc[b][:, a, :],
                                 start=(a == 0), stop=(a == 1))
 
-        def second_product(b):
-            acc = bank(b, [P, PACK, BLK])
+        def second_product(b, k):
+            acc = bank(k, [P, PACK, BLK])
             for t in range(PACK):
                 for a in range(2):
                     out_pass(acc[:, t, :], b, t, a)
-            nc.scalar.copy(out=o_bf[b][:].rearrange("p (n t) -> p n t", t=PACK), in_=acc[:].rearrange("p t n -> p n t"))
             nc.scalar.copy(out=o_f32[b][:], in_=acc[:])
             nc.sync.dma_start(out=out_v[:, :, toks_of(b)], in_=o_f32[b][:])
+            nc.scalar.copy(out=o_bf[b].rearrange("p (n t) -> p n t", t=PACK), in_=acc[:].rearrange("p t n -> p n t"))
 
-        def hand_on(b):
-            toks = toks_of(b)
-            nc.vector.quantize_mx(out=o_codes[:, toks].bitcast(FP8X4), scales=o_sc[:, toks], in_=o_bf[b][:])
+        def hand_on(first, end):
+            toks = slice(first * BLK, end * BLK)
+            nc.vector.quantize_mx(out=o_codes[:, toks].bitcast(FP8X4), scales=o_sc[:, toks], in_=o_all[:, first * BLK * PACK : end * BLK * PACK])
             nc.sync.dma_start(out=out_words[:, toks], in_=o_codes[:, toks].bitcast(I32))
 
+        aside = 0
         last = NBLK - 1
-        for b in range(NBLK):
-            rotate(b, 0)
-            rotate(b, 1)
-            if b >= 2:
-                hand_on(b - 2)
-            quantize_z(b, 0)
-            quantize_z(b, 1)
-            if b < last:
-                second_product(b)
-        hand_on(last - 1)
-        accs = [bank(last + t, [P, BLK]) for t in range(PACK)]
+        toks = toks_of(aside)
+        minus_eq = sb("minus_eq", [P, PACK, BLK], F32)
+        z_aside = z_all[:, : 2 * BLK * PACK]
+        for t in range(PACK):
+            nc.scalar.mul(minus_eq[:, t, :], prod[:, t, 1, 1, toks], -1.0)
+        words = bank(1, [P, 2, 2, BLK])
+        for u in range(2):
+            turned = bank(2 * u, [P, 2, 2, P])
+            for t in ((0, 1), (3, 2))[u]:
+                e = t % 2
+                for a, second in ((1, prod[:, t, 0, 1, toks]), (0, minus_eq[:, t, :])):
+                    nc.tensor.matmul(turned[:, a, e, :], lhsT=second, rhs=ident[:], is_transpose=True, start=True, stop=False)
+                    nc.tensor.matmul(turned[:, a, e, :], lhsT=prod[:, t, a, 0, toks], rhs=ident[:], is_transpose=True, start=False, stop=True)
+            pairs = sb("pairs%d" % u, [P, 2, 2 * P], BF16)
+            nc.scalar.copy(out=pairs[:].rearrange("n a (p e) -> n a p e", e=2), in_=turned[:].rearrange("n a e p -> n a p e"))
+            for a in range(2):
+                nc.tensor.transpose(words[:, a, u, :], pairs[:, a, :].bitcast(F32), ident[:])
+        nc.scalar.copy(out=z_aside.bitcast(F32).rearrange("p (a n u) -> p a n u", a=2, u=2), in_=words[:].rearrange("p a u n -> p a n u"))
+        rotate(1, 0)
+        rotate(1, 1)
+        rotate(2, 0)
+        quantize_z(1, 0, 2)
+        second_product(1, 3)
+        rotate(2, 1)
+        quantize_z(aside, 0, 2)
+        second_product(aside, 0)
+        rotate(last, 0)
+        quantize_z(2, 0, 2)
+        second_product(2, 4)
+        rotate(last, 1)
+        quantize_z(last, 0, 1)
+        quantize_z(last, 1, 2)
+        hand_on(0, 2)
+        accs = [bank(k, [P, BLK]) for k in (5, 6, 7, 2)]
         for t in range(PACK):
             out_pass(accs[t][:], last, t, 0)
         for t in range(PACK):
             out_pass(accs[t][:], last, t, 1)
-            if t % 2:
-                nc.vector.tensor_copy(out=o_f32[last][:, t, :], in_=accs[t][:])
-            else:
-                nc.scalar.copy(out=o_f32[last][:, t, :], in_=accs[t][:])
+            nc.vector.tensor_copy(out=o_f32[last][:, t, :], in_=accs[t][:])
         nc.sync.dma_start(out=out_v[:, :, toks_of(last)], in_=o_f32[last][:])
-        nc.vector.tensor_copy(out=o_bf[last][:].rearrange("p (c i t) -> p c t i", i=4, t=PACK),
+        nc.vector.tensor_copy(out=o_bf[last].rearrange("p (c i t) -> p c t i", i=4, t=PACK),
                               in_=o_f32[last][:].rearrange("p t (c i) -> p c t i", i=4))
-        hand_on(last)
+        hand_on(2, 4)
         for q in range(4):
             queue = nc.scalar if q % 2 else nc.sync
             queue.dma_start(out=out_2[0][4 * q : 4 * q + 4, :].bitcast(I32), in_=o_sc[32 * q : 32 * q + 4, :].bitcast(I32))

@@ -185,7 +185,8 @@ def tile_picked_headrope_none_po_kernel(tc, x_words, x_scales, w1, w2, ct, st, w
                     out_pass(acc[:, t, :], b, t, a)
             nc.scalar.copy(out=o_f32[b][:], in_=acc[:])
             nc.sync.dma_start(out=out_v[:, :, toks_of(b)], in_=o_f32[b][:])
-            nc.scalar.copy(out=o_bf[b].rearrange("p (n t) -> p n t", t=PACK), in_=acc[:].rearrange("p t n -> p n t"))
+            if b < 2:
+                nc.scalar.copy(out=o_bf[b].rearrange("p (n t) -> p n t", t=PACK), in_=acc[:].rearrange("p t n -> p n t"))
 
         def hand_on(first, end):
             toks = slice(first * BLK, end * BLK)
@@ -200,6 +201,7 @@ def tile_picked_headrope_none_po_kernel(tc, x_words, x_scales, w1, w2, ct, st, w
         for t in range(PACK):
             nc.scalar.mul(minus_eq[:, t, :], prod[:, t, 1, 1, toks], -1.0)
         words = bank(1, [P, 2, 2, BLK])
+        pairs = [sb("pairs%d" % u, [P, 2, 2 * P], BF16) for u in range(2)]
         for u in range(2):
             turned = bank(2 * u, [P, 2, 2, P])
             for t in ((0, 1), (3, 2))[u]:
@@ -207,22 +209,23 @@ def tile_picked_headrope_none_po_kernel(tc, x_words, x_scales, w1, w2, ct, st, w
                 for a, second in ((1, prod[:, t, 0, 1, toks]), (0, minus_eq[:, t, :])):
                     nc.tensor.matmul(turned[:, a, e, :], lhsT=second, rhs=ident[:], is_transpose=True, start=True, stop=False)
                     nc.tensor.matmul(turned[:, a, e, :], lhsT=prod[:, t, a, 0, toks], rhs=ident[:], is_transpose=True, start=False, stop=True)
-            pairs = sb("pairs%d" % u, [P, 2, 2 * P], BF16)
-            nc.scalar.copy(out=pairs[:].rearrange("n a (p e) -> n a p e", e=2), in_=turned[:].rearrange("n a e p -> n a p e"))
+            nc.scalar.copy(out=pairs[u][:].rearrange("n a (p e) -> n a p e", e=2), in_=turned[:].rearrange("n a e p -> n a p e"))
+        for u in range(2):
             for a in range(2):
-                nc.tensor.transpose(words[:, a, u, :], pairs[:, a, :].bitcast(F32), ident[:])
+                nc.tensor.transpose(words[:, a, u, :], pairs[u][:, a, :].bitcast(F32), ident[:])
         nc.scalar.copy(out=z_aside.bitcast(F32).rearrange("p (a n u) -> p a n u", a=2, u=2), in_=words[:].rearrange("p a u n -> p a n u"))
         rotate(1, 0)
         rotate(1, 1)
-        rotate(2, 0)
-        quantize_z(1, 0, 2)
+        quantize_z(1, 0, 1)
+        quantize_z(1, 1, 2)
         second_product(1, 3)
+        rotate(2, 0)
         rotate(2, 1)
         quantize_z(aside, 0, 2)
         second_product(aside, 0)
-        rotate(last, 0)
         quantize_z(2, 0, 2)
         second_product(2, 4)
+        rotate(last, 0)
         rotate(last, 1)
         quantize_z(last, 0, 1)
         quantize_z(last, 1, 2)
@@ -232,11 +235,16 @@ def tile_picked_headrope_none_po_kernel(tc, x_words, x_scales, w1, w2, ct, st, w
             out_pass(accs[t][:], last, t, 0)
         for t in range(PACK):
             out_pass(accs[t][:], last, t, 1)
-            nc.vector.tensor_copy(out=o_f32[last][:, t, :], in_=accs[t][:])
+            if t % 2:
+                nc.vector.tensor_copy(out=o_f32[last][:, t, :], in_=accs[t][:])
+            else:
+                nc.scalar.copy(out=o_f32[last][:, t, :], in_=accs[t][:])
         nc.sync.dma_start(out=out_v[:, :, toks_of(last)], in_=o_f32[last][:])
-        nc.vector.tensor_copy(out=o_bf[last].rearrange("p (c i t) -> p c t i", i=4, t=PACK),
-                              in_=o_f32[last][:].rearrange("p t (c i) -> p c t i", i=4))
-        hand_on(2, 4)
+        for b in (2, last):
+            nc.vector.tensor_copy(out=o_bf[b].rearrange("p (c i t) -> p c t i", i=4, t=PACK),
+                                  in_=o_f32[b][:].rearrange("p t (c i) -> p c t i", i=4))
+        for b in (2, last):
+            hand_on(b, b + 1)
         for q in range(4):
             queue = nc.scalar if q % 2 else nc.sync
             queue.dma_start(out=out_2[0][4 * q : 4 * q + 4, :].bitcast(I32), in_=o_sc[32 * q : 32 * q + 4, :].bitcast(I32))

@@ -185,8 +185,12 @@ def tile_picked_headrope_none_po_kernel(tc, x_words, x_scales, w1, w2, ct, st, w
                     out_pass(acc[:, t, :], b, t, a)
             nc.scalar.copy(out=o_f32[b][:], in_=acc[:])
             nc.sync.dma_start(out=out_v[:, :, toks_of(b)], in_=o_f32[b][:])
-            if b < 2:
+            if b != aside:
                 nc.scalar.copy(out=o_bf[b].rearrange("p (n t) -> p n t", t=PACK), in_=acc[:].rearrange("p t n -> p n t"))
+
+        def round_out(b):
+            nc.vector.tensor_copy(out=o_bf[b].rearrange("p (c i t) -> p c t i", i=4, t=PACK),
+                                  in_=o_f32[b][:].rearrange("p t (c i) -> p c t i", i=4))
 
         def hand_on(first, end):
             toks = slice(first * BLK, end * BLK)
@@ -210,39 +214,45 @@ def tile_picked_headrope_none_po_kernel(tc, x_words, x_scales, w1, w2, ct, st, w
                     nc.tensor.matmul(turned[:, a, e, :], lhsT=second, rhs=ident[:], is_transpose=True, start=True, stop=False)
                     nc.tensor.matmul(turned[:, a, e, :], lhsT=prod[:, t, a, 0, toks], rhs=ident[:], is_transpose=True, start=False, stop=True)
             nc.scalar.copy(out=pairs[u][:].rearrange("n a (p e) -> n a p e", e=2), in_=turned[:].rearrange("n a e p -> n a p e"))
+        toks2 = toks_of(2)
+        turned2 = bank(3, [P, 2, 2, P])
+        for t in (0, 1, 3, 2):
+            nc.tensor.matmul(turned2[:, t // 2, t % 2, :], lhsT=prod[:, t, 0, 1, toks2], rhs=ident[:], is_transpose=True, start=True, stop=False)
+            nc.tensor.matmul(turned2[:, t // 2, t % 2, :], lhsT=prod[:, t, 1, 0, toks2], rhs=ident[:], is_transpose=True, start=False, stop=True)
+        pairs2 = sb("pairs2", [P, 2, 2 * P], BF16)
+        nc.scalar.copy(out=pairs2[:].rearrange("n u (p e) -> n u p e", e=2), in_=turned2[:].rearrange("n u e p -> n u p e"))
         for u in range(2):
             for a in range(2):
                 nc.tensor.transpose(words[:, a, u, :], pairs[u][:, a, :].bitcast(F32), ident[:])
+        words2 = bank(4, [P, 2, BLK])
+        for u in range(2):
+            nc.tensor.transpose(words2[:, u, :], pairs2[:, u, :].bitcast(F32), ident[:])
         nc.scalar.copy(out=z_aside.bitcast(F32).rearrange("p (a n u) -> p a n u", a=2, u=2), in_=words[:].rearrange("p a u n -> p a n u"))
+        nc.scalar.copy(out=z_bf[2][1].bitcast(F32).rearrange("p (n u) -> p n u", u=2), in_=words2[:].rearrange("p u n -> p n u"))
         rotate(1, 0)
         rotate(1, 1)
         quantize_z(1, 0, 1)
         quantize_z(1, 1, 2)
-        second_product(1, 3)
+        second_product(1, 0)
         rotate(2, 0)
-        rotate(2, 1)
-        quantize_z(aside, 0, 2)
-        second_product(aside, 0)
-        quantize_z(2, 0, 2)
-        second_product(2, 4)
         rotate(last, 0)
+        quantize_z(aside, 0, 2)
+        second_product(aside, 2)
+        quantize_z(2, 0, 2)
+        second_product(2, 3)
         rotate(last, 1)
         quantize_z(last, 0, 1)
         quantize_z(last, 1, 2)
-        hand_on(0, 2)
-        accs = [bank(k, [P, BLK]) for k in (5, 6, 7, 2)]
+        round_out(aside)
+        accs = [bank(k, [P, BLK]) for k in (5, 6, 7, 1)]
         for t in range(PACK):
             out_pass(accs[t][:], last, t, 0)
         for t in range(PACK):
             out_pass(accs[t][:], last, t, 1)
-            if t % 2:
-                nc.vector.tensor_copy(out=o_f32[last][:, t, :], in_=accs[t][:])
-            else:
-                nc.scalar.copy(out=o_f32[last][:, t, :], in_=accs[t][:])
+            nc.vector.tensor_copy(out=o_f32[last][:, t, :], in_=accs[t][:])
         nc.sync.dma_start(out=out_v[:, :, toks_of(last)], in_=o_f32[last][:])
-        for b in (2, last):
-            nc.vector.tensor_copy(out=o_bf[b].rearrange("p (c i t) -> p c t i", i=4, t=PACK),
-                                  in_=o_f32[b][:].rearrange("p t (c i) -> p c t i", i=4))
+        hand_on(0, 2)
+        round_out(last)
         for b in (2, last):
             hand_on(b, b + 1)
         for q in range(4):

@@ -20,6 +20,7 @@ PACK = 4
 BLK = 128
 NBLK = S // BLK
 W1_SPLIT = 92
+ASIDE = 1
 
 
 def tile_picked_headrope_none_po_kernel(tc, x_words, x_scales, w1, w2, ct, st, w3_words, w3_scales, w4_words, w4_scales, offs, pos, out_0, out_1, out_2):
@@ -61,9 +62,8 @@ def tile_picked_headrope_none_po_kernel(tc, x_words, x_scales, w1, w2, ct, st, w
         ct_v = ct.rearrange("(p t) u -> p t u", t=PACK)
         st_v = st.rearrange("(p t) u -> p t u", t=PACK)
 
-        def load_tables(t):
-            nc.sync.dma_start(out=c_tab[t][:], in_=ct_v[:, t, :])
-            nc.sync.dma_start(out=s_tab[t][:], in_=st_v[:, t, :])
+        tabs = (c_tab, s_tab)
+        tab_order = ((0, 0), (1, 0), (0, 2), (0, 1), (1, 2), (1, 1), (0, 3), (1, 3))
 
         nc.sync.dma_start(offs_t[:], offs)
         nc.sync.dma_start(out=x_tab[:].bitcast(I32), in_=words_of(x_words))
@@ -71,13 +71,15 @@ def tile_picked_headrope_none_po_kernel(tc, x_words, x_scales, w1, w2, ct, st, w
         nc.sync.dma_start(out=w_raw[0][:], in_=w1.rearrange("(p j) c -> p j c", j=PACK))
         nc.sync.dma_start(pos_t[:], pos)
         nc.sync.dma_start(out=w_raw[1][:], in_=w2.rearrange("(p j) c -> p j c", j=PACK))
-        load_tables(0)
-        for t in range(1, PACK):
-            load_tables(t)
-        nc.sync.dma_start(out=wo_raw[:, 0, :], in_=words_of(w3_words))
-        nc.sync.dma_start(out=wo_raw[:, 1, :], in_=words_of(w4_words))
-        load_scale_rows(nc.sync, wos_raw, 0, w3_scales)
-        load_scale_rows(nc.sync, wos_raw, 4, w4_scales)
+        for n, (k, t) in enumerate(tab_order):
+            if (k, t) == (0, 3):
+                nc.sync.dma_start(out=wo_raw[:, 0, :], in_=words_of(w3_words))
+                nc.sync.dma_start(out=wo_raw[:, 1, :], in_=words_of(w4_words))
+            nc.sync.dma_start(out=tabs[k][t][:], in_=(ct_v, st_v)[k][:, t, :])
+            if 2 <= n < 6:
+                for a, dram in enumerate((w3_scales, w4_scales)):
+                    q = n - 2
+                    nc.sync.dma_start(out=wos_raw[32 * q + 4 * a : 32 * q + 4 * a + 4, :].bitcast(I32), in_=dram[0][4 * q : 4 * q + 4, :].bitcast(I32))
 
         x_codes = sb("x_codes", [P, S], U32)
         x_sc = sb("x_sc", [P, S], U8)
@@ -96,19 +98,15 @@ def tile_picked_headrope_none_po_kernel(tc, x_words, x_scales, w1, w2, ct, st, w
         def quantize_w(i):
             nc.vector.quantize_mx(out=w_codes[i][:].bitcast(FP8X4), scales=w_sc[i][:], in_=w_bf[i][:])
 
-        def project(i, t):
-            acc = bank(2 * t + i, [P, S])
+        def project(i, t, k):
+            acc = bank(k, [P, S])
             cols = slice(t * P, (t + 1) * P)
             nc.tensor.matmul_mx(out=acc[:], lhsT=w_codes[i][:, cols].bitcast(FP8X4), lhsT_scale=w_sc[i][:, cols],
                                 rhs=x_codes[:].bitcast(FP8X4), rhs_scale=x_sc[:], start=True, stop=True)
             return acc
 
-        trig = [sb("trig%d" % t, [P, 2, S], F32) for t in range(PACK)]
-        prod = sb("prod", [P, PACK, 2, 2, S], F32)
-
-        def look_up(t):
-            nc.vector.tensor_copy(trig[t][:, 0, :], c_tab[t][:].indirect(pos_t[:]))
-            nc.vector.tensor_copy(trig[t][:, 1, :], s_tab[t][:].indirect(pos_t[:]))
+        trig = [[sb("trig%d_%d" % (k, t), [P, S], F32) for t in range(PACK)] for k in range(2)]
+        prod = sb("prod", [P, PACK, 2, NBLK, 2, BLK], F32)
 
         for i in range(2):
             dst, src = deal_views(i, slice(0, W1_SPLIT))
@@ -116,38 +114,82 @@ def tile_picked_headrope_none_po_kernel(tc, x_words, x_scales, w1, w2, ct, st, w
             dst, src = deal_views(i, slice(W1_SPLIT, P))
             nc.scalar.copy(out=dst, in_=src)
             quantize_w(i)
-        for t in range(PACK):
-            look_up(t)
+        y_bank = (0, 5, 2, 4)
+        e_bank = (1, 6, 3, 7)
+        y = {}
+        e = {}
+        for t in (0, 2, 1, 3):
+            y[t] = project(0, t, y_bank[t])
+            e[t] = project(1, t, e_bank[t])
+        plain = {t: sb("plain%d" % t, [P, 3, S], F32) for t in (0, 2)}
+        for t in (0, 2):
+            nc.scalar.copy(out=plain[t][:, 1, :], in_=y[t][:])
+            nc.scalar.copy(out=plain[t][:, 2, :], in_=e[t][:])
+            nc.scalar.mul(plain[t][:, 0, :], e[t][:], -1.0)
+        plain3 = sb("plain3", [P, 3, S], F32)
+        nc.scalar.copy(out=plain3[:, 1, :], in_=y[3][:])
+        nc.scalar.copy(out=plain3[:, 2, :], in_=e[3][:])
+        plain[3] = plain3
 
-        def from_psum(t, i, acc, factors):
-            n = factors.stop - factors.start
-            nc.vector.tensor_tensor(out=prod[:, t, factors, i, :], in0=acc[:].unsqueeze(1).to_broadcast([P, n, S]),
-                                    in1=trig[t][:, factors, :], op=ALU.mult)
+        def blocks(ap):
+            return ap.rearrange("p (b n) -> p b n", b=NBLK)
 
-        for t in range(PACK):
-            accs = [project(i, t) for i in range(2)]
-            if t < 2:
-                plain = sb("plain%d" % t, [P, 2, S], F32)
-                for i in range(2):
-                    nc.scalar.copy(out=plain[:, i, :], in_=accs[i][:])
-                for a in range(2):
-                    nc.gpsimd.tensor_tensor(out=prod[:, t, a, :, :], in0=plain[:], in1=trig[t][:, a, :].unsqueeze(1).to_broadcast([P, 2, S]), op=ALU.mult)
-            elif t == 2:
-                plain = sb("plain%d" % t, [P, S], F32)
-                nc.scalar.copy(out=plain[:], in_=accs[0][:])
-                nc.gpsimd.tensor_tensor(out=prod[:, t, :, 0, :], in0=plain[:].unsqueeze(1).to_broadcast([P, 2, S]), in1=trig[t][:], op=ALU.mult)
-                from_psum(t, 1, accs[1], slice(0, 2))
+        def from_psum(t, k, a, bs):
+            dst = prod[:, t, k, bs, a, :]
+            factor = blocks(trig[k][t][:])[:, bs]
+            if k == 1 and a == 0:
+                nc.vector.scalar_tensor_tensor(out=dst, in0=blocks(e[t][:])[:, bs], scalar=-1.0, in1=factor, op0=ALU.mult, op1=ALU.mult)
             else:
-                for i in (1, 0):
-                    from_psum(t, i, accs[i], slice(0, 2))
+                nc.vector.tensor_tensor(out=dst, in0=blocks((y if k == a else e)[t][:])[:, bs], in1=factor, op=ALU.mult)
 
-        wo = sb("wo", [P, 2, N], I32)
-        nc.vector.tensor_copy(out=wo[:].rearrange("p a (t m) -> p a m t", t=PACK), in_=wo_raw[:].rearrange("p a (m t) -> p a m t", t=PACK))
-        wos = sb("wos", [P, N], U8)
-        nc.vector.tensor_copy(out=wos[:].rearrange("p (t m) -> p m t", t=PACK), in_=wos_raw[:].rearrange("p (m t) -> p m t", t=PACK))
+        for k, t in tab_order:
+            nc.vector.tensor_copy(trig[k][t][:], tabs[k][t][:].indirect(pos_t[:]))
+            for bs in (slice(0, ASIDE), slice(ASIDE, NBLK)) if t == 3 else (slice(0, NBLK),):
+                if t in (0, 2) or (k, t) == (0, 3):
+                    nc.gpsimd.tensor_tensor(out=prod[:, t, k, bs].rearrange("p b a n -> p a b n"),
+                                            in0=plain[t][:, 1 - k : 3 - k, :].rearrange("p a (b n) -> p a b n", b=NBLK)[:, :, bs],
+                                            in1=blocks(trig[k][t][:])[:, bs].unsqueeze(1).to_broadcast([P, 2, bs.stop - bs.start, BLK]), op=ALU.mult)
+                else:
+                    for a in range(2):
+                        from_psum(t, k, a, bs)
 
-        z_all = sb("z_all", [P, 2 * S * PACK], BF16, "wos_raw")
-        z_bf = [[z_all[:, (2 * b + a) * BLK * PACK : (2 * b + a + 1) * BLK * PACK] for a in range(2)] for b in range(NBLK)]
+        aside = 0
+        last = NBLK - 1
+        z_bf = [sb("z_bf%d" % b, [P, 2 * BLK * PACK], BF16) for b in range(NBLK)]
+        halves = {b: sb("halves%d" % b, [P, 2, 2 * BLK], F32) for b in range(1, NBLK)}
+
+        def add_turned(dst, t, b):
+            for a in range(2):
+                for k in range(2):
+                    nc.tensor.matmul(dst[:, a, t % 2, :], lhsT=prod[:, t, k, b, a, :], rhs=ident[:], is_transpose=True, start=(k == 0), stop=(k == 1))
+
+        def turn_back(src, words, name):
+            pairs = sb(name, [P, 2, 2 * P], BF16)
+            nc.scalar.copy(out=pairs[:].rearrange("n a (p e) -> n a p e", e=2), in_=src[:].rearrange("n a e p -> n a p e"))
+            dst = words()
+            for a in range(2):
+                nc.tensor.transpose(dst[:, a, :], pairs[:, a, :].bitcast(F32), ident[:])
+            return dst
+
+        order = (1, 2, last, aside)
+        turned = {b: bank(b, [P, 2, 2, P]) for b in order}
+        for t in range(2):
+            for b in order:
+                add_turned(turned[b], t, b)
+        for b in order[:-1]:
+            words = turn_back(turned[b], lambda: bank(b, [P, 2, BLK]), "pairs%d" % b)
+            nc.scalar.copy(out=halves[b][:, 0, :], in_=words[:].rearrange("p a n -> p (a n)"))
+        held = []
+
+        def hold():
+            held.append(bank(aside, [P, 2, 2, BLK]))
+            return held[0][:, 0]
+
+        turn_back(turned[aside], hold, "pairs_low")
+        upper = bank(5, [P, 2, 2, P])
+        for t in (2, 3):
+            add_turned(upper, t, aside)
+
         z_codes = [sb("z_codes%d" % b, [P, 2, BLK], U32) for b in range(NBLK)]
         z_sc = [sb("z_sc%d" % b, [P, 2, BLK], U8) for b in range(NBLK)]
         o_all = sb("o_all", [P, S * PACK], BF16)
@@ -157,36 +199,34 @@ def tile_picked_headrope_none_po_kernel(tc, x_words, x_scales, w1, w2, ct, st, w
         o_sc = sb("o_sc", [P, S], U8)
         out_v = out_0.rearrange("(p t) n -> p t n", t=PACK)
         out_words = words_of(out_1)
+        wo = sb("wo", [P, 2, N], I32, "trig1_3")
+        wos = sb("wos", [P, N], U8, "s_tab3")
 
         def toks_of(b):
             return slice(b * BLK, (b + 1) * BLK)
 
-        def rotate(b, a):
-            dst = z_bf[b][a].rearrange("p (c i t) -> p c t i", i=2, t=PACK)
-            in0 = prod[:, :, a, 0, toks_of(b)].rearrange("p t (c i) -> p c t i", i=2)
-            in1 = prod[:, :, 1 - a, 1, toks_of(b)].rearrange("p t (c i) -> p c t i", i=2)
-            nc.vector.tensor_tensor(out=dst, in0=in0, in1=in1, op=(ALU.subtract, ALU.add)[a])
+        def rotate(b):
+            terms = [prod[:, 2:4, k, b].rearrange("p e a (c i) -> p (a c) e i", i=4) for k in range(2)]
+            nc.vector.tensor_tensor(out=halves[b][:, 1, :].bitcast(BF16).rearrange("p (c i e) -> p c e i", i=4, e=2), in0=terms[0], in1=terms[1], op=ALU.add)
+            nc.scalar.copy(out=z_bf[b][:].bitcast(F32).rearrange("p (n u) -> p n u", u=2), in_=halves[b][:].rearrange("p u n -> p n u"))
 
-        def quantize_z(b, first, end):
-            nc.vector.quantize_mx(out=z_codes[b][:, first:end, :].rearrange("p a n -> p (a n)").bitcast(FP8X4),
-                                  scales=z_sc[b][:, first:end, :].rearrange("p a n -> p (a n)"),
-                                  in_=z_all[:, (2 * b + first) * BLK * PACK : (2 * b + end) * BLK * PACK])
+        def quantize_z(b):
+            nc.vector.quantize_mx(out=z_codes[b][:].rearrange("p a n -> p (a n)").bitcast(FP8X4),
+                                  scales=z_sc[b][:].rearrange("p a n -> p (a n)"), in_=z_bf[b][:])
 
-        def out_pass(dst, b, t, a):
-            cols = slice(t * P, (t + 1) * P)
-            nc.tensor.matmul_mx(out=dst, lhsT=wo[:, a, cols].bitcast(FP8X4), lhsT_scale=wos[4 * a :, cols],
-                                rhs=z_codes[b][:, a, :].bitcast(FP8X4), rhs_scale=z_sc[b][:, a, :],
-                                start=(a == 0), stop=(a == 1))
+        def out_passes(acc, b, ts):
+            for n, t in enumerate(ts):
+                cols = slice(t * P, (t + 1) * P)
+                for a in range(2):
+                    nc.tensor.matmul_mx(out=acc[:, n, :], lhsT=wo[:, a, cols].bitcast(FP8X4), lhsT_scale=wos[4 * a :, cols],
+                                        rhs=z_codes[b][:, a, :].bitcast(FP8X4), rhs_scale=z_sc[b][:, a, :],
+                                        start=(a == 0), stop=(a == 1))
 
         def second_product(b, k):
             acc = bank(k, [P, PACK, BLK])
-            for t in range(PACK):
-                for a in range(2):
-                    out_pass(acc[:, t, :], b, t, a)
+            out_passes(acc, b, range(PACK))
             nc.scalar.copy(out=o_f32[b][:], in_=acc[:])
             nc.sync.dma_start(out=out_v[:, :, toks_of(b)], in_=o_f32[b][:])
-            if b != aside:
-                nc.scalar.copy(out=o_bf[b].rearrange("p (n t) -> p n t", t=PACK), in_=acc[:].rearrange("p t n -> p n t"))
 
         def round_out(b):
             nc.vector.tensor_copy(out=o_bf[b].rearrange("p (c i t) -> p c t i", i=4, t=PACK),
@@ -197,64 +237,36 @@ def tile_picked_headrope_none_po_kernel(tc, x_words, x_scales, w1, w2, ct, st, w
             nc.vector.quantize_mx(out=o_codes[:, toks].bitcast(FP8X4), scales=o_sc[:, toks], in_=o_all[:, first * BLK * PACK : end * BLK * PACK])
             nc.sync.dma_start(out=out_words[:, toks], in_=o_codes[:, toks].bitcast(I32))
 
-        aside = 0
-        last = NBLK - 1
-        toks = toks_of(aside)
-        minus_eq = sb("minus_eq", [P, PACK, BLK], F32)
-        z_aside = z_all[:, : 2 * BLK * PACK]
-        for t in range(PACK):
-            nc.scalar.mul(minus_eq[:, t, :], prod[:, t, 1, 1, toks], -1.0)
-        words = bank(1, [P, 2, 2, BLK])
-        pairs = [sb("pairs%d" % u, [P, 2, 2 * P], BF16) for u in range(2)]
-        for u in range(2):
-            turned = bank(2 * u, [P, 2, 2, P])
-            for t in ((0, 1), (3, 2))[u]:
-                e = t % 2
-                for a, second in ((1, prod[:, t, 0, 1, toks]), (0, minus_eq[:, t, :])):
-                    nc.tensor.matmul(turned[:, a, e, :], lhsT=second, rhs=ident[:], is_transpose=True, start=True, stop=False)
-                    nc.tensor.matmul(turned[:, a, e, :], lhsT=prod[:, t, a, 0, toks], rhs=ident[:], is_transpose=True, start=False, stop=True)
-            nc.scalar.copy(out=pairs[u][:].rearrange("n a (p e) -> n a p e", e=2), in_=turned[:].rearrange("n a e p -> n a p e"))
-        toks2 = toks_of(2)
-        turned2 = bank(3, [P, 2, 2, P])
-        for t in (0, 1, 3, 2):
-            nc.tensor.matmul(turned2[:, t // 2, t % 2, :], lhsT=prod[:, t, 0, 1, toks2], rhs=ident[:], is_transpose=True, start=True, stop=False)
-            nc.tensor.matmul(turned2[:, t // 2, t % 2, :], lhsT=prod[:, t, 1, 0, toks2], rhs=ident[:], is_transpose=True, start=False, stop=True)
-        pairs2 = sb("pairs2", [P, 2, 2 * P], BF16)
-        nc.scalar.copy(out=pairs2[:].rearrange("n u (p e) -> n u p e", e=2), in_=turned2[:].rearrange("n u e p -> n u p e"))
-        for u in range(2):
-            for a in range(2):
-                nc.tensor.transpose(words[:, a, u, :], pairs[u][:, a, :].bitcast(F32), ident[:])
-        words2 = bank(4, [P, 2, BLK])
-        for u in range(2):
-            nc.tensor.transpose(words2[:, u, :], pairs2[:, u, :].bitcast(F32), ident[:])
-        nc.scalar.copy(out=z_aside.bitcast(F32).rearrange("p (a n u) -> p a n u", a=2, u=2), in_=words[:].rearrange("p a u n -> p a n u"))
-        nc.scalar.copy(out=z_bf[2][1].bitcast(F32).rearrange("p (n u) -> p n u", u=2), in_=words2[:].rearrange("p u n -> p n u"))
-        rotate(1, 0)
-        rotate(1, 1)
-        quantize_z(1, 0, 1)
-        quantize_z(1, 1, 2)
-        second_product(1, 0)
-        rotate(2, 0)
-        rotate(last, 0)
-        quantize_z(aside, 0, 2)
+        for k in (e_bank[3], y_bank[3]):
+            for n in range(2):
+                project(0, 0, k)
+        rotate(1)
+        turn_back(upper, lambda: held[0][:, 1], "pairs_high")
+        nc.scalar.copy(out=z_bf[aside][:].bitcast(F32).rearrange("p (n u) -> p n u", u=2), in_=held[0][:].rearrange("p u a n -> p (a n) u"))
+        nc.vector.tensor_copy(out=wo[:].rearrange("p a (t m) -> p a m t", t=PACK), in_=wo_raw[:].rearrange("p a (m t) -> p a m t", t=PACK))
+        nc.vector.tensor_copy(out=wos[:].rearrange("p (t m) -> p m t", t=PACK), in_=wos_raw[:].rearrange("p (m t) -> p m t", t=PACK))
+        quantize_z(1)
+        rotate(2)
+        rotate(last)
+        quantize_z(2)
+        quantize_z(aside)
+        quantize_z(last)
+        second_product(1, 6)
+        second_product(2, 1)
         second_product(aside, 2)
-        quantize_z(2, 0, 2)
-        second_product(2, 3)
-        rotate(last, 1)
-        quantize_z(last, 0, 1)
-        quantize_z(last, 1, 2)
+        accs = [bank(k, [P, 2, BLK]) for k in (3, 5)]
+        for h in range(2):
+            out_passes(accs[h], last, (2 * h, 2 * h + 1))
+        nc.scalar.copy(out=o_f32[last][:, 0:2, :], in_=accs[0][:])
+        round_out(1)
         round_out(aside)
-        accs = [bank(k, [P, BLK]) for k in (5, 6, 7, 1)]
-        for t in range(PACK):
-            out_pass(accs[t][:], last, t, 0)
-        for t in range(PACK):
-            out_pass(accs[t][:], last, t, 1)
-            nc.vector.tensor_copy(out=o_f32[last][:, t, :], in_=accs[t][:])
-        nc.sync.dma_start(out=out_v[:, :, toks_of(last)], in_=o_f32[last][:])
+        round_out(2)
         hand_on(0, 2)
+        nc.vector.tensor_copy(out=o_f32[last][:, 2:4, :], in_=accs[1][:])
+        nc.sync.dma_start(out=out_v[:, :, toks_of(last)], in_=o_f32[last][:])
+        hand_on(2, 3)
         round_out(last)
-        for b in (2, last):
-            hand_on(b, b + 1)
+        hand_on(last, last + 1)
         for q in range(4):
             queue = nc.scalar if q % 2 else nc.sync
             queue.dma_start(out=out_2[0][4 * q : 4 * q + 4, :].bitcast(I32), in_=o_sc[32 * q : 32 * q + 4, :].bitcast(I32))

@@ -27,6 +27,7 @@ def tile_picked_headrope_none_po_kernel(tc, x_words, x_scales, w1, w2, ct, st, w
     nc = tc.nc
     with ExitStack() as ctx:
         keep = ctx.enter_context(tc.tile_pool(name="keep", bufs=1))
+        reused = ctx.enter_context(tc.tile_pool(name="reused", bufs=1))
         psum = ctx.enter_context(tc.psum_pool(name="psum", bufs=1))
 
         def sb(name, shape, dtype, tag=""):
@@ -71,15 +72,14 @@ def tile_picked_headrope_none_po_kernel(tc, x_words, x_scales, w1, w2, ct, st, w
         nc.sync.dma_start(out=w_raw[0][:], in_=w1.rearrange("(p j) c -> p j c", j=PACK))
         nc.sync.dma_start(pos_t[:], pos)
         nc.sync.dma_start(out=w_raw[1][:], in_=w2.rearrange("(p j) c -> p j c", j=PACK))
-        for n, (k, t) in enumerate(tab_order):
-            if (k, t) == (0, 3):
-                nc.sync.dma_start(out=wo_raw[:, 0, :], in_=words_of(w3_words))
-                nc.sync.dma_start(out=wo_raw[:, 1, :], in_=words_of(w4_words))
-            nc.sync.dma_start(out=tabs[k][t][:], in_=(ct_v, st_v)[k][:, t, :])
-            if 2 <= n < 6:
-                for a, dram in enumerate((w3_scales, w4_scales)):
-                    q = n - 2
-                    nc.sync.dma_start(out=wos_raw[32 * q + 4 * a : 32 * q + 4 * a + 4, :].bitcast(I32), in_=dram[0][4 * q : 4 * q + 4, :].bitcast(I32))
+        wide = [(tabs[k][t][:], (ct_v, st_v)[k][:, t, :]) for k, t in tab_order]
+        wide[6:6] = [(wo_raw[:, 0, :], words_of(w3_words)), (wo_raw[:, 1, :], words_of(w4_words))]
+        narrow = [(wos_raw[32 * q + 4 * a : 32 * q + 4 * a + 4, :].bitcast(I32), dram[0][4 * q : 4 * q + 4, :].bitcast(I32))
+                  for a, dram in enumerate((w3_scales, w4_scales)) for q in range(4)]
+        for n, (dst, src) in enumerate(wide):
+            nc.sync.dma_start(out=dst, in_=src)
+            if n < len(narrow):
+                nc.sync.dma_start(out=narrow[n][0], in_=narrow[n][1])
 
         x_codes = sb("x_codes", [P, S], U32)
         x_sc = sb("x_sc", [P, S], U8)
@@ -105,7 +105,8 @@ def tile_picked_headrope_none_po_kernel(tc, x_words, x_scales, w1, w2, ct, st, w
                                 rhs=x_codes[:].bitcast(FP8X4), rhs_scale=x_sc[:], start=True, stop=True)
             return acc
 
-        trig = [[sb("trig%d_%d" % (k, t), [P, S], F32) for t in range(PACK)] for k in range(2)]
+        trig = [[sb("trig%d_%d" % (k, t), [P, S], F32) if (k, t) != (1, 3) else None for t in range(PACK)] for k in range(2)]
+        trig[1][3] = reused.tile([P, S], F32, name="last_sines", offset=0, align_bytes=64)
         prod = sb("prod", [P, PACK, 2, NBLK, 2, BLK], F32)
 
         for i in range(2):
@@ -199,8 +200,8 @@ def tile_picked_headrope_none_po_kernel(tc, x_words, x_scales, w1, w2, ct, st, w
         o_sc = sb("o_sc", [P, S], U8)
         out_v = out_0.rearrange("(p t) n -> p t n", t=PACK)
         out_words = words_of(out_1)
-        wo = sb("wo", [P, 2, N], I32, "trig1_3")
-        wos = sb("wos", [P, N], U8, "s_tab3")
+        wo = reused.tile([P, 2, N], I32, name="wo", offset=N, align_bytes=64)
+        wos = reused.tile([P, N], U8, name="wos", offset=0, align_bytes=64)
 
         def toks_of(b):
             return slice(b * BLK, (b + 1) * BLK)
@@ -208,7 +209,9 @@ def tile_picked_headrope_none_po_kernel(tc, x_words, x_scales, w1, w2, ct, st, w
         def rotate(b):
             terms = [prod[:, 2:4, k, b].rearrange("p e a (c i) -> p (a c) e i", i=4) for k in range(2)]
             nc.vector.tensor_tensor(out=halves[b][:, 1, :].bitcast(BF16).rearrange("p (c i e) -> p c e i", i=4, e=2), in0=terms[0], in1=terms[1], op=ALU.add)
-            nc.scalar.copy(out=z_bf[b][:].bitcast(F32).rearrange("p (n u) -> p n u", u=2), in_=halves[b][:].rearrange("p u n -> p n u"))
+
+        def weave(b, copy):
+            copy(out=z_bf[b][:].bitcast(F32).rearrange("p (c i u) -> p c u i", i=2, u=2), in_=halves[b][:].rearrange("p u (c i) -> p c u i", i=2))
 
         def quantize_z(b):
             nc.vector.quantize_mx(out=z_codes[b][:].rearrange("p a n -> p (a n)").bitcast(FP8X4),
@@ -241,19 +244,22 @@ def tile_picked_headrope_none_po_kernel(tc, x_words, x_scales, w1, w2, ct, st, w
             for n in range(2):
                 project(0, 0, k)
         rotate(1)
+        weave(1, nc.scalar.copy)
         turn_back(upper, lambda: held[0][:, 1], "pairs_high")
         nc.scalar.copy(out=z_bf[aside][:].bitcast(F32).rearrange("p (n u) -> p n u", u=2), in_=held[0][:].rearrange("p u a n -> p (a n) u"))
         nc.vector.tensor_copy(out=wo[:].rearrange("p a (t m) -> p a m t", t=PACK), in_=wo_raw[:].rearrange("p a (m t) -> p a m t", t=PACK))
         nc.vector.tensor_copy(out=wos[:].rearrange("p (t m) -> p m t", t=PACK), in_=wos_raw[:].rearrange("p (m t) -> p m t", t=PACK))
         quantize_z(1)
         rotate(2)
+        weave(2, nc.scalar.copy)
+        quantize_z(aside)
         rotate(last)
         quantize_z(2)
-        quantize_z(aside)
+        weave(last, nc.vector.tensor_copy)
         quantize_z(last)
         second_product(1, 6)
-        second_product(2, 1)
         second_product(aside, 2)
+        second_product(2, 1)
         accs = [bank(k, [P, 2, BLK]) for k in (3, 5)]
         for h in range(2):
             out_passes(accs[h], last, (2 * h, 2 * h + 1))

@@ -20,7 +20,6 @@ PACK = 4
 BLK = 128
 NBLK = S // BLK
 W1_SPLIT = 92
-ASIDE = 1
 
 
 def tile_picked_headrope_none_po_kernel(tc, x_words, x_scales, w1, w2, ct, st, w3_words, w3_scales, w4_words, w4_scales, offs, pos, out_0, out_1, out_2):
@@ -64,7 +63,7 @@ def tile_picked_headrope_none_po_kernel(tc, x_words, x_scales, w1, w2, ct, st, w
         st_v = st.rearrange("(p t) u -> p t u", t=PACK)
 
         tabs = (c_tab, s_tab)
-        tab_order = ((0, 0), (1, 0), (0, 2), (0, 1), (1, 2), (1, 1), (0, 3), (1, 3))
+        tab_order = [(k, t) for t in range(PACK) for k in range(2)]
 
         nc.sync.dma_start(offs_t[:], offs)
         nc.sync.dma_start(out=x_tab[:].bitcast(I32), in_=words_of(x_words))
@@ -115,81 +114,89 @@ def tile_picked_headrope_none_po_kernel(tc, x_words, x_scales, w1, w2, ct, st, w
             dst, src = deal_views(i, slice(W1_SPLIT, P))
             nc.scalar.copy(out=dst, in_=src)
             quantize_w(i)
-        y_bank = (0, 5, 2, 4)
-        e_bank = (1, 6, 3, 7)
-        y = {}
-        e = {}
-        for t in (0, 2, 1, 3):
+        aside = 0
+        last = NBLK - 1
+        y_bank = (0, 2, 5, 4)
+        e_bank = (1, 3, 6, 7)
+        y = [None] * PACK
+        e = [None] * PACK
+        both = {}
+        for t in range(PACK):
             y[t] = project(0, t, y_bank[t])
             e[t] = project(1, t, e_bank[t])
-        plain = {t: sb("plain%d" % t, [P, 3, S], F32) for t in (0, 2)}
-        for t in (0, 2):
-            nc.scalar.copy(out=plain[t][:, 1, :], in_=y[t][:])
-            nc.scalar.copy(out=plain[t][:, 2, :], in_=e[t][:])
-            nc.scalar.mul(plain[t][:, 0, :], e[t][:], -1.0)
-        plain3 = sb("plain3", [P, 3, S], F32)
-        nc.scalar.copy(out=plain3[:, 1, :], in_=y[3][:])
-        nc.scalar.copy(out=plain3[:, 2, :], in_=e[3][:])
-        plain[3] = plain3
+            if t == 0:
+                plain = sb("plain0", [P, 3, S], F32)
+                both[0, t], both[1, t] = plain[:, 1:3, :], plain[:, 0:2, :]
+                nc.scalar.copy(out=plain[:, 1, :], in_=y[t][:])
+                nc.scalar.copy(out=plain[:, 2, :], in_=e[t][:])
+                nc.scalar.mul(plain[:, 0, :], e[t][:], -1.0)
+            elif t == 1:
+                plain = sb("plain1", [P, 2, S], F32)
+                both[1, t] = plain[:]
+                nc.scalar.mul(plain[:, 0, :], e[t][:], -1.0)
+                nc.scalar.copy(out=plain[:, 1, :], in_=y[t][:])
+            else:
+                plain = sb("plain%d" % t, [P, 2, S], F32)
+                both[0, t] = plain[:]
+                nc.scalar.copy(out=plain[:, 0, :], in_=y[t][:])
+                nc.scalar.copy(out=plain[:, 1, :], in_=e[t][:])
 
         def blocks(ap):
             return ap.rearrange("p (b n) -> p b n", b=NBLK)
 
-        def from_psum(t, k, a, bs):
-            dst = prod[:, t, k, bs, a, :]
-            factor = blocks(trig[k][t][:])[:, bs]
-            if k == 1 and a == 0:
-                nc.vector.scalar_tensor_tensor(out=dst, in0=blocks(e[t][:])[:, bs], scalar=-1.0, in1=factor, op0=ALU.mult, op1=ALU.mult)
-            else:
-                nc.vector.tensor_tensor(out=dst, in0=blocks((y if k == a else e)[t][:])[:, bs], in1=factor, op=ALU.mult)
+        def on_vector(t, k, bs):
+            for a in range(2):
+                nc.vector.tensor_tensor(out=prod[:, t, k, bs, a, :], in0=blocks((y if k == a else e)[t][:])[:, bs], in1=blocks(trig[k][t][:])[:, bs], op=ALU.mult)
+
+        def on_gpsimd(t, k, bs):
+            nc.gpsimd.tensor_tensor(out=prod[:, t, k, bs].rearrange("p b a n -> p a b n"),
+                                    in0=both[k, t].rearrange("p a (b n) -> p a b n", b=NBLK)[:, :, bs],
+                                    in1=blocks(trig[k][t][:])[:, bs].unsqueeze(1).to_broadcast([P, 2, bs.stop - bs.start, BLK]), op=ALU.mult)
 
         for k, t in tab_order:
             nc.vector.tensor_copy(trig[k][t][:], tabs[k][t][:].indirect(pos_t[:]))
-            for bs in (slice(0, ASIDE), slice(ASIDE, NBLK)) if t == 3 else (slice(0, NBLK),):
-                if t in (0, 2) or (k, t) == (0, 3):
-                    nc.gpsimd.tensor_tensor(out=prod[:, t, k, bs].rearrange("p b a n -> p a b n"),
-                                            in0=plain[t][:, 1 - k : 3 - k, :].rearrange("p a (b n) -> p a b n", b=NBLK)[:, :, bs],
-                                            in1=blocks(trig[k][t][:])[:, bs].unsqueeze(1).to_broadcast([P, 2, bs.stop - bs.start, BLK]), op=ALU.mult)
-                else:
-                    for a in range(2):
-                        from_psum(t, k, a, bs)
+            engine = on_gpsimd if (k, t) in both else on_vector
+            if t == 3:
+                on_vector(t, k, slice(0, 1))
+                engine(t, k, slice(1, NBLK))
+            else:
+                engine(t, k, slice(0, NBLK))
 
-        aside = 0
-        last = NBLK - 1
         z_bf = [sb("z_bf%d" % b, [P, 2 * BLK * PACK], BF16) for b in range(NBLK)]
-        halves = {b: sb("halves%d" % b, [P, 2, 2 * BLK], F32) for b in range(1, NBLK)}
+        halves = {b: sb("halves%d" % b, [P, 2, 2, BLK], F32) for b in range(1, NBLK)}
 
-        def add_turned(dst, t, b):
-            for a in range(2):
-                for k in range(2):
-                    nc.tensor.matmul(dst[:, a, t % 2, :], lhsT=prod[:, t, k, b, a, :], rhs=ident[:], is_transpose=True, start=(k == 0), stop=(k == 1))
+        def add_turned(dst, first, second):
+            nc.tensor.matmul(dst, lhsT=first, rhs=ident[:], is_transpose=True, start=True, stop=False)
+            nc.tensor.matmul(dst, lhsT=second, rhs=ident[:], is_transpose=True, start=False, stop=True)
 
-        def turn_back(src, words, name):
+        def round_pairs(src, name):
             pairs = sb(name, [P, 2, 2 * P], BF16)
             nc.scalar.copy(out=pairs[:].rearrange("n a (p e) -> n a p e", e=2), in_=src[:].rearrange("n a e p -> n a p e"))
-            dst = words()
+            return pairs
+
+        def turn_back(dst, pairs):
             for a in range(2):
                 nc.tensor.transpose(dst[:, a, :], pairs[:, a, :].bitcast(F32), ident[:])
-            return dst
 
         order = (1, 2, last, aside)
-        turned = {b: bank(b, [P, 2, 2, P]) for b in order}
+        lower = {b: bank(b, [P, 2, 2, P]) for b in order}
         for t in range(2):
             for b in order:
-                add_turned(turned[b], t, b)
-        for b in order[:-1]:
-            words = turn_back(turned[b], lambda: bank(b, [P, 2, BLK]), "pairs%d" % b)
-            nc.scalar.copy(out=halves[b][:, 0, :], in_=words[:].rearrange("p a n -> p (a n)"))
-        held = []
-
-        def hold():
-            held.append(bank(aside, [P, 2, 2, BLK]))
-            return held[0][:, 0]
-
-        turn_back(turned[aside], hold, "pairs_low")
+                for a in range(2):
+                    add_turned(lower[b][:, a, t, :], prod[:, t, 0, b, a, :], prod[:, t, 1, b, a, :])
+        words = {}
+        for b in order:
+            pairs = round_pairs(lower[b], "lower%d" % b)
+            words[b] = bank(b, [P, 2, 2, BLK])
+            turn_back(words[b][:, 0], pairs)
+            if b != aside:
+                nc.scalar.copy(out=halves[b][:, 0], in_=words[b][:, 0])
         upper = bank(5, [P, 2, 2, P])
+        minus = sb("minus", [P, 2, BLK], F32)
         for t in (2, 3):
-            add_turned(upper, t, aside)
+            nc.scalar.mul(minus[:, t - 2, :], prod[:, t, 1, aside, 0, :], -1.0)
+            add_turned(upper[:, 1, t - 2, :], prod[:, t, 0, aside, 1, :], prod[:, t, 1, aside, 1, :])
+            add_turned(upper[:, 0, t - 2, :], prod[:, t, 0, aside, 0, :], minus[:, t - 2, :])
 
         z_codes = [sb("z_codes%d" % b, [P, 2, BLK], U32) for b in range(NBLK)]
         z_sc = [sb("z_sc%d" % b, [P, 2, BLK], U8) for b in range(NBLK)]
@@ -207,11 +214,13 @@ def tile_picked_headrope_none_po_kernel(tc, x_words, x_scales, w1, w2, ct, st, w
             return slice(b * BLK, (b + 1) * BLK)
 
         def rotate(b):
-            terms = [prod[:, 2:4, k, b].rearrange("p e a (c i) -> p (a c) e i", i=4) for k in range(2)]
-            nc.vector.tensor_tensor(out=halves[b][:, 1, :].bitcast(BF16).rearrange("p (c i e) -> p c e i", i=4, e=2), in0=terms[0], in1=terms[1], op=ALU.add)
+            for a in range(2):
+                terms = [prod[:, 2:4, k, b, a, :].rearrange("p e (c i) -> p c e i", i=4) for k in range(2)]
+                nc.vector.tensor_tensor(out=halves[b][:, 1, a, :].bitcast(BF16).rearrange("p (c i e) -> p c e i", i=4, e=2), in0=terms[0], in1=terms[1], op=(ALU.subtract, ALU.add)[a])
 
         def weave(b, copy):
-            copy(out=z_bf[b][:].bitcast(F32).rearrange("p (c i u) -> p c u i", i=2, u=2), in_=halves[b][:].rearrange("p u (c i) -> p c u i", i=2))
+            src = (words if b == aside else halves)[b][:].rearrange("p u a n -> p u (a n)")
+            copy(out=z_bf[b][:].bitcast(F32).rearrange("p (c i u) -> p c u i", i=2, u=2), in_=src.rearrange("p u (c i) -> p c u i", i=2))
 
         def quantize_z(b):
             nc.vector.quantize_mx(out=z_codes[b][:].rearrange("p a n -> p (a n)").bitcast(FP8X4),
@@ -240,13 +249,10 @@ def tile_picked_headrope_none_po_kernel(tc, x_words, x_scales, w1, w2, ct, st, w
             nc.vector.quantize_mx(out=o_codes[:, toks].bitcast(FP8X4), scales=o_sc[:, toks], in_=o_all[:, first * BLK * PACK : end * BLK * PACK])
             nc.sync.dma_start(out=out_words[:, toks], in_=o_codes[:, toks].bitcast(I32))
 
-        for k in (e_bank[3], y_bank[3]):
-            for n in range(2):
-                project(0, 0, k)
         rotate(1)
         weave(1, nc.scalar.copy)
-        turn_back(upper, lambda: held[0][:, 1], "pairs_high")
-        nc.scalar.copy(out=z_bf[aside][:].bitcast(F32).rearrange("p (n u) -> p n u", u=2), in_=held[0][:].rearrange("p u a n -> p (a n) u"))
+        turn_back(words[aside][:, 1], round_pairs(upper, "upper"))
+        weave(aside, nc.scalar.copy)
         nc.vector.tensor_copy(out=wo[:].rearrange("p a (t m) -> p a m t", t=PACK), in_=wo_raw[:].rearrange("p a (m t) -> p a m t", t=PACK))
         nc.vector.tensor_copy(out=wos[:].rearrange("p (t m) -> p m t", t=PACK), in_=wos_raw[:].rearrange("p (m t) -> p m t", t=PACK))
         quantize_z(1)

@@ -178,25 +178,30 @@ def tile_picked_headrope_none_po_kernel(tc, x_words, x_scales, w1, w2, ct, st, w
             for a in range(2):
                 nc.tensor.transpose(dst[:, a, :], pairs[:, a, :].bitcast(F32), ident[:])
 
-        order = (1, 2, last, aside)
-        lower = {b: bank(b, [P, 2, 2, P]) for b in order}
-        for t in range(2):
-            for b in order:
-                for a in range(2):
-                    add_turned(lower[b][:, a, t, :], prod[:, t, 0, b, a, :], prod[:, t, 1, b, a, :])
         words = {}
-        for b in order:
-            pairs = round_pairs(lower[b], "lower%d" % b)
+
+        def lower_half(b):
+            acc = bank(b, [P, 2, 2, P])
+            for n, (k, t) in enumerate(((0, 0), (0, 1), (1, 0), (1, 1))):
+                for a in range(2):
+                    nc.tensor.matmul(acc[:, a, t, :], lhsT=prod[:, t, k, b, a, :], rhs=ident[:], is_transpose=True,
+                                     start=(n == 0 and a == 0), stop=(n == 3 and a == 1))
+            pairs = round_pairs(acc, "lower%d" % b)
             words[b] = bank(b, [P, 2, 2, BLK])
             turn_back(words[b][:, 0], pairs)
             if b != aside:
                 nc.scalar.copy(out=halves[b][:, 0], in_=words[b][:, 0])
+
+        lower_half(1)
+        lower_half(aside)
         upper = bank(5, [P, 2, 2, P])
         minus = sb("minus", [P, 2, BLK], F32)
         for t in (2, 3):
             nc.scalar.mul(minus[:, t - 2, :], prod[:, t, 1, aside, 0, :], -1.0)
             add_turned(upper[:, 1, t - 2, :], prod[:, t, 0, aside, 1, :], prod[:, t, 1, aside, 1, :])
             add_turned(upper[:, 0, t - 2, :], prod[:, t, 0, aside, 0, :], minus[:, t - 2, :])
+        lower_half(2)
+        lower_half(last)
 
         z_codes = [sb("z_codes%d" % b, [P, 2, BLK], U32) for b in range(NBLK)]
         z_sc = [sb("z_sc%d" % b, [P, 2, BLK], U8) for b in range(NBLK)]

@@ -1,7 +1,6 @@
 from contextlib import ExitStack
 
 import concourse.mybir as mybir
-from concourse.masks import make_identity
 
 K, T, S, N, H, U = 512, 2048, 512, 512, 512, 1024
 FLOPS = 2 * S * (2 * K * H + 2 * H * N)
@@ -14,23 +13,23 @@ U16 = mybir.dt.uint16
 U8 = mybir.dt.uint8
 FP8X4 = mybir.dt.float8_e4m3fn_x4
 ALU = mybir.AluOpType
+COPY = mybir.ActivationFunctionType.Copy
 
 P = 128
 PACK = 4
 BLK = 128
 NBLK = S // BLK
-W1_SPLIT = 92
+VECTOR_GROUPS = 92
 
 
 def tile_picked_headrope_none_po_kernel(tc, x_words, x_scales, w1, w2, ct, st, w3_words, w3_scales, w4_words, w4_scales, offs, pos, out_0, out_1, out_2):
     nc = tc.nc
     with ExitStack() as ctx:
         keep = ctx.enter_context(tc.tile_pool(name="keep", bufs=1))
-        reused = ctx.enter_context(tc.tile_pool(name="reused", bufs=1))
         psum = ctx.enter_context(tc.psum_pool(name="psum", bufs=1))
 
-        def sb(name, shape, dtype, tag=""):
-            return keep.tile(shape, dtype, name=name, tag=tag or name, align_bytes=64)
+        def sb(name, shape, dtype):
+            return keep.tile(shape, dtype, name=name, align_bytes=64)
 
         def bank(k, shape):
             return psum.tile(shape, F32, name="bank%d" % k)
@@ -38,47 +37,37 @@ def tile_picked_headrope_none_po_kernel(tc, x_words, x_scales, w1, w2, ct, st, w
         def words_of(dram):
             return dram[0].rearrange("p n j -> p (n j)").bitcast(I32)
 
-        def load_scale_rows(queue, tile, first_row, dram):
-            for q in range(4):
-                rows = slice(32 * q + first_row, 32 * q + first_row + 4)
-                queue.dma_start(out=tile[rows, :].bitcast(I32), in_=dram[0][4 * q : 4 * q + 4, :].bitcast(I32))
+        def scale_rows(tile, first_row, dram):
+            return [(tile[32 * q + first_row : 32 * q + first_row + 4, :].bitcast(I32), dram[0][4 * q : 4 * q + 4, :].bitcast(I32)) for q in range(4)]
 
         offs_t = keep.tile([P, S // 16], U16, name="offs_t")
         pos_t = keep.tile([P, S // 16], U16, name="pos_t")
         x_tab = sb("x_tab", [P, T], U32)
         xs_tab = sb("xs_tab", [P, T], U8)
         w_raw = [sb("w_raw%d" % i, [P, PACK, H], F32) for i in range(2)]
-        c_tab = [sb("c_tab%d" % t, [P, U], F32) for t in range(PACK)]
-        s_tab = [sb("s_tab%d" % t, [P, U], F32) for t in range(PACK)]
-        wo_raw = sb("wo_raw", [P, 2, N], I32)
+        tabs = [[sb("tab%d_%d" % (k, t), [P, U], F32) for t in range(PACK)] for k in range(2)]
+        wo_raw = sb("wo_raw", [P, 2, N], U32)
         wos_raw = sb("wos_raw", [P, N], U8)
 
         nc.gpsimd.memset(xs_tab[:].bitcast(I32), 0)
         nc.vector.memset(wos_raw[:].bitcast(I32), 0)
 
-        ident = sb("ident", [P, P], F32)
-        make_identity(nc, ident[:])
-
-        ct_v = ct.rearrange("(p t) u -> p t u", t=PACK)
-        st_v = st.rearrange("(p t) u -> p t u", t=PACK)
-
-        tabs = (c_tab, s_tab)
+        tab_v = [dram.rearrange("(p t) u -> p t u", t=PACK) for dram in (ct, st)]
         tab_order = [(k, t) for t in range(PACK) for k in range(2)]
 
         nc.sync.dma_start(offs_t[:], offs)
         nc.sync.dma_start(out=x_tab[:].bitcast(I32), in_=words_of(x_words))
-        load_scale_rows(nc.sync, xs_tab, 0, x_scales)
+        for dst, src in scale_rows(xs_tab, 0, x_scales):
+            nc.sync.dma_start(out=dst, in_=src)
         nc.sync.dma_start(out=w_raw[0][:], in_=w1.rearrange("(p j) c -> p j c", j=PACK))
         nc.sync.dma_start(pos_t[:], pos)
         nc.sync.dma_start(out=w_raw[1][:], in_=w2.rearrange("(p j) c -> p j c", j=PACK))
-        wide = [(tabs[k][t][:], (ct_v, st_v)[k][:, t, :]) for k, t in tab_order]
-        wide[6:6] = [(wo_raw[:, 0, :], words_of(w3_words)), (wo_raw[:, 1, :], words_of(w4_words))]
-        narrow = [(wos_raw[32 * q + 4 * a : 32 * q + 4 * a + 4, :].bitcast(I32), dram[0][4 * q : 4 * q + 4, :].bitcast(I32))
-                  for a, dram in enumerate((w3_scales, w4_scales)) for q in range(4)]
-        for n, (dst, src) in enumerate(wide):
-            nc.sync.dma_start(out=dst, in_=src)
-            if n < len(narrow):
-                nc.sync.dma_start(out=narrow[n][0], in_=narrow[n][1])
+        narrow = scale_rows(wos_raw, 0, w3_scales) + scale_rows(wos_raw, 4, w4_scales)
+        for n, (k, t) in enumerate(tab_order):
+            nc.sync.dma_start(out=tabs[k][t][:], in_=tab_v[k][:, t, :])
+            nc.sync.dma_start(out=narrow[n][0], in_=narrow[n][1])
+        for a, dram in enumerate((w3_words, w4_words)):
+            nc.sync.dma_start(out=wo_raw[:, a, :].bitcast(I32), in_=words_of(dram))
 
         x_codes = sb("x_codes", [P, S], U32)
         x_sc = sb("x_sc", [P, S], U8)
@@ -94,196 +83,105 @@ def tile_picked_headrope_none_po_kernel(tc, x_words, x_scales, w1, w2, ct, st, w
             src = w_raw[i][:].rearrange("p j (m t) -> p m j t", t=PACK)
             return dst[:, ms], src[:, ms]
 
-        def quantize_w(i):
-            nc.vector.quantize_mx(out=w_codes[i][:].bitcast(FP8X4), scales=w_sc[i][:], in_=w_bf[i][:])
-
-        def project(i, t, k):
-            acc = bank(k, [P, S])
-            cols = slice(t * P, (t + 1) * P)
-            nc.tensor.matmul_mx(out=acc[:], lhsT=w_codes[i][:, cols].bitcast(FP8X4), lhsT_scale=w_sc[i][:, cols],
-                                rhs=x_codes[:].bitcast(FP8X4), rhs_scale=x_sc[:], start=True, stop=True)
-            return acc
-
-        trig = [[sb("trig%d_%d" % (k, t), [P, S], F32) if (k, t) != (1, 3) else None for t in range(PACK)] for k in range(2)]
-        trig[1][3] = reused.tile([P, S], F32, name="last_sines", offset=0, align_bytes=64)
-        prod = sb("prod", [P, PACK, 2, NBLK, 2, BLK], F32)
-
+        proj = [[None] * PACK for i in range(2)]
         for i in range(2):
-            dst, src = deal_views(i, slice(0, W1_SPLIT))
+            dst, src = deal_views(i, slice(0, VECTOR_GROUPS))
             nc.vector.tensor_copy(out=dst, in_=src)
-            dst, src = deal_views(i, slice(W1_SPLIT, P))
-            nc.scalar.copy(out=dst, in_=src)
-            quantize_w(i)
-        aside = 0
-        last = NBLK - 1
-        y_bank = (0, 2, 5, 4)
-        e_bank = (1, 3, 6, 7)
-        y = [None] * PACK
-        e = [None] * PACK
-        both = {}
-        for t in range(PACK):
-            y[t] = project(0, t, y_bank[t])
-            e[t] = project(1, t, e_bank[t])
-            if t == 0:
-                plain = sb("plain0", [P, 3, S], F32)
-                both[0, t], both[1, t] = plain[:, 1:3, :], plain[:, 0:2, :]
-                nc.scalar.copy(out=plain[:, 1, :], in_=y[t][:])
-                nc.scalar.copy(out=plain[:, 2, :], in_=e[t][:])
-                nc.scalar.mul(plain[:, 0, :], e[t][:], -1.0)
-            elif t == 1:
-                plain = sb("plain1", [P, 2, S], F32)
-                both[1, t] = plain[:]
-                nc.scalar.mul(plain[:, 0, :], e[t][:], -1.0)
-                nc.scalar.copy(out=plain[:, 1, :], in_=y[t][:])
-            else:
-                plain = sb("plain%d" % t, [P, 2, S], F32)
-                both[0, t] = plain[:]
-                nc.scalar.copy(out=plain[:, 0, :], in_=y[t][:])
-                nc.scalar.copy(out=plain[:, 1, :], in_=e[t][:])
+            dst, src = deal_views(i, slice(VECTOR_GROUPS, P))
+            nc.scalar.activation(out=dst, in_=src, func=COPY)
+            nc.vector.quantize_mx(out=w_codes[i][:].bitcast(FP8X4), scales=w_sc[i][:], in_=w_bf[i][:])
+            for t in range(PACK):
+                proj[i][t] = bank(2 * t + i, [P, S])
+                cols = slice(t * P, (t + 1) * P)
+                nc.tensor.matmul_mx(out=proj[i][t][:], lhsT=w_codes[i][:, cols].bitcast(FP8X4), lhsT_scale=w_sc[i][:, cols],
+                                    rhs=x_codes[:].bitcast(FP8X4), rhs_scale=x_sc[:], start=True, stop=True)
+
+        trig = [[sb("trig%d_%d" % (k, t), [P, S], F32) for t in range(PACK)] for k in range(2)]
+        prod = [[sb("prod%d_%d" % (u, k), [P, 2, NBLK, 2, BLK], F32) for k in range(2)] for u in range(2)]
+        halves = [sb("halves%d" % b, [P, 2, 2 * BLK], F32) for b in range(NBLK)]
 
         def blocks(ap):
             return ap.rearrange("p (b n) -> p b n", b=NBLK)
 
-        def on_vector(t, k, bs):
-            for a in range(2):
-                nc.vector.tensor_tensor(out=prod[:, t, k, bs, a, :], in0=blocks((y if k == a else e)[t][:])[:, bs], in1=blocks(trig[k][t][:])[:, bs], op=ALU.mult)
+        def products(k, t):
+            look = blocks(trig[k][t][:])
+            dst = prod[t // 2][k][:, t % 2]
+            y, e = blocks(proj[0][t][:]), blocks(proj[1][t][:])
+            if k == 0:
+                nc.vector.tensor_tensor(out=dst[:, :, 0, :], in0=y, in1=look, op=ALU.mult)
+                nc.vector.tensor_tensor(out=dst[:, :, 1, :], in0=e, in1=look, op=ALU.mult)
+            else:
+                nc.vector.scalar_tensor_tensor(out=dst[:, :, 0, :], in0=e, scalar=-1.0, in1=look, op0=ALU.mult, op1=ALU.mult)
+                nc.vector.tensor_tensor(out=dst[:, :, 1, :], in0=y, in1=look, op=ALU.mult)
 
-        def on_gpsimd(t, k, bs):
-            nc.gpsimd.tensor_tensor(out=prod[:, t, k, bs].rearrange("p b a n -> p a b n"),
-                                    in0=both[k, t].rearrange("p a (b n) -> p a b n", b=NBLK)[:, :, bs],
-                                    in1=blocks(trig[k][t][:])[:, bs].unsqueeze(1).to_broadcast([P, 2, bs.stop - bs.start, BLK]), op=ALU.mult)
+        def pair_sums(engine, u, b):
+            terms = [prod[u][k][:, :, b].rearrange("p e a (c i) -> p (a c) e i", i=4) for k in range(2)]
+            engine.tensor_tensor(out=halves[b][:, u, :].bitcast(BF16).rearrange("p (c i e) -> p c e i", i=4, e=2), in0=terms[0], in1=terms[1], op=ALU.add)
 
         for k, t in tab_order:
-            nc.vector.tensor_copy(trig[k][t][:], tabs[k][t][:].indirect(pos_t[:]))
-            engine = on_gpsimd if (k, t) in both else on_vector
-            if t == 3:
-                on_vector(t, k, slice(0, 1))
-                engine(t, k, slice(1, NBLK))
-            else:
-                engine(t, k, slice(0, NBLK))
+            nc.scalar.activation(out=trig[k][t][:], in_=tabs[k][t][:].indirect(pos_t[:]), func=COPY)
+            products(k, t)
+            if (k, t) == (1, 1):
+                for b in range(NBLK):
+                    pair_sums(nc.gpsimd, 0, b)
+
+        wo = sb("wo", [P, 2, N], U32)
+        wos = sb("wos", [P, N], U8)
+        nc.scalar.copy(out=wo[:].rearrange("p a (t m) -> p a m t", t=PACK), in_=wo_raw[:].rearrange("p a (m t) -> p a m t", t=PACK))
+        nc.vector.tensor_copy(out=wos[:].rearrange("p (t m) -> p m t", t=PACK), in_=wos_raw[:].rearrange("p (m t) -> p m t", t=PACK))
 
         z_bf = [sb("z_bf%d" % b, [P, 2 * BLK * PACK], BF16) for b in range(NBLK)]
-        halves = {b: sb("halves%d" % b, [P, 2, 2, BLK], F32) for b in range(1, NBLK)}
-
-        def add_turned(dst, first, second):
-            nc.tensor.matmul(dst, lhsT=first, rhs=ident[:], is_transpose=True, start=True, stop=False)
-            nc.tensor.matmul(dst, lhsT=second, rhs=ident[:], is_transpose=True, start=False, stop=True)
-
-        def round_pairs(src, name):
-            pairs = sb(name, [P, 2, 2 * P], BF16)
-            nc.scalar.copy(out=pairs[:].rearrange("n a (p e) -> n a p e", e=2), in_=src[:].rearrange("n a e p -> n a p e"))
-            return pairs
-
-        def turn_back(dst, pairs):
-            for a in range(2):
-                nc.tensor.transpose(dst[:, a, :], pairs[:, a, :].bitcast(F32), ident[:])
-
-        words = {}
-
-        def lower_half(b):
-            acc = bank(b, [P, 2, 2, P])
-            for n, (k, t) in enumerate(((0, 0), (0, 1), (1, 0), (1, 1))):
-                for a in range(2):
-                    nc.tensor.matmul(acc[:, a, t, :], lhsT=prod[:, t, k, b, a, :], rhs=ident[:], is_transpose=True,
-                                     start=(n == 0 and a == 0), stop=(n == 3 and a == 1))
-            pairs = round_pairs(acc, "lower%d" % b)
-            words[b] = bank(b, [P, 2, 2, BLK])
-            turn_back(words[b][:, 0], pairs)
-            if b != aside:
-                nc.scalar.copy(out=halves[b][:, 0], in_=words[b][:, 0])
-
-        lower_half(1)
-        lower_half(aside)
-        upper = bank(5, [P, 2, 2, P])
-        minus = sb("minus", [P, 2, BLK], F32)
-        for t in (2, 3):
-            nc.scalar.mul(minus[:, t - 2, :], prod[:, t, 1, aside, 0, :], -1.0)
-            add_turned(upper[:, 1, t - 2, :], prod[:, t, 0, aside, 1, :], prod[:, t, 1, aside, 1, :])
-            add_turned(upper[:, 0, t - 2, :], prod[:, t, 0, aside, 0, :], minus[:, t - 2, :])
-        lower_half(2)
-        lower_half(last)
-
         z_codes = [sb("z_codes%d" % b, [P, 2, BLK], U32) for b in range(NBLK)]
         z_sc = [sb("z_sc%d" % b, [P, 2, BLK], U8) for b in range(NBLK)]
-        o_all = sb("o_all", [P, S * PACK], BF16)
-        o_bf = [o_all[:, b * BLK * PACK : (b + 1) * BLK * PACK] for b in range(NBLK)]
+        o_bf = [sb("o_bf%d" % b, [P, BLK * PACK], BF16) for b in range(NBLK)]
         o_f32 = [sb("o_f32%d" % b, [P, PACK, BLK], F32) for b in range(NBLK)]
         o_codes = sb("o_codes", [P, S], U32)
         o_sc = sb("o_sc", [P, S], U8)
         out_v = out_0.rearrange("(p t) n -> p t n", t=PACK)
         out_words = words_of(out_1)
-        wo = reused.tile([P, 2, N], I32, name="wo", offset=N, align_bytes=64)
-        wos = reused.tile([P, N], U8, name="wos", offset=0, align_bytes=64)
 
         def toks_of(b):
             return slice(b * BLK, (b + 1) * BLK)
 
-        def rotate(b):
-            for a in range(2):
-                terms = [prod[:, 2:4, k, b, a, :].rearrange("p e (c i) -> p c e i", i=4) for k in range(2)]
-                nc.vector.tensor_tensor(out=halves[b][:, 1, a, :].bitcast(BF16).rearrange("p (c i e) -> p c e i", i=4, e=2), in0=terms[0], in1=terms[1], op=(ALU.subtract, ALU.add)[a])
-
-        def weave(b, copy):
-            src = (words if b == aside else halves)[b][:].rearrange("p u a n -> p u (a n)")
-            copy(out=z_bf[b][:].bitcast(F32).rearrange("p (c i u) -> p c u i", i=2, u=2), in_=src.rearrange("p u (c i) -> p c u i", i=2))
+        def weave(b):
+            nc.scalar.copy(out=z_bf[b][:].bitcast(F32).rearrange("p (c i u) -> p c u i", i=2, u=2), in_=halves[b][:].rearrange("p u (c i) -> p c u i", i=2))
 
         def quantize_z(b):
             nc.vector.quantize_mx(out=z_codes[b][:].rearrange("p a n -> p (a n)").bitcast(FP8X4),
                                   scales=z_sc[b][:].rearrange("p a n -> p (a n)"), in_=z_bf[b][:])
 
-        def out_passes(acc, b, ts):
-            for n, t in enumerate(ts):
+        def second_product(b):
+            acc = bank(b, [P, PACK, BLK])
+            for t in range(PACK):
                 cols = slice(t * P, (t + 1) * P)
                 for a in range(2):
-                    nc.tensor.matmul_mx(out=acc[:, n, :], lhsT=wo[:, a, cols].bitcast(FP8X4), lhsT_scale=wos[4 * a :, cols],
+                    nc.tensor.matmul_mx(out=acc[:, t, :], lhsT=wo[:, a, cols].bitcast(FP8X4), lhsT_scale=wos[4 * a :, cols],
                                         rhs=z_codes[b][:, a, :].bitcast(FP8X4), rhs_scale=z_sc[b][:, a, :],
                                         start=(a == 0), stop=(a == 1))
-
-        def second_product(b, k):
-            acc = bank(k, [P, PACK, BLK])
-            out_passes(acc, b, range(PACK))
             nc.scalar.copy(out=o_f32[b][:], in_=acc[:])
             nc.sync.dma_start(out=out_v[:, :, toks_of(b)], in_=o_f32[b][:])
 
         def round_out(b):
-            nc.vector.tensor_copy(out=o_bf[b].rearrange("p (c i t) -> p c t i", i=4, t=PACK),
+            nc.vector.tensor_copy(out=o_bf[b][:].rearrange("p (c i t) -> p c t i", i=4, t=PACK),
                                   in_=o_f32[b][:].rearrange("p t (c i) -> p c t i", i=4))
 
-        def hand_on(first, end):
-            toks = slice(first * BLK, end * BLK)
-            nc.vector.quantize_mx(out=o_codes[:, toks].bitcast(FP8X4), scales=o_sc[:, toks], in_=o_all[:, first * BLK * PACK : end * BLK * PACK])
+        def hand_on(b):
+            toks = toks_of(b)
+            nc.vector.quantize_mx(out=o_codes[:, toks].bitcast(FP8X4), scales=o_sc[:, toks], in_=o_bf[b][:])
             nc.sync.dma_start(out=out_words[:, toks], in_=o_codes[:, toks].bitcast(I32))
 
-        rotate(1)
-        weave(1, nc.scalar.copy)
-        turn_back(words[aside][:, 1], round_pairs(upper, "upper"))
-        weave(aside, nc.scalar.copy)
-        nc.vector.tensor_copy(out=wo[:].rearrange("p a (t m) -> p a m t", t=PACK), in_=wo_raw[:].rearrange("p a (m t) -> p a m t", t=PACK))
-        nc.vector.tensor_copy(out=wos[:].rearrange("p (t m) -> p m t", t=PACK), in_=wos_raw[:].rearrange("p (m t) -> p m t", t=PACK))
-        quantize_z(1)
-        rotate(2)
-        weave(2, nc.scalar.copy)
-        quantize_z(aside)
-        rotate(last)
-        quantize_z(2)
-        weave(last, nc.vector.tensor_copy)
-        quantize_z(last)
-        second_product(1, 6)
-        second_product(aside, 2)
-        second_product(2, 1)
-        accs = [bank(k, [P, 2, BLK]) for k in (3, 5)]
-        for h in range(2):
-            out_passes(accs[h], last, (2 * h, 2 * h + 1))
-        nc.scalar.copy(out=o_f32[last][:, 0:2, :], in_=accs[0][:])
-        round_out(1)
-        round_out(aside)
-        round_out(2)
-        hand_on(0, 2)
-        nc.vector.tensor_copy(out=o_f32[last][:, 2:4, :], in_=accs[1][:])
-        nc.sync.dma_start(out=out_v[:, :, toks_of(last)], in_=o_f32[last][:])
-        hand_on(2, 3)
-        round_out(last)
-        hand_on(last, last + 1)
+        for step in range(NBLK + 1):
+            if step < NBLK:
+                pair_sums(nc.vector, 1, step)
+                weave(step)
+            if step >= 1:
+                quantize_z(step - 1)
+                second_product(step - 1)
+        for step in range(NBLK + 1):
+            if step < NBLK:
+                round_out(step)
+            if step >= 1:
+                hand_on(step - 1)
         for q in range(4):
             queue = nc.scalar if q % 2 else nc.sync
             queue.dma_start(out=out_2[0][4 * q : 4 * q + 4, :].bitcast(I32), in_=o_sc[32 * q : 32 * q + 4, :].bitcast(I32))

@@ -103,31 +103,63 @@ def tile_picked_headrope_none_po_kernel(tc, x_words, x_scales, w1, w2, ct, st, w
         def blocks(ap):
             return ap.rearrange("p (b n) -> p b n", b=NBLK)
 
-        def products(k, t):
-            look = blocks(trig[k][t][:])
-            dst = prod[t // 2][k][:, t % 2]
-            y, e = blocks(proj[0][t][:]), blocks(proj[1][t][:])
+        def products(k, t, bs):
+            look = blocks(trig[k][t][:])[:, bs]
+            dst = prod[t // 2][k][:, t % 2, bs]
+            y, e = blocks(proj[0][t][:])[:, bs], blocks(proj[1][t][:])[:, bs]
             if k == 0:
-                nc.vector.tensor_tensor(out=dst[:, :, 0, :], in0=y, in1=look, op=ALU.mult)
                 nc.vector.tensor_tensor(out=dst[:, :, 1, :], in0=e, in1=look, op=ALU.mult)
             else:
                 nc.vector.scalar_tensor_tensor(out=dst[:, :, 0, :], in0=e, scalar=-1.0, in1=look, op0=ALU.mult, op1=ALU.mult)
-                nc.vector.tensor_tensor(out=dst[:, :, 1, :], in0=y, in1=look, op=ALU.mult)
+            if (k, t) in on_gpsimd:
+                nc.gpsimd.tensor_tensor(out=dst[:, :, k, :], in0=blocks(y_sb[t][:])[:, bs], in1=look, op=ALU.mult)
+            else:
+                nc.vector.tensor_tensor(out=dst[:, :, k, :], in0=y, in1=look, op=ALU.mult)
 
         def pair_sums(engine, u, b):
             terms = [prod[u][k][:, :, b].rearrange("p e a (c i) -> p (a c) e i", i=4) for k in range(2)]
             engine.tensor_tensor(out=halves[b][:, u, :].bitcast(BF16).rearrange("p (c i e) -> p c e i", i=4, e=2), in0=terms[0], in1=terms[1], op=ALU.add)
 
-        for k, t in tab_order:
-            nc.scalar.activation(out=trig[k][t][:], in_=tabs[k][t][:].indirect(pos_t[:]), func=COPY)
-            products(k, t)
-            if (k, t) == (1, 1):
+        def slot_sums(t, b):
+            terms = [prod[0][k][:, t, b].rearrange("p a n -> p (a n)") for k in range(2)]
+            nc.gpsimd.tensor_tensor(out=halves[b][:, 0, :].bitcast(BF16).rearrange("p (n e) -> p e n", e=2)[:, t], in0=terms[0], in1=terms[1], op=ALU.add)
+
+        on_gpsimd = ((0, 0), (1, 0))
+        y_sb = [sb("y_sb0", [P, S], F32)]
+
+        early, late = slice(0, NBLK // 2), slice(NBLK // 2, NBLK)
+
+        def window(k, t, bs):
+            return tabs[k][t][:].indirect(pos_t[:, bs.start * BLK // 16 : bs.stop * BLK // 16])
+
+        def look_up_scalar(k, t, bs):
+            nc.scalar.activation(out=trig[k][t][:, bs.start * BLK : bs.stop * BLK], in_=window(k, t, bs), func=COPY)
+
+        def look_up_vector(k, t, bs):
+            nc.vector.tensor_copy(trig[k][t][:, bs.start * BLK : bs.stop * BLK], window(k, t, bs))
+
+        whole = slice(0, NBLK)
+        nc.scalar.copy(out=y_sb[0][:], in_=proj[0][0][:])
+        for k, t in tab_order[:-1]:
+            if (k, t) == (1, 0):
+                look_up_vector(k, t, late)
+                look_up_scalar(k, t, early)
+            else:
+                look_up_scalar(k, t, whole)
+            products(k, t, whole)
+            if k == 1 and t < 2:
                 for b in range(NBLK):
-                    pair_sums(nc.gpsimd, 0, b)
+                    slot_sums(t, b)
+        look_up_scalar(1, 3, early)
+        look_up_scalar(1, 3, late)
+        products(1, 3, early)
+        products(1, 3, late)
 
         wo = sb("wo", [P, 2, N], U32)
+        for a in range(2):
+            nc.scalar.copy(out=wo[:, a].rearrange("p (t m) -> p m t", t=PACK), in_=wo_raw[:, a].rearrange("p (m t) -> p m t", t=PACK))
+
         wos = sb("wos", [P, N], U8)
-        nc.scalar.copy(out=wo[:].rearrange("p a (t m) -> p a m t", t=PACK), in_=wo_raw[:].rearrange("p a (m t) -> p a m t", t=PACK))
         nc.vector.tensor_copy(out=wos[:].rearrange("p (t m) -> p m t", t=PACK), in_=wos_raw[:].rearrange("p (m t) -> p m t", t=PACK))
 
         z_bf = [sb("z_bf%d" % b, [P, 2 * BLK * PACK], BF16) for b in range(NBLK)]
@@ -140,25 +172,38 @@ def tile_picked_headrope_none_po_kernel(tc, x_words, x_scales, w1, w2, ct, st, w
         out_v = out_0.rearrange("(p t) n -> p t n", t=PACK)
         out_words = words_of(out_1)
 
+        last = NBLK - 1
+
         def toks_of(b):
             return slice(b * BLK, (b + 1) * BLK)
 
-        def weave(b):
-            nc.scalar.copy(out=z_bf[b][:].bitcast(F32).rearrange("p (c i u) -> p c u i", i=2, u=2), in_=halves[b][:].rearrange("p u (c i) -> p c u i", i=2))
+        def weave(b, cols):
+            nc.scalar.copy(out=z_bf[b][:].bitcast(F32).rearrange("p (c i u) -> p c u i", i=2, u=2)[:, cols], in_=halves[b][:].rearrange("p u (c i) -> p c u i", i=2)[:, cols])
 
-        def quantize_z(b):
-            nc.vector.quantize_mx(out=z_codes[b][:].rearrange("p a n -> p (a n)").bitcast(FP8X4),
-                                  scales=z_sc[b][:].rearrange("p a n -> p (a n)"), in_=z_bf[b][:])
+        def quantize_z(b, a):
+            nc.vector.quantize_mx(out=z_codes[b][:, a].rearrange("p a n -> p (a n)").bitcast(FP8X4),
+                                  scales=z_sc[b][:, a].rearrange("p a n -> p (a n)"),
+                                  in_=z_bf[b][:].rearrange("p (a m) -> p a m", a=2)[:, a].rearrange("p a m -> p (a m)"))
+
+        def one_pass(out, b, t, a, start, stop):
+            cols = slice(t * P, (t + 1) * P)
+            nc.tensor.matmul_mx(out=out, lhsT=wo[:, a, cols].bitcast(FP8X4), lhsT_scale=wos[4 * a :, cols],
+                                rhs=z_codes[b][:, a, :].bitcast(FP8X4), rhs_scale=z_sc[b][:, a, :], start=start, stop=stop)
 
         def second_product(b):
-            acc = bank(b, [P, PACK, BLK])
-            for t in range(PACK):
-                cols = slice(t * P, (t + 1) * P)
+            if b < last:
+                acc = bank(b, [P, PACK, BLK])
+                for t in range(PACK):
+                    for a in range(2):
+                        one_pass(acc[:, t, :], b, t, a, a == 0, a == 1)
+                nc.scalar.copy(out=o_f32[b][:], in_=acc[:])
+            else:
+                accs = [bank(b + h, [P, 2, BLK]) for h in range(2)]
                 for a in range(2):
-                    nc.tensor.matmul_mx(out=acc[:, t, :], lhsT=wo[:, a, cols].bitcast(FP8X4), lhsT_scale=wos[4 * a :, cols],
-                                        rhs=z_codes[b][:, a, :].bitcast(FP8X4), rhs_scale=z_sc[b][:, a, :],
-                                        start=(a == 0), stop=(a == 1))
-            nc.scalar.copy(out=o_f32[b][:], in_=acc[:])
+                    for t in range(PACK):
+                        one_pass(accs[t // 2][:, t % 2, :], b, t, a, a == 0 and t % 2 == 0, a == 1 and t % 2 == 1)
+                for h, copy in enumerate((nc.scalar.copy, nc.vector.tensor_copy)):
+                    copy(out=o_f32[b][:, 2 * h : 2 * h + 2], in_=accs[h][:])
             nc.sync.dma_start(out=out_v[:, :, toks_of(b)], in_=o_f32[b][:])
 
         def round_out(b):
@@ -168,20 +213,30 @@ def tile_picked_headrope_none_po_kernel(tc, x_words, x_scales, w1, w2, ct, st, w
         def hand_on(b):
             toks = toks_of(b)
             nc.vector.quantize_mx(out=o_codes[:, toks].bitcast(FP8X4), scales=o_sc[:, toks], in_=o_bf[b][:])
-            nc.sync.dma_start(out=out_words[:, toks], in_=o_codes[:, toks].bitcast(I32))
+            if b % 2:
+                both = slice((b - 1) * BLK, (b + 1) * BLK)
+                nc.sync.dma_start(out=out_words[:, both], in_=o_codes[:, both].bitcast(I32))
 
-        for step in range(NBLK + 1):
-            if step < NBLK:
-                pair_sums(nc.vector, 1, step)
-                weave(step)
-            if step >= 1:
-                quantize_z(step - 1)
-                second_product(step - 1)
-        for step in range(NBLK + 1):
-            if step < NBLK:
-                round_out(step)
-            if step >= 1:
-                hand_on(step - 1)
+        for b in range(NBLK):
+            pair_sums(nc.vector, 1, b)
+            if b < last:
+                weave(b, slice(0, BLK))
+            else:
+                weave(b, slice(0, BLK // 2))
+                weave(b, slice(BLK // 2, BLK))
+            if b >= 1:
+                quantize_z(b - 1, slice(0, 2))
+        quantize_z(last, slice(0, 1))
+        quantize_z(last, slice(1, 2))
+        for b in range(last):
+            second_product(b)
+        for b in range(last):
+            round_out(b)
+        for b in range(last):
+            hand_on(b)
+        second_product(last)
+        round_out(last)
+        hand_on(last)
         for q in range(4):
             queue = nc.scalar if q % 2 else nc.sync
             queue.dma_start(out=out_2[0][4 * q : 4 * q + 4, :].bitcast(I32), in_=o_sc[32 * q : 32 * q + 4, :].bitcast(I32))

@@ -55,17 +55,24 @@ def tile_picked_headrope_none_po_kernel(tc, x_words, x_scales, w1, w2, ct, st, w
         tab_v = [dram.rearrange("(p t) u -> p t u", t=PACK) for dram in (ct, st)]
         tab_order = [(k, t) for t in range(PACK) for k in range(2)]
 
-        nc.sync.dma_start(offs_t[:], offs)
         nc.sync.dma_start(out=x_tab[:].bitcast(I32), in_=words_of(x_words))
+        nc.sync.dma_start(offs_t[:], offs)
         for dst, src in scale_rows(xs_tab, 0, x_scales):
             nc.sync.dma_start(out=dst, in_=src)
+        narrow = scale_rows(wos_raw, 0, w3_scales) + scale_rows(wos_raw, 4, w4_scales)
+
+        def load_narrow(first, end):
+            for dst, src in narrow[first:end]:
+                nc.sync.dma_start(out=dst, in_=src)
+
         nc.sync.dma_start(out=w_raw[0][:], in_=w1.rearrange("(p j) c -> p j c", j=PACK))
         nc.sync.dma_start(pos_t[:], pos)
         nc.sync.dma_start(out=w_raw[1][:], in_=w2.rearrange("(p j) c -> p j c", j=PACK))
-        narrow = scale_rows(wos_raw, 0, w3_scales) + scale_rows(wos_raw, 4, w4_scales)
+        load_narrow(0, 4)
         for n, (k, t) in enumerate(tab_order):
             nc.sync.dma_start(out=tabs[k][t][:], in_=tab_v[k][:, t, :])
-            nc.sync.dma_start(out=narrow[n][0], in_=narrow[n][1])
+            if n == 2:
+                load_narrow(4, 8)
         for a, dram in enumerate((w3_words, w4_words)):
             nc.sync.dma_start(out=wo_raw[:, a, :].bitcast(I32), in_=words_of(dram))
 
@@ -98,7 +105,8 @@ def tile_picked_headrope_none_po_kernel(tc, x_words, x_scales, w1, w2, ct, st, w
 
         trig = [[sb("trig%d_%d" % (k, t), [P, S], F32) for t in range(PACK)] for k in range(2)]
         prod = [[sb("prod%d_%d" % (u, k), [P, 2, NBLK, 2, BLK], F32) for k in range(2)] for u in range(2)]
-        halves = [sb("halves%d" % b, [P, 2, 2 * BLK], F32) for b in range(NBLK)]
+        halves2 = [sb("halves%d" % h, [P, 2, 2, 2 * BLK], F32) for h in range(2)]
+        halves = [halves2[b // 2][:, :, b % 2] for b in range(NBLK)]
 
         def blocks(ap):
             return ap.rearrange("p (b n) -> p b n", b=NBLK)
@@ -116,13 +124,15 @@ def tile_picked_headrope_none_po_kernel(tc, x_words, x_scales, w1, w2, ct, st, w
             else:
                 nc.vector.tensor_tensor(out=dst[:, :, k, :], in0=y, in1=look, op=ALU.mult)
 
-        def pair_sums(engine, u, b):
-            terms = [prod[u][k][:, :, b].rearrange("p e a (c i) -> p (a c) e i", i=4) for k in range(2)]
-            engine.tensor_tensor(out=halves[b][:, u, :].bitcast(BF16).rearrange("p (c i e) -> p c e i", i=4, e=2), in0=terms[0], in1=terms[1], op=ALU.add)
+        def pair_sums(b, a):
+            terms = [prod[1][k][:, :, b, a].rearrange("p e a (c i) -> p (a c) e i", i=4) for k in range(2)]
+            upper = halves[b][:, 1, a.start * BLK : a.stop * BLK]
+            nc.vector.tensor_tensor(out=upper.bitcast(BF16).rearrange("p (c i e) -> p c e i", i=4, e=2), in0=terms[0], in1=terms[1], op=ALU.add)
 
-        def slot_sums(t, b):
-            terms = [prod[0][k][:, t, b].rearrange("p a n -> p (a n)") for k in range(2)]
-            nc.gpsimd.tensor_tensor(out=halves[b][:, 0, :].bitcast(BF16).rearrange("p (n e) -> p e n", e=2)[:, t], in0=terms[0], in1=terms[1], op=ALU.add)
+        def slot_sums(t, h):
+            terms = [prod[0][k][:, t, 2 * h : 2 * h + 2].rearrange("p b a n -> p (b a n)") for k in range(2)]
+            lower = halves2[h][:, 0].rearrange("p b n -> p (b n)")
+            nc.gpsimd.tensor_tensor(out=lower.bitcast(BF16).rearrange("p (n e) -> p e n", e=2)[:, t], in0=terms[0], in1=terms[1], op=ALU.add)
 
         on_gpsimd = ((0, 0), (1, 0))
         y_sb = [sb("y_sb0", [P, S], F32)]
@@ -147,20 +157,20 @@ def tile_picked_headrope_none_po_kernel(tc, x_words, x_scales, w1, w2, ct, st, w
             else:
                 look_up_scalar(k, t, whole)
             products(k, t, whole)
+            if (k, t) == (1, 0):
+                wos = keep.tile([P, N], U8, name="wos", tag="trig0_0", align_bytes=64)
+                nc.vector.tensor_copy(out=wos[:].rearrange("p (t m) -> p m t", t=PACK), in_=wos_raw[:].rearrange("p (m t) -> p m t", t=PACK))
             if k == 1 and t < 2:
-                for b in range(NBLK):
-                    slot_sums(t, b)
+                for h in range(2):
+                    slot_sums(t, h)
         look_up_scalar(1, 3, early)
         look_up_scalar(1, 3, late)
         products(1, 3, early)
-        products(1, 3, late)
 
         wo = sb("wo", [P, 2, N], U32)
         for a in range(2):
             nc.scalar.copy(out=wo[:, a].rearrange("p (t m) -> p m t", t=PACK), in_=wo_raw[:, a].rearrange("p (m t) -> p m t", t=PACK))
 
-        wos = sb("wos", [P, N], U8)
-        nc.vector.tensor_copy(out=wos[:].rearrange("p (t m) -> p m t", t=PACK), in_=wos_raw[:].rearrange("p (m t) -> p m t", t=PACK))
 
         z_bf = [sb("z_bf%d" % b, [P, 2 * BLK * PACK], BF16) for b in range(NBLK)]
         z_codes = [sb("z_codes%d" % b, [P, 2, BLK], U32) for b in range(NBLK)]
@@ -178,7 +188,7 @@ def tile_picked_headrope_none_po_kernel(tc, x_words, x_scales, w1, w2, ct, st, w
             return slice(b * BLK, (b + 1) * BLK)
 
         def weave(b, cols):
-            nc.scalar.copy(out=z_bf[b][:].bitcast(F32).rearrange("p (c i u) -> p c u i", i=2, u=2)[:, cols], in_=halves[b][:].rearrange("p u (c i) -> p c u i", i=2)[:, cols])
+            nc.scalar.copy(out=z_bf[b][:].bitcast(F32).rearrange("p (c i u) -> p c u i", i=2, u=2)[:, cols], in_=halves[b].rearrange("p u (c i) -> p c u i", i=2)[:, cols])
 
         def quantize_z(b, a):
             nc.vector.quantize_mx(out=z_codes[b][:, a].rearrange("p a n -> p (a n)").bitcast(FP8X4),
@@ -218,13 +228,18 @@ def tile_picked_headrope_none_po_kernel(tc, x_words, x_scales, w1, w2, ct, st, w
                 nc.sync.dma_start(out=out_words[:, both], in_=o_codes[:, both].bitcast(I32))
 
         for b in range(NBLK):
-            pair_sums(nc.vector, 1, b)
             if b < last:
+                pair_sums(b, slice(0, 2))
                 weave(b, slice(0, BLK))
             else:
+                pair_sums(b, slice(0, 1))
                 weave(b, slice(0, BLK // 2))
+                pair_sums(b, slice(1, 2))
                 weave(b, slice(BLK // 2, BLK))
-            if b >= 1:
+            if b == 0:
+                products(1, 3, late)
+                quantize_z(0, slice(0, 2))
+            if b >= 2:
                 quantize_z(b - 1, slice(0, 2))
         quantize_z(last, slice(0, 1))
         quantize_z(last, slice(1, 2))

@@ -20,6 +20,7 @@ PACK = 4
 BLK = 128
 NBLK = S // BLK
 VECTOR_GROUPS = 92
+WARM_UPS = 6
 
 
 def tile_picked_headrope_none_po_kernel(tc, x_words, x_scales, w1, w2, ct, st, w3_words, w3_scales, w4_words, w4_scales, offs, pos, out_0, out_1, out_2):
@@ -238,6 +239,10 @@ def tile_picked_headrope_none_po_kernel(tc, x_words, x_scales, w1, w2, ct, st, w
                 weave(b, slice(BLK // 2, BLK))
             if b == 0:
                 products(1, 3, late)
+                idle = bank(2 * PACK - 2, [P, PACK, BLK])
+                for n in range(WARM_UPS):
+                    nc.tensor.matmul_mx(out=idle[:, n % PACK, :], lhsT=w_codes[0][:, :P].bitcast(FP8X4), lhsT_scale=w_sc[0][:, :P],
+                                        rhs=w_codes[1][:, :BLK].bitcast(FP8X4), rhs_scale=w_sc[1][:, :BLK], start=True, stop=True)
                 quantize_z(0, slice(0, 2))
             if b >= 2:
                 quantize_z(b - 1, slice(0, 2))

@@ -202,20 +202,25 @@ def tile_picked_headrope_none_po_kernel(tc, x_words, x_scales, w1, w2, ct, st, w
                                 rhs=z_codes[b][:, a, :].bitcast(FP8X4), rhs_scale=z_sc[b][:, a, :], start=start, stop=stop)
 
         def second_product(b):
-            if b < last:
-                acc = bank(b, [P, PACK, BLK])
+            if 0 < b < last:
+                acc = bank(b + 1, [P, PACK, BLK])
                 for t in range(PACK):
                     for a in range(2):
                         one_pass(acc[:, t, :], b, t, a, a == 0, a == 1)
                 nc.scalar.copy(out=o_f32[b][:], in_=acc[:])
-            else:
-                accs = [bank(b + h, [P, 2, BLK]) for h in range(2)]
-                for a in range(2):
-                    for t in range(PACK):
-                        one_pass(accs[t // 2][:, t % 2, :], b, t, a, a == 0 and t % 2 == 0, a == 1 and t % 2 == 1)
-                for h, copy in enumerate((nc.scalar.copy, nc.vector.tensor_copy)):
-                    copy(out=o_f32[b][:, 2 * h : 2 * h + 2], in_=accs[h][:])
-            nc.sync.dma_start(out=out_v[:, :, toks_of(b)], in_=o_f32[b][:])
+                nc.sync.dma_start(out=out_v[:, :, toks_of(b)], in_=o_f32[b][:])
+                return
+            accs = [bank((b + 1 if b else 0) + h, [P, 2, BLK]) for h in range(2)]
+            for a in range(2):
+                for t in range(PACK):
+                    one_pass(accs[t // 2][:, t % 2, :], b, t, a, a == 0 and t % 2 == 0, a == 1 and t % 2 == 1)
+            for h, copy in enumerate((nc.scalar.copy, nc.vector.tensor_copy if b else nc.scalar.copy)):
+                ts = slice(2 * h, 2 * h + 2)
+                copy(out=o_f32[b][:, ts], in_=accs[h][:])
+                if b == 0:
+                    nc.sync.dma_start(out=out_v[:, ts, toks_of(b)], in_=o_f32[b][:, ts])
+            if b:
+                nc.sync.dma_start(out=out_v[:, :, toks_of(b)], in_=o_f32[b][:])
 
         def round_out(b):
             nc.vector.tensor_copy(out=o_bf[b][:].rearrange("p (c i t) -> p c t i", i=4, t=PACK),
@@ -229,7 +234,7 @@ def tile_picked_headrope_none_po_kernel(tc, x_words, x_scales, w1, w2, ct, st, w
                 nc.sync.dma_start(out=out_words[:, both], in_=o_codes[:, both].bitcast(I32))
 
         for b in range(NBLK):
-            if b < last:
+            if 0 < b < last:
                 pair_sums(b, slice(0, 2))
                 weave(b, slice(0, BLK))
             else:
@@ -243,7 +248,8 @@ def tile_picked_headrope_none_po_kernel(tc, x_words, x_scales, w1, w2, ct, st, w
                 for n in range(WARM_UPS):
                     nc.tensor.matmul_mx(out=idle[:, n % PACK, :], lhsT=w_codes[0][:, :P].bitcast(FP8X4), lhsT_scale=w_sc[0][:, :P],
                                         rhs=w_codes[1][:, :BLK].bitcast(FP8X4), rhs_scale=w_sc[1][:, :BLK], start=True, stop=True)
-                quantize_z(0, slice(0, 2))
+                quantize_z(0, slice(0, 1))
+                quantize_z(0, slice(1, 2))
             if b >= 2:
                 quantize_z(b - 1, slice(0, 2))
         quantize_z(last, slice(0, 1))

@@ -105,16 +105,17 @@ def tile_picked_headrope_none_po_kernel(tc, x_words, x_scales, w1, w2, ct, st, w
                                     rhs=x_codes[:].bitcast(FP8X4), rhs_scale=x_sc[:], start=True, stop=True)
 
         trig = [[sb("trig%d_%d" % (k, t), [P, S], F32) for t in range(PACK)] for k in range(2)]
-        prod = [[sb("prod%d_%d" % (u, k), [P, 2, NBLK, 2, BLK], F32) for k in range(2)] for u in range(2)]
-        halves2 = [sb("halves%d" % h, [P, 2, 2, 2 * BLK], F32) for h in range(2)]
-        halves = [halves2[b // 2][:, :, b % 2] for b in range(NBLK)]
+        prod = [sb("prod%d" % k, [P, PACK, NBLK, 2, BLK], F32) for k in range(2)]
+        groups = (slice(0, 2), slice(2, 3))
+        halves2 = [sb("halves%d" % h, [P, 2, bs.stop - bs.start, 2 * BLK], F32) for h, bs in enumerate(groups)]
+        halves = [halves2[b // 2][:, :, b % 2] for b in range(NBLK - 1)]
 
         def blocks(ap):
             return ap.rearrange("p (b n) -> p b n", b=NBLK)
 
         def products(k, t, bs):
             look = blocks(trig[k][t][:])[:, bs]
-            dst = prod[t // 2][k][:, t % 2, bs]
+            dst = prod[k][:, t, bs]
             y, e = blocks(proj[0][t][:])[:, bs], blocks(proj[1][t][:])[:, bs]
             if k == 0:
                 nc.vector.tensor_tensor(out=dst[:, :, 1, :], in0=e, in1=look, op=ALU.mult)
@@ -126,12 +127,12 @@ def tile_picked_headrope_none_po_kernel(tc, x_words, x_scales, w1, w2, ct, st, w
                 nc.vector.tensor_tensor(out=dst[:, :, k, :], in0=y, in1=look, op=ALU.mult)
 
         def pair_sums(b, a):
-            terms = [prod[1][k][:, :, b, a].rearrange("p e a (c i) -> p (a c) e i", i=4) for k in range(2)]
+            terms = [prod[k][:, 2:4, b, a].rearrange("p e a (c i) -> p (a c) e i", i=4) for k in range(2)]
             upper = halves[b][:, 1, a.start * BLK : a.stop * BLK]
             nc.vector.tensor_tensor(out=upper.bitcast(BF16).rearrange("p (c i e) -> p c e i", i=4, e=2), in0=terms[0], in1=terms[1], op=ALU.add)
 
         def slot_sums(t, h):
-            terms = [prod[0][k][:, t, 2 * h : 2 * h + 2].rearrange("p b a n -> p (b a n)") for k in range(2)]
+            terms = [prod[k][:, t, groups[h]].rearrange("p b a n -> p (b a n)") for k in range(2)]
             lower = halves2[h][:, 0].rearrange("p b n -> p (b n)")
             nc.gpsimd.tensor_tensor(out=lower.bitcast(BF16).rearrange("p (n e) -> p e n", e=2)[:, t], in0=terms[0], in1=terms[1], op=ALU.add)
 
@@ -191,6 +192,11 @@ def tile_picked_headrope_none_po_kernel(tc, x_words, x_scales, w1, w2, ct, st, w
         def weave(b, cols):
             nc.scalar.copy(out=z_bf[b][:].bitcast(F32).rearrange("p (c i u) -> p c u i", i=2, u=2)[:, cols], in_=halves[b].rearrange("p u (c i) -> p c u i", i=2)[:, cols])
 
+        def whole_sums(b, a):
+            terms = [prod[k][:, :, b, a].rearrange("p t (c i) -> p c t i", i=2) for k in range(2)]
+            dst = z_bf[b][:].rearrange("p (a c i t) -> p a c t i", a=2, i=2, t=PACK)[:, a]
+            nc.vector.tensor_tensor(out=dst, in0=terms[0], in1=terms[1], op=ALU.add)
+
         def quantize_z(b, a):
             nc.vector.quantize_mx(out=z_codes[b][:, a].rearrange("p a n -> p (a n)").bitcast(FP8X4),
                                   scales=z_sc[b][:, a].rearrange("p a n -> p (a n)"),
@@ -209,6 +215,8 @@ def tile_picked_headrope_none_po_kernel(tc, x_words, x_scales, w1, w2, ct, st, w
                         one_pass(acc[:, t, :], b, t, a, a == 0, a == 1)
                 nc.scalar.copy(out=o_f32[b][:], in_=acc[:])
                 nc.sync.dma_start(out=out_v[:, :, toks_of(b)], in_=o_f32[b][:])
+                if b == 1:
+                    nc.scalar.copy(out=o_bf[b][:].rearrange("p (n t) -> p n t", t=PACK), in_=acc[:].rearrange("p t n -> p n t"))
                 return
             accs = [bank((b + 1 if b else 0) + h, [P, 2, BLK]) for h in range(2)]
             for a in range(2):
@@ -234,7 +242,10 @@ def tile_picked_headrope_none_po_kernel(tc, x_words, x_scales, w1, w2, ct, st, w
                 nc.sync.dma_start(out=out_words[:, both], in_=o_codes[:, both].bitcast(I32))
 
         for b in range(NBLK):
-            if 0 < b < last:
+            if b == last:
+                whole_sums(b, 0)
+                whole_sums(b, 1)
+            elif b:
                 pair_sums(b, slice(0, 2))
                 weave(b, slice(0, BLK))
             else:
@@ -256,7 +267,7 @@ def tile_picked_headrope_none_po_kernel(tc, x_words, x_scales, w1, w2, ct, st, w
         quantize_z(last, slice(1, 2))
         for b in range(last):
             second_product(b)
-        for b in range(last):
+        for b in (0, 2):
             round_out(b)
         for b in range(last):
             hand_on(b)

@@ -106,9 +106,9 @@ def tile_picked_headrope_none_po_kernel(tc, x_words, x_scales, w1, w2, ct, st, w
 
         trig = [[sb("trig%d_%d" % (k, t), [P, S], F32) for t in range(PACK)] for k in range(2)]
         prod = [sb("prod%d" % k, [P, PACK, NBLK, 2, BLK], F32) for k in range(2)]
-        groups = (slice(0, 2), slice(2, 3))
-        halves2 = [sb("halves%d" % h, [P, 2, bs.stop - bs.start, 2 * BLK], F32) for h, bs in enumerate(groups)]
-        halves = [halves2[b // 2][:, :, b % 2] for b in range(NBLK - 1)]
+        woven = NBLK - 1
+        halves = sb("halves", [P, 2, woven, 2, BLK], F32)
+        sign = (ALU.subtract, ALU.add)
 
         def blocks(ap):
             return ap.rearrange("p (b n) -> p b n", b=NBLK)
@@ -117,24 +117,19 @@ def tile_picked_headrope_none_po_kernel(tc, x_words, x_scales, w1, w2, ct, st, w
             look = blocks(trig[k][t][:])[:, bs]
             dst = prod[k][:, t, bs]
             y, e = blocks(proj[0][t][:])[:, bs], blocks(proj[1][t][:])[:, bs]
-            if k == 0:
-                nc.vector.tensor_tensor(out=dst[:, :, 1, :], in0=e, in1=look, op=ALU.mult)
-            else:
-                nc.vector.scalar_tensor_tensor(out=dst[:, :, 0, :], in0=e, scalar=-1.0, in1=look, op0=ALU.mult, op1=ALU.mult)
+            nc.vector.tensor_tensor(out=dst[:, :, 1 - k, :], in0=e, in1=look, op=ALU.mult)
             if (k, t) in on_gpsimd:
                 nc.gpsimd.tensor_tensor(out=dst[:, :, k, :], in0=blocks(y_sb[t][:])[:, bs], in1=look, op=ALU.mult)
             else:
                 nc.vector.tensor_tensor(out=dst[:, :, k, :], in0=y, in1=look, op=ALU.mult)
 
         def pair_sums(b, a):
-            terms = [prod[k][:, 2:4, b, a].rearrange("p e a (c i) -> p (a c) e i", i=4) for k in range(2)]
-            upper = halves[b][:, 1, a.start * BLK : a.stop * BLK]
-            nc.vector.tensor_tensor(out=upper.bitcast(BF16).rearrange("p (c i e) -> p c e i", i=4, e=2), in0=terms[0], in1=terms[1], op=ALU.add)
+            terms = [prod[k][:, 2:4, b, a].rearrange("p e (c i) -> p c e i", i=4) for k in range(2)]
+            nc.vector.tensor_tensor(out=halves[:, 1, b, a].bitcast(BF16).rearrange("p (c i e) -> p c e i", i=4, e=2), in0=terms[0], in1=terms[1], op=sign[a])
 
-        def slot_sums(t, h):
-            terms = [prod[k][:, t, groups[h]].rearrange("p b a n -> p (b a n)") for k in range(2)]
-            lower = halves2[h][:, 0].rearrange("p b n -> p (b n)")
-            nc.gpsimd.tensor_tensor(out=lower.bitcast(BF16).rearrange("p (n e) -> p e n", e=2)[:, t], in0=terms[0], in1=terms[1], op=ALU.add)
+        def slot_sums(t, a):
+            terms = [prod[k][:, t, :woven, a] for k in range(2)]
+            nc.gpsimd.tensor_tensor(out=halves[:, 0, :, a].bitcast(BF16).rearrange("p b (n e) -> p e b n", e=2)[:, t], in0=terms[0], in1=terms[1], op=sign[a])
 
         on_gpsimd = ((0, 0), (1, 0))
         y_sb = [sb("y_sb0", [P, S], F32)]
@@ -163,8 +158,8 @@ def tile_picked_headrope_none_po_kernel(tc, x_words, x_scales, w1, w2, ct, st, w
                 wos = keep.tile([P, N], U8, name="wos", tag="trig0_0", align_bytes=64)
                 nc.vector.tensor_copy(out=wos[:].rearrange("p (t m) -> p m t", t=PACK), in_=wos_raw[:].rearrange("p (m t) -> p m t", t=PACK))
             if k == 1 and t < 2:
-                for h in range(2):
-                    slot_sums(t, h)
+                for a in range(2):
+                    slot_sums(t, a)
         look_up_scalar(1, 3, early)
         look_up_scalar(1, 3, late)
         products(1, 3, early)
@@ -178,7 +173,8 @@ def tile_picked_headrope_none_po_kernel(tc, x_words, x_scales, w1, w2, ct, st, w
         z_codes = [sb("z_codes%d" % b, [P, 2, BLK], U32) for b in range(NBLK)]
         z_sc = [sb("z_sc%d" % b, [P, 2, BLK], U8) for b in range(NBLK)]
         o_bf = [sb("o_bf%d" % b, [P, BLK * PACK], BF16) for b in range(NBLK)]
-        o_f32 = [sb("o_f32%d" % b, [P, PACK, BLK], F32) for b in range(NBLK)]
+        o_f32 = [keep.tile([P, PACK, BLK], F32, name="o_f32_0", tag="halves", align_bytes=64)]
+        o_f32 = o_f32 + [sb("o_f32%d" % b, [P, PACK, BLK], F32) for b in range(1, NBLK)]
         o_codes = sb("o_codes", [P, S], U32)
         o_sc = sb("o_sc", [P, S], U8)
         out_v = out_0.rearrange("(p t) n -> p t n", t=PACK)
@@ -190,12 +186,12 @@ def tile_picked_headrope_none_po_kernel(tc, x_words, x_scales, w1, w2, ct, st, w
             return slice(b * BLK, (b + 1) * BLK)
 
         def weave(b, cols):
-            nc.scalar.copy(out=z_bf[b][:].bitcast(F32).rearrange("p (c i u) -> p c u i", i=2, u=2)[:, cols], in_=halves[b].rearrange("p u (c i) -> p c u i", i=2)[:, cols])
+            nc.scalar.copy(out=z_bf[b][:].bitcast(F32).rearrange("p (c i u) -> p c u i", i=2, u=2)[:, cols], in_=halves[:, :, b].rearrange("p u a (c i) -> p (a c) u i", i=2)[:, cols])
 
         def whole_sums(b, a):
             terms = [prod[k][:, :, b, a].rearrange("p t (c i) -> p c t i", i=2) for k in range(2)]
             dst = z_bf[b][:].rearrange("p (a c i t) -> p a c t i", a=2, i=2, t=PACK)[:, a]
-            nc.vector.tensor_tensor(out=dst, in0=terms[0], in1=terms[1], op=ALU.add)
+            nc.vector.tensor_tensor(out=dst, in0=terms[0], in1=terms[1], op=sign[a])
 
         def quantize_z(b, a):
             nc.vector.quantize_mx(out=z_codes[b][:, a].rearrange("p a n -> p (a n)").bitcast(FP8X4),
@@ -215,8 +211,6 @@ def tile_picked_headrope_none_po_kernel(tc, x_words, x_scales, w1, w2, ct, st, w
                         one_pass(acc[:, t, :], b, t, a, a == 0, a == 1)
                 nc.scalar.copy(out=o_f32[b][:], in_=acc[:])
                 nc.sync.dma_start(out=out_v[:, :, toks_of(b)], in_=o_f32[b][:])
-                if b == 1:
-                    nc.scalar.copy(out=o_bf[b][:].rearrange("p (n t) -> p n t", t=PACK), in_=acc[:].rearrange("p t n -> p n t"))
                 return
             accs = [bank((b + 1 if b else 0) + h, [P, 2, BLK]) for h in range(2)]
             for a in range(2):
@@ -246,12 +240,13 @@ def tile_picked_headrope_none_po_kernel(tc, x_words, x_scales, w1, w2, ct, st, w
                 whole_sums(b, 0)
                 whole_sums(b, 1)
             elif b:
-                pair_sums(b, slice(0, 2))
+                pair_sums(b, 0)
+                pair_sums(b, 1)
                 weave(b, slice(0, BLK))
             else:
-                pair_sums(b, slice(0, 1))
+                pair_sums(b, 0)
                 weave(b, slice(0, BLK // 2))
-                pair_sums(b, slice(1, 2))
+                pair_sums(b, 1)
                 weave(b, slice(BLK // 2, BLK))
             if b == 0:
                 products(1, 3, late)
@@ -267,7 +262,7 @@ def tile_picked_headrope_none_po_kernel(tc, x_words, x_scales, w1, w2, ct, st, w
         quantize_z(last, slice(1, 2))
         for b in range(last):
             second_product(b)
-        for b in (0, 2):
+        for b in range(last):
             round_out(b)
         for b in range(last):
             hand_on(b)

@@ -60,7 +60,7 @@ def tile_picked_headrope_none_po_kernel(tc, x_words, x_scales, w1, w2, ct, st, w
         nc.sync.dma_start(offs_t[:], offs)
         for dst, src in scale_rows(xs_tab, 0, x_scales):
             nc.sync.dma_start(out=dst, in_=src)
-        narrow = scale_rows(wos_raw, 0, w3_scales) + scale_rows(wos_raw, 4, w4_scales)
+        narrow = scale_rows(wos_raw, 4, w3_scales) + scale_rows(wos_raw, 8, w4_scales)
 
         def load_narrow(first, end):
             for dst, src in narrow[first:end]:
@@ -98,7 +98,7 @@ def tile_picked_headrope_none_po_kernel(tc, x_words, x_scales, w1, w2, ct, st, w
             dst, src = deal_views(i, slice(VECTOR_GROUPS, P))
             nc.scalar.activation(out=dst, in_=src, func=COPY)
             nc.vector.quantize_mx(out=w_codes[i][:].bitcast(FP8X4), scales=w_sc[i][:], in_=w_bf[i][:])
-            for t in range(PACK):
+            for t in ((0, 3, 1, 2), (0, 1, 2, 3))[i]:
                 proj[i][t] = bank(2 * t + i, [P, S])
                 cols = slice(t * P, (t + 1) * P)
                 nc.tensor.matmul_mx(out=proj[i][t][:], lhsT=w_codes[i][:, cols].bitcast(FP8X4), lhsT_scale=w_sc[i][:, cols],
@@ -113,15 +113,11 @@ def tile_picked_headrope_none_po_kernel(tc, x_words, x_scales, w1, w2, ct, st, w
         def blocks(ap):
             return ap.rearrange("p (b n) -> p b n", b=NBLK)
 
-        def products(k, t, bs):
-            look = blocks(trig[k][t][:])[:, bs]
-            dst = prod[k][:, t, bs]
-            y, e = blocks(proj[0][t][:])[:, bs], blocks(proj[1][t][:])[:, bs]
-            nc.vector.tensor_tensor(out=dst[:, :, 1 - k, :], in0=e, in1=look, op=ALU.mult)
-            if (k, t) in on_gpsimd:
-                nc.gpsimd.tensor_tensor(out=dst[:, :, k, :], in0=blocks(y_sb[t][:])[:, bs], in1=look, op=ALU.mult)
-            else:
-                nc.vector.tensor_tensor(out=dst[:, :, k, :], in0=y, in1=look, op=ALU.mult)
+        def product(engine, i, k, t, bs, factor):
+            engine.tensor_tensor(out=prod[k][:, t, bs, k if i == 0 else 1 - k, :], in0=factor, in1=blocks(trig[k][t][:])[:, bs], op=ALU.mult)
+
+        def on_vector(i, k, t, bs):
+            product(nc.vector, i, k, t, bs, blocks(proj[i][t][:])[:, bs])
 
         def pair_sums(b, a):
             terms = [prod[k][:, 2:4, b, a].rearrange("p e (c i) -> p c e i", i=4) for k in range(2)]
@@ -130,9 +126,6 @@ def tile_picked_headrope_none_po_kernel(tc, x_words, x_scales, w1, w2, ct, st, w
         def slot_sums(t, a):
             terms = [prod[k][:, t, :woven, a] for k in range(2)]
             nc.gpsimd.tensor_tensor(out=halves[:, 0, :, a].bitcast(BF16).rearrange("p b (n e) -> p e b n", e=2)[:, t], in0=terms[0], in1=terms[1], op=sign[a])
-
-        on_gpsimd = ((0, 0), (1, 0))
-        y_sb = [sb("y_sb0", [P, S], F32)]
 
         early, late = slice(0, NBLK // 2), slice(NBLK // 2, NBLK)
 
@@ -146,23 +139,39 @@ def tile_picked_headrope_none_po_kernel(tc, x_words, x_scales, w1, w2, ct, st, w
             nc.vector.tensor_copy(trig[k][t][:, bs.start * BLK : bs.stop * BLK], window(k, t, bs))
 
         whole = slice(0, NBLK)
-        nc.scalar.copy(out=y_sb[0][:], in_=proj[0][0][:])
-        for k, t in tab_order[:-1]:
-            if (k, t) == (1, 0):
-                look_up_vector(k, t, late)
-                look_up_scalar(k, t, early)
-            else:
+        y_first = sb("y_first", [P, NBLK, BLK], F32)
+        y_late = sb("y_late", [P, NBLK // 2, BLK], F32)
+        nc.scalar.copy(out=y_first[:], in_=blocks(proj[0][0][:]))
+        nc.scalar.copy(out=y_late[:], in_=blocks(proj[0][3][:])[:, late])
+
+        look_up_scalar(0, 0, whole)
+        on_vector(1, 0, 0, whole)
+        product(nc.gpsimd, 0, 0, 0, whole, y_first[:])
+        look_up_vector(1, 0, late)
+        look_up_scalar(1, 0, early)
+        on_vector(1, 1, 0, whole)
+        product(nc.gpsimd, 0, 1, 0, whole, y_first[:])
+        wos = keep.tile([P, N], U8, name="wos", tag="trig0_0", align_bytes=64)
+        nc.vector.tensor_copy(out=wos[:].rearrange("p (t m) -> p m t", t=PACK), in_=wos_raw[:].rearrange("p (m t) -> p m t", t=PACK))
+        for a in range(2):
+            slot_sums(0, a)
+        for t in (1, 2):
+            for k in range(2):
                 look_up_scalar(k, t, whole)
-            products(k, t, whole)
-            if (k, t) == (1, 0):
-                wos = keep.tile([P, N], U8, name="wos", tag="trig0_0", align_bytes=64)
-                nc.vector.tensor_copy(out=wos[:].rearrange("p (t m) -> p m t", t=PACK), in_=wos_raw[:].rearrange("p (m t) -> p m t", t=PACK))
-            if k == 1 and t < 2:
+                on_vector(1, k, t, whole)
+                on_vector(0, k, t, whole)
+            if t == 1:
                 for a in range(2):
-                    slot_sums(t, a)
+                    slot_sums(1, a)
+        look_up_scalar(0, 3, whole)
+        on_vector(1, 0, 3, whole)
+        on_vector(0, 0, 3, early)
+        product(nc.gpsimd, 0, 0, 3, late, y_late[:])
         look_up_scalar(1, 3, early)
         look_up_scalar(1, 3, late)
-        products(1, 3, early)
+        on_vector(1, 1, 3, early)
+        on_vector(0, 1, 3, early)
+        product(nc.gpsimd, 0, 1, 3, late, y_late[:])
 
         wo = sb("wo", [P, 2, N], U32)
         for a in range(2):
@@ -173,8 +182,9 @@ def tile_picked_headrope_none_po_kernel(tc, x_words, x_scales, w1, w2, ct, st, w
         z_codes = [sb("z_codes%d" % b, [P, 2, BLK], U32) for b in range(NBLK)]
         z_sc = [sb("z_sc%d" % b, [P, 2, BLK], U8) for b in range(NBLK)]
         o_bf = [sb("o_bf%d" % b, [P, BLK * PACK], BF16) for b in range(NBLK)]
-        o_f32 = [keep.tile([P, PACK, BLK], F32, name="o_f32_0", tag="halves", align_bytes=64)]
-        o_f32 = o_f32 + [sb("o_f32%d" % b, [P, PACK, BLK], F32) for b in range(1, NBLK)]
+        o_first = halves[:, 1, 1:woven].rearrange("p b a n -> p (b a) n")
+        o_mid = {b: sb("o_mid%d" % b, [P, PACK, BLK], F32) for b in (1, 2)}
+        o_last = sb("o_last", [P, PACK, BLK], F32)
         o_codes = sb("o_codes", [P, S], U32)
         o_sc = sb("o_sc", [P, S], U8)
         out_v = out_0.rearrange("(p t) n -> p t n", t=PACK)
@@ -200,40 +210,34 @@ def tile_picked_headrope_none_po_kernel(tc, x_words, x_scales, w1, w2, ct, st, w
 
         def one_pass(out, b, t, a, start, stop):
             cols = slice(t * P, (t + 1) * P)
-            nc.tensor.matmul_mx(out=out, lhsT=wo[:, a, cols].bitcast(FP8X4), lhsT_scale=wos[4 * a :, cols],
+            nc.tensor.matmul_mx(out=out, lhsT=wo[:, a, cols].bitcast(FP8X4), lhsT_scale=wos[4 + 4 * a :, cols],
                                 rhs=z_codes[b][:, a, :].bitcast(FP8X4), rhs_scale=z_sc[b][:, a, :], start=start, stop=stop)
 
-        def second_product(b):
-            if 0 < b < last:
-                acc = bank(b + 1, [P, PACK, BLK])
-                for t in range(PACK):
-                    for a in range(2):
-                        one_pass(acc[:, t, :], b, t, a, a == 0, a == 1)
-                nc.scalar.copy(out=o_f32[b][:], in_=acc[:])
-                nc.sync.dma_start(out=out_v[:, :, toks_of(b)], in_=o_f32[b][:])
-                return
-            accs = [bank((b + 1 if b else 0) + h, [P, 2, BLK]) for h in range(2)]
+        def whole_bank(b):
+            acc = bank(b + 1, [P, PACK, BLK])
+            for t in range(PACK):
+                for a in range(2):
+                    one_pass(acc[:, t, :], b, t, a, a == 0, a == 1)
+            nc.scalar.copy(out=o_mid[b][:], in_=acc[:])
+            nc.sync.dma_start(out=out_v[:, :, toks_of(b)], in_=o_mid[b][:])
+
+        def two_banks(b, first_bank):
+            accs = [bank(first_bank + h, [P, 2, BLK]) for h in range(2)]
             for a in range(2):
                 for t in range(PACK):
                     one_pass(accs[t // 2][:, t % 2, :], b, t, a, a == 0 and t % 2 == 0, a == 1 and t % 2 == 1)
-            for h, copy in enumerate((nc.scalar.copy, nc.vector.tensor_copy if b else nc.scalar.copy)):
-                ts = slice(2 * h, 2 * h + 2)
-                copy(out=o_f32[b][:, ts], in_=accs[h][:])
-                if b == 0:
-                    nc.sync.dma_start(out=out_v[:, ts, toks_of(b)], in_=o_f32[b][:, ts])
-            if b:
-                nc.sync.dma_start(out=out_v[:, :, toks_of(b)], in_=o_f32[b][:])
+            return accs
 
-        def round_out(b):
-            nc.vector.tensor_copy(out=o_bf[b][:].rearrange("p (c i t) -> p c t i", i=4, t=PACK),
-                                  in_=o_f32[b][:].rearrange("p t (c i) -> p c t i", i=4))
+        def round_out(b, src):
+            nc.vector.tensor_copy(out=o_bf[b][:].rearrange("p (c i t) -> p c t i", i=4, t=PACK), in_=src.rearrange("p t (c i) -> p c t i", i=4))
 
-        def hand_on(b):
+        def quantize_out(b):
             toks = toks_of(b)
             nc.vector.quantize_mx(out=o_codes[:, toks].bitcast(FP8X4), scales=o_sc[:, toks], in_=o_bf[b][:])
-            if b % 2:
-                both = slice((b - 1) * BLK, (b + 1) * BLK)
-                nc.sync.dma_start(out=out_words[:, both], in_=o_codes[:, both].bitcast(I32))
+
+        def store_words(first, end):
+            toks = slice(first * BLK, end * BLK)
+            nc.sync.dma_start(out=out_words[:, toks], in_=o_codes[:, toks].bitcast(I32))
 
         for b in range(NBLK):
             if b == last:
@@ -249,8 +253,8 @@ def tile_picked_headrope_none_po_kernel(tc, x_words, x_scales, w1, w2, ct, st, w
                 pair_sums(b, 1)
                 weave(b, slice(BLK // 2, BLK))
             if b == 0:
-                products(1, 3, late)
-                idle = bank(2 * PACK - 2, [P, PACK, BLK])
+                on_vector(1, 1, 3, late)
+                idle = bank(2 * PACK - 1, [P, PACK, BLK])
                 for n in range(WARM_UPS):
                     nc.tensor.matmul_mx(out=idle[:, n % PACK, :], lhsT=w_codes[0][:, :P].bitcast(FP8X4), lhsT_scale=w_sc[0][:, :P],
                                         rhs=w_codes[1][:, :BLK].bitcast(FP8X4), rhs_scale=w_sc[1][:, :BLK], start=True, stop=True)
@@ -260,15 +264,23 @@ def tile_picked_headrope_none_po_kernel(tc, x_words, x_scales, w1, w2, ct, st, w
                 quantize_z(b - 1, slice(0, 2))
         quantize_z(last, slice(0, 1))
         quantize_z(last, slice(1, 2))
+        for h, acc in enumerate(two_banks(0, 0)):
+            ts = slice(2 * h, 2 * h + 2)
+            nc.scalar.copy(out=o_first[:, ts], in_=acc[:])
+            nc.sync.dma_start(out=out_v[:, ts, toks_of(0)], in_=o_first[:, ts])
+        whole_bank(1)
+        whole_bank(2)
+        round_out(0, o_first)
+        for b in (1, 2):
+            round_out(b, o_mid[b][:])
         for b in range(last):
-            second_product(b)
-        for b in range(last):
-            round_out(b)
-        for b in range(last):
-            hand_on(b)
-        second_product(last)
-        round_out(last)
-        hand_on(last)
+            quantize_out(b)
+        store_words(0, last)
+        for h, (acc, copy) in enumerate(zip(two_banks(last, 4), (nc.scalar.copy, nc.vector.tensor_copy))):
+            copy(out=o_last[:, 2 * h : 2 * h + 2], in_=acc[:])
+        nc.sync.dma_start(out=out_v[:, :, toks_of(last)], in_=o_last[:])
+        round_out(last, o_last[:])
+        quantize_out(last)
+        store_words(last, NBLK)
         for q in range(4):
-            queue = nc.scalar if q % 2 else nc.sync
-            queue.dma_start(out=out_2[0][4 * q : 4 * q + 4, :].bitcast(I32), in_=o_sc[32 * q : 32 * q + 4, :].bitcast(I32))
+            nc.scalar.dma_start(out=out_2[0][4 * q : 4 * q + 4, :].bitcast(I32), in_=o_sc[32 * q : 32 * q + 4, :].bitcast(I32))

@@ -144,15 +144,16 @@ def tile_picked_headrope_none_po_kernel(tc, x_words, x_scales, w1, w2, ct, st, w
         nc.scalar.copy(out=y_first[:], in_=blocks(proj[0][0][:]))
         nc.scalar.copy(out=y_late[:], in_=blocks(proj[0][3][:])[:, late])
 
-        look_up_scalar(0, 0, whole)
+        look_up_vector(0, 0, late)
+        look_up_scalar(0, 0, early)
         on_vector(1, 0, 0, whole)
         product(nc.gpsimd, 0, 0, 0, whole, y_first[:])
-        look_up_vector(1, 0, late)
-        look_up_scalar(1, 0, early)
+        look_up_scalar(1, 0, whole)
         on_vector(1, 1, 0, whole)
         product(nc.gpsimd, 0, 1, 0, whole, y_first[:])
-        wos = keep.tile([P, N], U8, name="wos", tag="trig0_0", align_bytes=64)
-        nc.vector.tensor_copy(out=wos[:].rearrange("p (t m) -> p m t", t=PACK), in_=wos_raw[:].rearrange("p (m t) -> p m t", t=PACK))
+        wos = sb("wos", [P, N], U8)
+        for ms in (slice(0, P - 3), slice(P - 3, P)):
+            nc.vector.tensor_copy(out=wos[:].rearrange("p (t m) -> p m t", t=PACK)[:, ms], in_=wos_raw[:].rearrange("p (m t) -> p m t", t=PACK)[:, ms])
         for a in range(2):
             slot_sums(0, a)
         for t in (1, 2):

@@ -140,9 +140,9 @@ def tile_picked_headrope_none_po_kernel(tc, x_words, x_scales, w1, w2, ct, st, w
 
         whole = slice(0, NBLK)
         y_first = sb("y_first", [P, NBLK, BLK], F32)
-        y_late = sb("y_late", [P, NBLK // 2, BLK], F32)
+        y_last = sb("y_last", [P, NBLK // 2, BLK], F32)
         nc.scalar.copy(out=y_first[:], in_=blocks(proj[0][0][:]))
-        nc.scalar.copy(out=y_late[:], in_=blocks(proj[0][3][:])[:, late])
+        nc.scalar.copy(out=y_last[:], in_=blocks(proj[0][3][:])[:, early])
 
         look_up_vector(0, 0, late)
         look_up_scalar(0, 0, early)
@@ -166,13 +166,13 @@ def tile_picked_headrope_none_po_kernel(tc, x_words, x_scales, w1, w2, ct, st, w
                     slot_sums(1, a)
         look_up_scalar(0, 3, whole)
         on_vector(1, 0, 3, whole)
-        on_vector(0, 0, 3, early)
-        product(nc.gpsimd, 0, 0, 3, late, y_late[:])
+        product(nc.gpsimd, 0, 0, 3, early, y_last[:])
         look_up_scalar(1, 3, early)
         look_up_scalar(1, 3, late)
         on_vector(1, 1, 3, early)
-        on_vector(0, 1, 3, early)
-        product(nc.gpsimd, 0, 1, 3, late, y_late[:])
+        product(nc.gpsimd, 0, 1, 3, early, y_last[:])
+        on_vector(0, 0, 3, late)
+        on_vector(1, 1, 3, late)
 
         wo = sb("wo", [P, 2, N], U32)
         for a in range(2):
@@ -254,7 +254,7 @@ def tile_picked_headrope_none_po_kernel(tc, x_words, x_scales, w1, w2, ct, st, w
                 pair_sums(b, 1)
                 weave(b, slice(BLK // 2, BLK))
             if b == 0:
-                on_vector(1, 1, 3, late)
+                on_vector(0, 1, 3, late)
                 idle = bank(2 * PACK - 1, [P, PACK, BLK])
                 for n in range(WARM_UPS):
                     nc.tensor.matmul_mx(out=idle[:, n % PACK, :], lhsT=w_codes[0][:, :P].bitcast(FP8X4), lhsT_scale=w_sc[0][:, :P],

@@ -19,8 +19,11 @@ P = 128
 PACK = 4
 BLK = 128
 NBLK = S // BLK
-VECTOR_GROUPS = 92
+W1_GROUPS = 86
+W2_GROUPS = 92
 WARM_UPS = 6
+Y, E = 0, 1
+COS, SIN = 0, 1
 
 
 def tile_picked_headrope_none_po_kernel(tc, x_words, x_scales, w1, w2, ct, st, w3_words, w3_scales, w4_words, w4_scales, offs, pos, out_0, out_1, out_2):
@@ -45,8 +48,8 @@ def tile_picked_headrope_none_po_kernel(tc, x_words, x_scales, w1, w2, ct, st, w
         pos_t = keep.tile([P, S // 16], U16, name="pos_t")
         x_tab = sb("x_tab", [P, T], U32)
         xs_tab = sb("xs_tab", [P, T], U8)
-        w_raw = [sb("w_raw%d" % i, [P, PACK, H], F32) for i in range(2)]
-        tabs = [[sb("tab%d_%d" % (k, t), [P, U], F32) for t in range(PACK)] for k in range(2)]
+        w_raw = [sb("w_raw%d" % i, [P, PACK, H], F32) for i in (Y, E)]
+        tabs = [[sb("tab%d_%d" % (k, t), [P, U], F32) for t in range(PACK)] for k in (COS, SIN)]
         wo_raw = sb("wo_raw", [P, 2, N], U32)
         wos_raw = sb("wos_raw", [P, N], U8)
 
@@ -54,26 +57,24 @@ def tile_picked_headrope_none_po_kernel(tc, x_words, x_scales, w1, w2, ct, st, w
         nc.vector.memset(wos_raw[:].bitcast(I32), 0)
 
         tab_v = [dram.rearrange("(p t) u -> p t u", t=PACK) for dram in (ct, st)]
-        tab_order = [(k, t) for t in range(PACK) for k in range(2)]
+        narrow = scale_rows(wos_raw, 4, w3_scales) + scale_rows(wos_raw, 8, w4_scales)
+
+        def load_rows(rows):
+            for dst, src in rows:
+                nc.sync.dma_start(out=dst, in_=src)
 
         nc.sync.dma_start(out=x_tab[:].bitcast(I32), in_=words_of(x_words))
         nc.sync.dma_start(offs_t[:], offs)
-        for dst, src in scale_rows(xs_tab, 0, x_scales):
-            nc.sync.dma_start(out=dst, in_=src)
-        narrow = scale_rows(wos_raw, 4, w3_scales) + scale_rows(wos_raw, 8, w4_scales)
-
-        def load_narrow(first, end):
-            for dst, src in narrow[first:end]:
-                nc.sync.dma_start(out=dst, in_=src)
-
-        nc.sync.dma_start(out=w_raw[0][:], in_=w1.rearrange("(p j) c -> p j c", j=PACK))
+        load_rows(scale_rows(xs_tab, 0, x_scales))
+        nc.sync.dma_start(out=w_raw[Y][:], in_=w1.rearrange("(p j) c -> p j c", j=PACK))
         nc.sync.dma_start(pos_t[:], pos)
-        nc.sync.dma_start(out=w_raw[1][:], in_=w2.rearrange("(p j) c -> p j c", j=PACK))
-        load_narrow(0, 4)
-        for n, (k, t) in enumerate(tab_order):
-            nc.sync.dma_start(out=tabs[k][t][:], in_=tab_v[k][:, t, :])
-            if n == 2:
-                load_narrow(4, 8)
+        nc.sync.dma_start(out=w_raw[E][:], in_=w2.rearrange("(p j) c -> p j c", j=PACK))
+        load_rows(narrow[:4])
+        for t in range(PACK):
+            for k in (COS, SIN):
+                nc.sync.dma_start(out=tabs[k][t][:], in_=tab_v[k][:, t, :])
+                if (t, k) == (1, COS):
+                    load_rows(narrow[4:])
         for a, dram in enumerate((w3_words, w4_words)):
             nc.sync.dma_start(out=wo_raw[:, a, :].bitcast(I32), in_=words_of(dram))
 
@@ -82,108 +83,118 @@ def tile_picked_headrope_none_po_kernel(tc, x_words, x_scales, w1, w2, ct, st, w
         nc.vector.tensor_copy(x_codes[:], x_tab[:].indirect(offs_t[:]))
         nc.vector.tensor_copy(x_sc[:], xs_tab[:].indirect(offs_t[:]))
 
-        w_bf = [sb("w_bf%d" % i, [P, PACK * H], BF16) for i in range(2)]
-        w_codes = [sb("w_codes%d" % i, [P, H], U32) for i in range(2)]
-        w_sc = [sb("w_sc%d" % i, [P, H], U8) for i in range(2)]
+        w_bf = [sb("w_bf%d" % i, [P, PACK * H], BF16) for i in (Y, E)]
+        w_codes = [sb("w_codes%d" % i, [P, H], U32) for i in (Y, E)]
+        w_sc = [sb("w_sc%d" % i, [P, H], U8) for i in (Y, E)]
 
-        def deal_views(i, ms):
-            dst = w_bf[i][:].rearrange("p (t m j) -> p m j t", t=PACK, j=PACK)
-            src = w_raw[i][:].rearrange("p j (m t) -> p m j t", t=PACK)
-            return dst[:, ms], src[:, ms]
+        trig = [[sb("trig%d_%d" % (k, t), [P, S], F32) for t in range(PACK)] for k in (COS, SIN)]
+        whole, early, late = slice(0, NBLK), slice(0, NBLK // 2), slice(NBLK // 2, NBLK)
 
-        proj = [[None] * PACK for i in range(2)]
-        for i in range(2):
-            dst, src = deal_views(i, slice(0, VECTOR_GROUPS))
-            nc.vector.tensor_copy(out=dst, in_=src)
-            dst, src = deal_views(i, slice(VECTOR_GROUPS, P))
-            nc.scalar.activation(out=dst, in_=src, func=COPY)
-            nc.vector.quantize_mx(out=w_codes[i][:].bitcast(FP8X4), scales=w_sc[i][:], in_=w_bf[i][:])
-            for t in ((0, 3, 1, 2), (0, 1, 2, 3))[i]:
+        def look_up(on_vector, k, t, bs):
+            dst = trig[k][t][:, bs.start * BLK : bs.stop * BLK]
+            src = tabs[k][t][:].indirect(pos_t[:, bs.start * BLK // 16 : bs.stop * BLK // 16])
+            if on_vector:
+                nc.vector.tensor_copy(dst, src)
+            else:
+                nc.scalar.activation(out=dst, in_=src, func=COPY)
+
+        def round_weight(on_vector, i, ms, ts):
+            dst = w_bf[i][:].rearrange("p (t m j) -> p m j t", t=PACK, j=PACK)[:, ms, :, ts]
+            src = w_raw[i][:].rearrange("p j (m t) -> p m j t", t=PACK)[:, ms, :, ts]
+            if on_vector:
+                nc.vector.tensor_copy(out=dst, in_=src)
+            else:
+                nc.scalar.activation(out=dst, in_=src, func=COPY)
+
+        proj = [[None] * PACK for i in (Y, E)]
+
+        def project(i, first, end):
+            cols = slice(first * P, end * P)
+            nc.vector.quantize_mx(out=w_codes[i][:, cols].bitcast(FP8X4), scales=w_sc[i][:, cols], in_=w_bf[i][:, first * H : end * H])
+            for t in range(first, end):
                 proj[i][t] = bank(2 * t + i, [P, S])
                 cols = slice(t * P, (t + 1) * P)
                 nc.tensor.matmul_mx(out=proj[i][t][:], lhsT=w_codes[i][:, cols].bitcast(FP8X4), lhsT_scale=w_sc[i][:, cols],
                                     rhs=x_codes[:].bitcast(FP8X4), rhs_scale=x_sc[:], start=True, stop=True)
 
-        trig = [[sb("trig%d_%d" % (k, t), [P, S], F32) for t in range(PACK)] for k in range(2)]
-        prod = [sb("prod%d" % k, [P, PACK, NBLK, 2, BLK], F32) for k in range(2)]
-        woven = NBLK - 1
-        halves = sb("halves", [P, 2, woven, 2, BLK], F32)
-        sign = (ALU.subtract, ALU.add)
+        round_weight(True, Y, slice(0, W1_GROUPS), slice(0, PACK))
+        round_weight(False, Y, slice(W1_GROUPS, P), slice(0, PACK))
+        for first, end in ((0, 1), (3, 4), (1, 3)):
+            project(Y, first, end)
+        round_weight(True, E, slice(0, P), slice(0, 2))
+        round_weight(True, E, slice(0, W2_GROUPS), slice(2, 4))
+        round_weight(False, E, slice(W2_GROUPS, P), slice(2, 4))
+        for first in (0, 2):
+            project(E, first, first + 2)
+
+        term = [sb("term%d" % k, [P, PACK, NBLK, 2, BLK], F32) for k in (COS, SIN)]
+        last = NBLK - 1
+        pairs = sb("pairs", [P, 2, last, 2, BLK], F32)
 
         def blocks(ap):
             return ap.rearrange("p (b n) -> p b n", b=NBLK)
 
-        def product(engine, i, k, t, bs, factor):
-            engine.tensor_tensor(out=prod[k][:, t, bs, k if i == 0 else 1 - k, :], in0=factor, in1=blocks(trig[k][t][:])[:, bs], op=ALU.mult)
+        def term_of(i, k, t, bs):
+            return term[k][:, t, bs, (i + k) % 2, :]
 
-        def on_vector(i, k, t, bs):
-            product(nc.vector, i, k, t, bs, blocks(proj[i][t][:])[:, bs])
+        def vector_product(i, k, t, bs):
+            factor, table = blocks(proj[i][t][:])[:, bs], blocks(trig[k][t][:])[:, bs]
+            if (i, k) == (E, SIN):
+                nc.vector.scalar_tensor_tensor(out=term_of(i, k, t, bs), in0=factor, scalar=-1.0, in1=table, op0=ALU.mult, op1=ALU.mult)
+            else:
+                nc.vector.tensor_tensor(out=term_of(i, k, t, bs), in0=factor, in1=table, op=ALU.mult)
 
-        def pair_sums(b, a):
-            terms = [prod[k][:, 2:4, b, a].rearrange("p e (c i) -> p c e i", i=4) for k in range(2)]
-            nc.vector.tensor_tensor(out=halves[:, 1, b, a].bitcast(BF16).rearrange("p (c i e) -> p c e i", i=4, e=2), in0=terms[0], in1=terms[1], op=sign[a])
+        def gpsimd_product(y_copy, k, t, bs):
+            nc.gpsimd.tensor_tensor(out=term_of(Y, k, t, bs), in0=y_copy, in1=blocks(trig[k][t][:])[:, bs], op=ALU.mult)
 
-        def slot_sums(t, a):
-            terms = [prod[k][:, t, :woven, a] for k in range(2)]
-            nc.gpsimd.tensor_tensor(out=halves[:, 0, :, a].bitcast(BF16).rearrange("p b (n e) -> p e b n", e=2)[:, t], in0=terms[0], in1=terms[1], op=sign[a])
+        def slot_sum(engine, t, bs, zs):
+            dst = pairs[:, t // 2, bs, zs].bitcast(BF16).rearrange("p b a (n e) -> p e b a n", e=2)[:, t % 2]
+            engine.tensor_tensor(out=dst, in0=term[COS][:, t, bs, zs], in1=term[SIN][:, t, bs, zs], op=ALU.add)
 
-        early, late = slice(0, NBLK // 2), slice(NBLK // 2, NBLK)
-
-        def window(k, t, bs):
-            return tabs[k][t][:].indirect(pos_t[:, bs.start * BLK // 16 : bs.stop * BLK // 16])
-
-        def look_up_scalar(k, t, bs):
-            nc.scalar.activation(out=trig[k][t][:, bs.start * BLK : bs.stop * BLK], in_=window(k, t, bs), func=COPY)
-
-        def look_up_vector(k, t, bs):
-            nc.vector.tensor_copy(trig[k][t][:, bs.start * BLK : bs.stop * BLK], window(k, t, bs))
-
-        whole = slice(0, NBLK)
+        both = slice(0, 2)
         y_first = sb("y_first", [P, NBLK, BLK], F32)
         y_last = sb("y_last", [P, NBLK // 2, BLK], F32)
-        nc.scalar.copy(out=y_first[:], in_=blocks(proj[0][0][:]))
-        nc.scalar.copy(out=y_last[:], in_=blocks(proj[0][3][:])[:, early])
+        nc.scalar.copy(out=y_first[:], in_=blocks(proj[Y][0][:]))
+        nc.scalar.copy(out=y_last[:], in_=blocks(proj[Y][3][:])[:, early])
 
-        look_up_vector(0, 0, late)
-        look_up_scalar(0, 0, early)
-        on_vector(1, 0, 0, whole)
-        product(nc.gpsimd, 0, 0, 0, whole, y_first[:])
-        look_up_scalar(1, 0, whole)
-        on_vector(1, 1, 0, whole)
-        product(nc.gpsimd, 0, 1, 0, whole, y_first[:])
+        look_up(True, COS, 0, late)
+        look_up(False, COS, 0, early)
+        look_up(True, SIN, 0, late)
+        vector_product(E, COS, 0, whole)
+        gpsimd_product(y_first[:], COS, 0, whole)
+        look_up(False, SIN, 0, early)
+        vector_product(E, SIN, 0, whole)
+        gpsimd_product(y_first[:], SIN, 0, whole)
         wos = sb("wos", [P, N], U8)
         for ms in (slice(0, P - 3), slice(P - 3, P)):
             nc.vector.tensor_copy(out=wos[:].rearrange("p (t m) -> p m t", t=PACK)[:, ms], in_=wos_raw[:].rearrange("p (m t) -> p m t", t=PACK)[:, ms])
-        for a in range(2):
-            slot_sums(0, a)
+        slot_sum(nc.gpsimd, 0, slice(0, last), both)
         for t in (1, 2):
-            for k in range(2):
-                look_up_scalar(k, t, whole)
-                on_vector(1, k, t, whole)
-                on_vector(0, k, t, whole)
+            for k in (COS, SIN):
+                look_up(False, k, t, whole)
+                vector_product(E, k, t, whole)
+                vector_product(Y, k, t, whole)
             if t == 1:
-                for a in range(2):
-                    slot_sums(1, a)
-        look_up_scalar(0, 3, whole)
-        on_vector(1, 0, 3, whole)
-        product(nc.gpsimd, 0, 0, 3, early, y_last[:])
-        look_up_scalar(1, 3, early)
-        look_up_scalar(1, 3, late)
-        on_vector(1, 1, 3, early)
-        product(nc.gpsimd, 0, 1, 3, early, y_last[:])
-        on_vector(0, 0, 3, late)
-        on_vector(1, 1, 3, late)
+                slot_sum(nc.gpsimd, t, slice(0, last), both)
+        look_up(False, COS, 3, whole)
+        vector_product(E, COS, 3, whole)
+        gpsimd_product(y_last[:], COS, 3, early)
+        look_up(False, SIN, 3, early)
+        look_up(False, SIN, 3, late)
+        vector_product(E, SIN, 3, early)
+        gpsimd_product(y_last[:], SIN, 3, early)
+        vector_product(Y, COS, 3, late)
+        vector_product(E, SIN, 3, late)
 
         wo = sb("wo", [P, 2, N], U32)
         for a in range(2):
             nc.scalar.copy(out=wo[:, a].rearrange("p (t m) -> p m t", t=PACK), in_=wo_raw[:, a].rearrange("p (m t) -> p m t", t=PACK))
 
-
         z_bf = [sb("z_bf%d" % b, [P, 2 * BLK * PACK], BF16) for b in range(NBLK)]
         z_codes = [sb("z_codes%d" % b, [P, 2, BLK], U32) for b in range(NBLK)]
         z_sc = [sb("z_sc%d" % b, [P, 2, BLK], U8) for b in range(NBLK)]
         o_bf = [sb("o_bf%d" % b, [P, BLK * PACK], BF16) for b in range(NBLK)]
-        o_first = halves[:, 1, 1:woven].rearrange("p b a n -> p (b a) n")
+        o_first = pairs[:, 1, 1:last].rearrange("p b a n -> p (b a) n")
         o_mid = {b: sb("o_mid%d" % b, [P, PACK, BLK], F32) for b in (1, 2)}
         o_last = sb("o_last", [P, PACK, BLK], F32)
         o_codes = sb("o_codes", [P, S], U32)
@@ -191,18 +202,20 @@ def tile_picked_headrope_none_po_kernel(tc, x_words, x_scales, w1, w2, ct, st, w
         out_v = out_0.rearrange("(p t) n -> p t n", t=PACK)
         out_words = words_of(out_1)
 
-        last = NBLK - 1
-
         def toks_of(b):
             return slice(b * BLK, (b + 1) * BLK)
 
-        def weave(b, cols):
-            nc.scalar.copy(out=z_bf[b][:].bitcast(F32).rearrange("p (c i u) -> p c u i", i=2, u=2)[:, cols], in_=halves[:, :, b].rearrange("p u a (c i) -> p (a c) u i", i=2)[:, cols])
+        def upper_sum(b, zs):
+            terms = [term[k][:, 2:4, b, zs].rearrange("p e a (c i) -> p (a c) e i", i=4) for k in (COS, SIN)]
+            nc.vector.tensor_tensor(out=pairs[:, 1, b, zs].bitcast(BF16).rearrange("p a (c i e) -> p (a c) e i", i=4, e=2), in0=terms[0], in1=terms[1], op=ALU.add)
 
-        def whole_sums(b, a):
-            terms = [prod[k][:, :, b, a].rearrange("p t (c i) -> p c t i", i=2) for k in range(2)]
+        def weave(b, cols):
+            nc.scalar.copy(out=z_bf[b][:].bitcast(F32).rearrange("p (c i u) -> p c u i", i=2, u=2)[:, cols], in_=pairs[:, :, b].rearrange("p u a (c i) -> p (a c) u i", i=2)[:, cols])
+
+        def whole_sum(b, a):
+            terms = [term[k][:, :, b, a].rearrange("p t (c i) -> p c t i", i=2) for k in (COS, SIN)]
             dst = z_bf[b][:].rearrange("p (a c i t) -> p a c t i", a=2, i=2, t=PACK)[:, a]
-            nc.vector.tensor_tensor(out=dst, in0=terms[0], in1=terms[1], op=sign[a])
+            nc.vector.tensor_tensor(out=dst, in0=terms[0], in1=terms[1], op=ALU.add)
 
         def quantize_z(b, a):
             nc.vector.quantize_mx(out=z_codes[b][:, a].rearrange("p a n -> p (a n)").bitcast(FP8X4),
@@ -240,29 +253,24 @@ def tile_picked_headrope_none_po_kernel(tc, x_words, x_scales, w1, w2, ct, st, w
             toks = slice(first * BLK, end * BLK)
             nc.sync.dma_start(out=out_words[:, toks], in_=o_codes[:, toks].bitcast(I32))
 
-        for b in range(NBLK):
-            if b == last:
-                whole_sums(b, 0)
-                whole_sums(b, 1)
-            elif b:
-                pair_sums(b, 0)
-                pair_sums(b, 1)
-                weave(b, slice(0, BLK))
-            else:
-                pair_sums(b, 0)
-                weave(b, slice(0, BLK // 2))
-                pair_sums(b, 1)
-                weave(b, slice(BLK // 2, BLK))
-            if b == 0:
-                on_vector(0, 1, 3, late)
-                idle = bank(2 * PACK - 1, [P, PACK, BLK])
-                for n in range(WARM_UPS):
-                    nc.tensor.matmul_mx(out=idle[:, n % PACK, :], lhsT=w_codes[0][:, :P].bitcast(FP8X4), lhsT_scale=w_sc[0][:, :P],
-                                        rhs=w_codes[1][:, :BLK].bitcast(FP8X4), rhs_scale=w_sc[1][:, :BLK], start=True, stop=True)
-                quantize_z(0, slice(0, 1))
-                quantize_z(0, slice(1, 2))
-            if b >= 2:
-                quantize_z(b - 1, slice(0, 2))
+        for a in range(2):
+            upper_sum(0, slice(a, a + 1))
+            weave(0, slice(a * BLK // 2, (a + 1) * BLK // 2))
+        vector_product(Y, SIN, 3, late)
+        idle = bank(2 * PACK - 1, [P, PACK, BLK])
+        for n in range(WARM_UPS):
+            nc.tensor.matmul_mx(out=idle[:, n % PACK, :], lhsT=w_codes[Y][:, :P].bitcast(FP8X4), lhsT_scale=w_sc[Y][:, :P],
+                                rhs=w_codes[E][:, :BLK].bitcast(FP8X4), rhs_scale=w_sc[E][:, :BLK], start=True, stop=True)
+        quantize_z(0, slice(0, 1))
+        quantize_z(0, slice(1, 2))
+        upper_sum(1, both)
+        weave(1, slice(0, BLK))
+        upper_sum(2, both)
+        weave(2, slice(0, BLK))
+        quantize_z(1, both)
+        whole_sum(last, 0)
+        whole_sum(last, 1)
+        quantize_z(2, both)
         quantize_z(last, slice(0, 1))
         quantize_z(last, slice(1, 2))
         for h, acc in enumerate(two_banks(0, 0)):
@@ -284,4 +292,4 @@ def tile_picked_headrope_none_po_kernel(tc, x_words, x_scales, w1, w2, ct, st, w
         quantize_out(last)
         store_words(last, NBLK)
         for q in range(4):
-            nc.scalar.dma_start(out=out_2[0][4 * q : 4 * q + 4, :].bitcast(I32), in_=o_sc[32 * q : 32 * q + 4, :].bitcast(I32))
+            (nc.scalar, nc.sync)[q % 2].dma_start(out=out_2[0][4 * q : 4 * q + 4, :].bitcast(I32), in_=o_sc[32 * q : 32 * q + 4, :].bitcast(I32))

@@ -153,9 +153,9 @@ def tile_picked_headrope_none_po_kernel(tc, x_words, x_scales, w1, w2, ct, st, w
 
         both = slice(0, 2)
         y_first = sb("y_first", [P, NBLK, BLK], F32)
-        y_last = sb("y_last", [P, NBLK // 2, BLK], F32)
+        y_last = sb("y_last", [P, NBLK, BLK], F32)
         nc.scalar.copy(out=y_first[:], in_=blocks(proj[Y][0][:]))
-        nc.scalar.copy(out=y_last[:], in_=blocks(proj[Y][3][:])[:, early])
+        nc.scalar.copy(out=y_last[:], in_=blocks(proj[Y][3][:]))
 
         look_up(True, COS, 0, late)
         look_up(False, COS, 0, early)
@@ -178,13 +178,11 @@ def tile_picked_headrope_none_po_kernel(tc, x_words, x_scales, w1, w2, ct, st, w
                 slot_sum(nc.gpsimd, t, slice(0, last), both)
         look_up(False, COS, 3, whole)
         vector_product(E, COS, 3, whole)
-        gpsimd_product(y_last[:], COS, 3, early)
-        look_up(False, SIN, 3, early)
-        look_up(False, SIN, 3, late)
-        vector_product(E, SIN, 3, early)
-        gpsimd_product(y_last[:], SIN, 3, early)
-        vector_product(Y, COS, 3, late)
-        vector_product(E, SIN, 3, late)
+        gpsimd_product(y_last[:], COS, 3, whole)
+        for bs in (early, late):
+            look_up(False, SIN, 3, bs)
+            vector_product(E, SIN, 3, bs)
+            vector_product(Y, SIN, 3, bs)
 
         wo = sb("wo", [P, 2, N], U32)
         for a in range(2):
@@ -256,7 +254,6 @@ def tile_picked_headrope_none_po_kernel(tc, x_words, x_scales, w1, w2, ct, st, w
         for a in range(2):
             upper_sum(0, slice(a, a + 1))
             weave(0, slice(a * BLK // 2, (a + 1) * BLK // 2))
-        vector_product(Y, SIN, 3, late)
         idle = bank(2 * PACK - 1, [P, PACK, BLK])
         for n in range(WARM_UPS):
             nc.tensor.matmul_mx(out=idle[:, n % PACK, :], lhsT=w_codes[Y][:, :P].bitcast(FP8X4), lhsT_scale=w_sc[Y][:, :P],

from contextlib import ExitStack

import concourse.mybir as mybir

K, T, S, N, H, U = 512, 2048, 512, 512, 512, 1024
FLOPS = 2 * S * (2 * K * H + 2 * H * N)

F32 = mybir.dt.float32
BF16 = mybir.dt.bfloat16
I32 = mybir.dt.int32
U32 = mybir.dt.uint32
U16 = mybir.dt.uint16
U8 = mybir.dt.uint8
FP8X4 = mybir.dt.float8_e4m3fn_x4
ALU = mybir.AluOpType
COPY = mybir.ActivationFunctionType.Copy

P = 128
PACK = 4
BLK = 128
NBLK = S // BLK
W1_GROUPS = 86
W2_GROUPS = 92
WARM_UPS = 6
Y, E = 0, 1
COS, SIN = 0, 1


def tile_picked_headrope_none_po_kernel(tc, x_words, x_scales, w1, w2, ct, st, w3_words, w3_scales, w4_words, w4_scales, offs, pos, out_0, out_1, out_2):
    nc = tc.nc
    with ExitStack() as ctx:
        keep = ctx.enter_context(tc.tile_pool(name="keep", bufs=1))
        psum = ctx.enter_context(tc.psum_pool(name="psum", bufs=1))

        def sb(name, shape, dtype):
            return keep.tile(shape, dtype, name=name, align_bytes=64)

        def bank(k, shape):
            return psum.tile(shape, F32, name="bank%d" % k)

        def words_of(dram):
            return dram[0].rearrange("p n j -> p (n j)").bitcast(I32)

        def scale_rows(tile, first_row, dram):
            return [(tile[32 * q + first_row : 32 * q + first_row + 4, :].bitcast(I32), dram[0][4 * q : 4 * q + 4, :].bitcast(I32)) for q in range(4)]

        offs_t = keep.tile([P, S // 16], U16, name="offs_t")
        pos_t = keep.tile([P, S // 16], U16, name="pos_t")
        x_tab = sb("x_tab", [P, T], U32)
        xs_tab = sb("xs_tab", [P, T], U8)
        w_raw = [sb("w_raw%d" % i, [P, PACK, H], F32) for i in (Y, E)]
        tabs = [[sb("tab%d_%d" % (k, t), [P, U], F32) for t in range(PACK)] for k in (COS, SIN)]
        wo_raw = sb("wo_raw", [P, 2, N], U32)
        wos_raw = sb("wos_raw", [P, N], U8)

        nc.gpsimd.memset(xs_tab[:].bitcast(I32), 0)
        nc.vector.memset(wos_raw[:].bitcast(I32), 0)

        tab_v = [dram.rearrange("(p t) u -> p t u", t=PACK) for dram in (ct, st)]
        narrow = scale_rows(wos_raw, 4, w3_scales) + scale_rows(wos_raw, 8, w4_scales)

        def load_rows(rows):
            for dst, src in rows:
                nc.sync.dma_start(out=dst, in_=src)

        nc.sync.dma_start(out=x_tab[:].bitcast(I32), in_=words_of(x_words))
        nc.sync.dma_start(offs_t[:], offs)
        load_rows(scale_rows(xs_tab, 0, x_scales))
        nc.sync.dma_start(out=w_raw[Y][:], in_=w1.rearrange("(p j) c -> p j c", j=PACK))
        nc.sync.dma_start(pos_t[:], pos)
        nc.sync.dma_start(out=w_raw[E][:], in_=w2.rearrange("(p j) c -> p j c", j=PACK))
        load_rows(narrow[:4])
        for t in range(PACK):
            for k in (COS, SIN):
                nc.sync.dma_start(out=tabs[k][t][:], in_=tab_v[k][:, t, :])
                if (t, k) == (1, COS):
                    load_rows(narrow[4:])
        for a, dram in enumerate((w3_words, w4_words)):
            nc.sync.dma_start(out=wo_raw[:, a, :].bitcast(I32), in_=words_of(dram))

        x_codes = sb("x_codes", [P, S], U32)
        x_sc = sb("x_sc", [P, S], U8)
        nc.vector.tensor_copy(x_codes[:], x_tab[:].indirect(offs_t[:]))
        nc.vector.tensor_copy(x_sc[:], xs_tab[:].indirect(offs_t[:]))

        w_bf = [sb("w_bf%d" % i, [P, PACK * H], BF16) for i in (Y, E)]
        w_codes = [sb("w_codes%d" % i, [P, H], U32) for i in (Y, E)]
        w_sc = [sb("w_sc%d" % i, [P, H], U8) for i in (Y, E)]

        trig = [[sb("trig%d_%d" % (k, t), [P, S], F32) for t in range(PACK)] for k in (COS, SIN)]
        whole, early, late = slice(0, NBLK), slice(0, NBLK // 2), slice(NBLK // 2, NBLK)

        def look_up(on_vector, k, t, bs):
            dst = trig[k][t][:, bs.start * BLK : bs.stop * BLK]
            src = tabs[k][t][:].indirect(pos_t[:, bs.start * BLK // 16 : bs.stop * BLK // 16])
            if on_vector:
                nc.vector.tensor_copy(dst, src)
            else:
                nc.scalar.activation(out=dst, in_=src, func=COPY)

        def round_weight(on_vector, i, ms, ts):
            dst = w_bf[i][:].rearrange("p (t m j) -> p m j t", t=PACK, j=PACK)[:, ms, :, ts]
            src = w_raw[i][:].rearrange("p j (m t) -> p m j t", t=PACK)[:, ms, :, ts]
            if on_vector:
                nc.vector.tensor_copy(out=dst, in_=src)
            else:
                nc.scalar.activation(out=dst, in_=src, func=COPY)

        proj = [[None] * PACK for i in (Y, E)]

        def project(i, first, end):
            cols = slice(first * P, end * P)
            nc.vector.quantize_mx(out=w_codes[i][:, cols].bitcast(FP8X4), scales=w_sc[i][:, cols], in_=w_bf[i][:, first * H : end * H])
            for t in range(first, end):
                proj[i][t] = bank(2 * t + i, [P, S])
                cols = slice(t * P, (t + 1) * P)
                nc.tensor.matmul_mx(out=proj[i][t][:], lhsT=w_codes[i][:, cols].bitcast(FP8X4), lhsT_scale=w_sc[i][:, cols],
                                    rhs=x_codes[:].bitcast(FP8X4), rhs_scale=x_sc[:], start=True, stop=True)

        round_weight(True, Y, slice(0, W1_GROUPS), slice(0, PACK))
        round_weight(False, Y, slice(W1_GROUPS, P), slice(0, PACK))
        for first, end in ((0, 1), (3, 4), (1, 3)):
            project(Y, first, end)
        round_weight(True, E, slice(0, P), slice(0, 2))
        round_weight(True, E, slice(0, W2_GROUPS), slice(2, 4))
        round_weight(False, E, slice(W2_GROUPS, P), slice(2, 4))
        for first in (0, 2):
            project(E, first, first + 2)

        term = [sb("term%d" % k, [P, PACK, NBLK, 2, BLK], F32) for k in (COS, SIN)]
        last = NBLK - 1
        pairs = sb("pairs", [P, 2, last, 2, BLK], F32)

        def blocks(ap):
            return ap.rearrange("p (b n) -> p b n", b=NBLK)

        def term_of(i, k, t, bs):
            return term[k][:, t, bs, (i + k) % 2, :]

        def vector_product(i, k, t, bs):
            factor, table = blocks(proj[i][t][:])[:, bs], blocks(trig[k][t][:])[:, bs]
            if (i, k) == (E, SIN):
                nc.vector.scalar_tensor_tensor(out=term_of(i, k, t, bs), in0=factor, scalar=-1.0, in1=table, op0=ALU.mult, op1=ALU.mult)
            else:
                nc.vector.tensor_tensor(out=term_of(i, k, t, bs), in0=factor, in1=table, op=ALU.mult)

        def gpsimd_product(y_copy, k, t, bs):
            nc.gpsimd.tensor_tensor(out=term_of(Y, k, t, bs), in0=y_copy, in1=blocks(trig[k][t][:])[:, bs], op=ALU.mult)

        def slot_sum(engine, t, bs, zs):
            dst = pairs[:, t // 2, bs, zs].bitcast(BF16).rearrange("p b a (n e) -> p e b a n", e=2)[:, t % 2]
            engine.tensor_tensor(out=dst, in0=term[COS][:, t, bs, zs], in1=term[SIN][:, t, bs, zs], op=ALU.add)

        both = slice(0, 2)
        y_first = sb("y_first", [P, NBLK, BLK], F32)
        y_last = sb("y_last", [P, NBLK, BLK], F32)
        nc.scalar.copy(out=y_first[:], in_=blocks(proj[Y][0][:]))
        nc.scalar.copy(out=y_last[:], in_=blocks(proj[Y][3][:]))

        look_up(True, COS, 0, late)
        look_up(False, COS, 0, early)
        look_up(True, SIN, 0, late)
        vector_product(E, COS, 0, whole)
        gpsimd_product(y_first[:], COS, 0, whole)
        look_up(False, SIN, 0, early)
        vector_product(E, SIN, 0, whole)
        gpsimd_product(y_first[:], SIN, 0, whole)
        wos = sb("wos", [P, N], U8)
        for ms in (slice(0, P - 3), slice(P - 3, P)):
            nc.vector.tensor_copy(out=wos[:].rearrange("p (t m) -> p m t", t=PACK)[:, ms], in_=wos_raw[:].rearrange("p (m t) -> p m t", t=PACK)[:, ms])
        slot_sum(nc.gpsimd, 0, slice(0, last), both)
        for t in (1, 2):
            for k in (COS, SIN):
                look_up(False, k, t, whole)
                vector_product(E, k, t, whole)
                vector_product(Y, k, t, whole)
            if t == 1:
                slot_sum(nc.gpsimd, t, slice(0, last), both)
        look_up(False, COS, 3, whole)
        vector_product(E, COS, 3, whole)
        gpsimd_product(y_last[:], COS, 3, whole)
        for bs in (early, late):
            look_up(False, SIN, 3, bs)
            vector_product(E, SIN, 3, bs)
            vector_product(Y, SIN, 3, bs)

        wo = sb("wo", [P, 2, N], U32)
        for a in range(2):
            nc.scalar.copy(out=wo[:, a].rearrange("p (t m) -> p m t", t=PACK), in_=wo_raw[:, a].rearrange("p (m t) -> p m t", t=PACK))

        z_bf = [sb("z_bf%d" % b, [P, 2 * BLK * PACK], BF16) for b in range(NBLK)]
        z_codes = [sb("z_codes%d" % b, [P, 2, BLK], U32) for b in range(NBLK)]
        z_sc = [sb("z_sc%d" % b, [P, 2, BLK], U8) for b in range(NBLK)]
        o_bf = [sb("o_bf%d" % b, [P, BLK * PACK], BF16) for b in range(NBLK)]
        o_first = pairs[:, 1, 1:last].rearrange("p b a n -> p (b a) n")
        o_mid = {b: sb("o_mid%d" % b, [P, PACK, BLK], F32) for b in (1, 2)}
        o_last = sb("o_last", [P, PACK, BLK], F32)
        o_codes = sb("o_codes", [P, S], U32)
        o_sc = sb("o_sc", [P, S], U8)
        out_v = out_0.rearrange("(p t) n -> p t n", t=PACK)
        out_words = words_of(out_1)

        def toks_of(b):
            return slice(b * BLK, (b + 1) * BLK)

        def upper_sum(b, zs):
            terms = [term[k][:, 2:4, b, zs].rearrange("p e a (c i) -> p (a c) e i", i=4) for k in (COS, SIN)]
            nc.vector.tensor_tensor(out=pairs[:, 1, b, zs].bitcast(BF16).rearrange("p a (c i e) -> p (a c) e i", i=4, e=2), in0=terms[0], in1=terms[1], op=ALU.add)

        def weave(b, cols):
            nc.scalar.copy(out=z_bf[b][:].bitcast(F32).rearrange("p (c i u) -> p c u i", i=2, u=2)[:, cols], in_=pairs[:, :, b].rearrange("p u a (c i) -> p (a c) u i", i=2)[:, cols])

        def whole_sum(b, a):
            terms = [term[k][:, :, b, a].rearrange("p t (c i) -> p c t i", i=2) for k in (COS, SIN)]
            dst = z_bf[b][:].rearrange("p (a c i t) -> p a c t i", a=2, i=2, t=PACK)[:, a]
            nc.vector.tensor_tensor(out=dst, in0=terms[0], in1=terms[1], op=ALU.add)

        def quantize_z(b, a):
            nc.vector.quantize_mx(out=z_codes[b][:, a].rearrange("p a n -> p (a n)").bitcast(FP8X4),
                                  scales=z_sc[b][:, a].rearrange("p a n -> p (a n)"),
                                  in_=z_bf[b][:].rearrange("p (a m) -> p a m", a=2)[:, a].rearrange("p a m -> p (a m)"))

        def one_pass(out, b, t, a, start, stop):
            cols = slice(t * P, (t + 1) * P)
            nc.tensor.matmul_mx(out=out, lhsT=wo[:, a, cols].bitcast(FP8X4), lhsT_scale=wos[4 + 4 * a :, cols],
                                rhs=z_codes[b][:, a, :].bitcast(FP8X4), rhs_scale=z_sc[b][:, a, :], start=start, stop=stop)

        def whole_bank(b):
            acc = bank(b + 1, [P, PACK, BLK])
            for t in range(PACK):
                for a in range(2):
                    one_pass(acc[:, t, :], b, t, a, a == 0, a == 1)
            nc.scalar.copy(out=o_mid[b][:], in_=acc[:])
            nc.sync.dma_start(out=out_v[:, :, toks_of(b)], in_=o_mid[b][:])

        def two_banks(b, first_bank):
            accs = [bank(first_bank + h, [P, 2, BLK]) for h in range(2)]
            for a in range(2):
                for t in range(PACK):
                    one_pass(accs[t // 2][:, t % 2, :], b, t, a, a == 0 and t % 2 == 0, a == 1 and t % 2 == 1)
            return accs

        def round_out(b, src):
            nc.vector.tensor_copy(out=o_bf[b][:].rearrange("p (c i t) -> p c t i", i=4, t=PACK), in_=src.rearrange("p t (c i) -> p c t i", i=4))

        def quantize_out(b):
            toks = toks_of(b)
            nc.vector.quantize_mx(out=o_codes[:, toks].bitcast(FP8X4), scales=o_sc[:, toks], in_=o_bf[b][:])

        def store_words(first, end):
            toks = slice(first * BLK, end * BLK)
            nc.sync.dma_start(out=out_words[:, toks], in_=o_codes[:, toks].bitcast(I32))

        for a in range(2):
            upper_sum(0, slice(a, a + 1))
            weave(0, slice(a * BLK // 2, (a + 1) * BLK // 2))
        idle = bank(2 * PACK - 1, [P, PACK, BLK])
        for n in range(WARM_UPS):
            nc.tensor.matmul_mx(out=idle[:, n % PACK, :], lhsT=w_codes[Y][:, :P].bitcast(FP8X4), lhsT_scale=w_sc[Y][:, :P],
                                rhs=w_codes[E][:, :BLK].bitcast(FP8X4), rhs_scale=w_sc[E][:, :BLK], start=True, stop=True)
        quantize_z(0, slice(0, 1))
        quantize_z(0, slice(1, 2))
        upper_sum(1, both)
        weave(1, slice(0, BLK))
        upper_sum(2, both)
        weave(2, slice(0, BLK))
        quantize_z(1, both)
        whole_sum(last, 0)
        whole_sum(last, 1)
        quantize_z(2, both)
        quantize_z(last, slice(0, 1))
        quantize_z(last, slice(1, 2))
        for h, acc in enumerate(two_banks(0, 0)):
            ts = slice(2 * h, 2 * h + 2)
            nc.scalar.copy(out=o_first[:, ts], in_=acc[:])
            nc.sync.dma_start(out=out_v[:, ts, toks_of(0)], in_=o_first[:, ts])
        whole_bank(1)
        whole_bank(2)
        round_out(0, o_first)
        for b in (1, 2):
            round_out(b, o_mid[b][:])
        for b in range(last):
            quantize_out(b)
        store_words(0, last)
        for h, (acc, copy) in enumerate(zip(two_banks(last, 4), (nc.scalar.copy, nc.vector.tensor_copy))):
            copy(out=o_last[:, 2 * h : 2 * h + 2], in_=acc[:])
        nc.sync.dma_start(out=out_v[:, :, toks_of(last)], in_=o_last[:])
        round_out(last, o_last[:])
        quantize_out(last)
        store_words(last, NBLK)
        for q in range(4):
            (nc.scalar, nc.sync)[q % 2].dma_start(out=out_2[0][4 * q : 4 * q + 4, :].bitcast(I32), in_=o_sc[32 * q : 32 * q + 4, :].bitcast(I32))
